import numpy as np
import ml_dtypes


def mxq(x, axis, fmt="e4m3"):
    dtype, down = {"e4m3": (ml_dtypes.float8_e4m3fn, 7), "e5m2": (ml_dtypes.float8_e5m2, 14)}[fmt]
    v = np.moveaxis(np.asarray(x, np.float32).astype(ml_dtypes.bfloat16).astype(np.float64), axis, -1)
    blocks = v.reshape(v.shape[:-1] + (-1, 32))
    amax = np.abs(blocks).max(-1, keepdims=True)
    byte = np.maximum(np.where(amax > 0, np.frexp(amax)[1] - 1 + 127, 0) - down, 1)
    scale = np.exp2(byte - 127.0)
    codes = (blocks / scale).astype(np.float32).astype(dtype).astype(np.float64)
    return np.moveaxis((codes * scale).reshape(v.shape), -1, axis)


WIDE = False


def mx_kscale(k):
    if not WIDE:
        return np.ones(k)
    levels = np.array([10, -10, 5, -5, 0])
    if k % 512:
        return np.exp2(np.random.permutation(np.resize(levels, k // 32))).repeat(32)
    a = np.empty((k // 512, 16))
    for p in range(k // 512):
        a[p, :8] = np.random.permutation(np.resize(levels, 8))
        for g in range(8):
            far = levels[np.abs(levels - a[p, g]) >= 10]
            a[p, g + 8] = far[np.random.randint(len(far))]
    return np.exp2(a.ravel()).repeat(32)


def f64(x):
    return np.asarray(x).astype(np.float64)


def striped(idx):
    return np.tile(idx.reshape(-1, 16).T, (8, 1)).astype(np.uint16)


def unstriped(offs):
    return offs[:16].T.reshape(-1).astype(np.int64)


E2M1 = np.array([0.0, 0.5, 1.0, 1.5, 2.0, 3.0, 4.0, 6.0, -0.0, -0.5, -1.0, -1.5, -2.0, -3.0, -4.0, -6.0])


def pack_weight(w, fmt):
    k, n = w.shape
    w = f64(np.asarray(w, np.float32).astype(ml_dtypes.bfloat16)).reshape(k // 32, 32, n)
    amax = np.abs(w).max(1)
    if fmt == "e4m3":
        byte = np.frexp(amax)[1] - 1 + 127 - 7
    else:
        mant, ex = np.frexp(amax / 6.0)
        byte = np.where(mant > 0.5, ex, ex - 1) + 127
    byte = np.clip(np.where(amax > 0, byte, 1), 1, 254)
    scaled = (w * np.exp2(127.0 - byte)[:, None, :]).reshape(k, n).astype(np.float32)
    by_word = np.ascontiguousarray(scaled.reshape(k // 512, 128, 4, n).transpose(0, 1, 3, 2))
    if fmt == "e4m3":
        words = by_word.astype(ml_dtypes.float8_e4m3fn).view(np.uint8)
    else:
        c = by_word.astype(ml_dtypes.float4_e2m1fn).view(np.uint8) & 0xF
        words = (c[..., 0::2] | (c[..., 1::2] << 4)).reshape(k // 512, 128, 2 * n)
    return np.ascontiguousarray(words), np.ascontiguousarray(byte.astype(np.uint8).reshape(k // 512, 16, n))


def unpack_weight(words, scales, fmt):
    g, _, n = scales.shape
    words = np.ascontiguousarray(words).reshape(g, 128, n, -1)
    if fmt == "e4m3":
        vals = words.view(ml_dtypes.float8_e4m3fn).astype(np.float64)
    else:
        nib = np.empty((g, 128, n, 4), np.uint8)
        nib[..., 0::2] = words & 0xF
        nib[..., 1::2] = words >> 4
        vals = E2M1[nib]
    vals = vals * np.repeat(np.exp2(scales.astype(np.float64) - 127.0), 8, axis=1)[..., None]
    return vals.transpose(0, 1, 3, 2).reshape(g * 512, n)


def gelu(v):
    return 0.5 * v * (1.0 + np.tanh(np.sqrt(2.0 / np.pi) * (v + 0.044715 * v**3)))


K, M, H, N, T, T2, T3, S = 1024, 512, 1024, 512, 2048, 2048, 1024, 512

def setup_inputs():
    n = np.random.standard_normal
    s = mx_kscale(K)[:, None]
    s2 = mx_kscale(M)[:, None]
    u = mx_kscale(H)[:, None]
    tab_words, tab_scales = pack_weight(n((K, T)) * s, "e4m3")
    tab2_words, tab2_scales = pack_weight(n((M, T2)) * s2, "e4m3")
    tab3_words, tab3_scales = pack_weight(n((M, T3)) * s2, "e2m1")
    w2_words, w2_scales = pack_weight(1.2 * n((K, H)) / np.sqrt(K) / s * u.T, "e2m1")
    w4_words, w4_scales = pack_weight(n((H, N)) / np.sqrt(H) / u, "e4m3")
    return {
        "tab_words": tab_words, "tab_scales": tab_scales,
        "tab2_words": tab2_words, "tab2_scales": tab2_scales,
        "tab3_words": tab3_words, "tab3_scales": tab3_scales,
        "offs": striped(np.random.permutation(T)[:S]),
        "offs2": striped(np.random.permutation(T2)[:S]),
        "offs3": striped(np.random.permutation(T3)[:S]),
        "w1": (1.3 * n((K, H)) / np.sqrt(K) / s).astype(np.float32),
        "w2_words": w2_words, "w2_scales": w2_scales,
        "w3": (0.8 * n((M, H)) / np.sqrt(M) / s2 * u.T).astype(np.float32),
        "w4_words": w4_words, "w4_scales": w4_scales,
        "w5": (n((M, N)) / np.sqrt(M) / s2).astype(np.float32),
    }

def reference(tab_words, tab_scales, tab2_words, tab2_scales, tab3_words, tab3_scales, offs, offs2, offs3,
              w1, w2_words, w2_scales, w3, w4_words, w4_scales, w5):
    v = unpack_weight(tab_words, tab_scales, "e4m3")[:, unstriped(offs)]
    v2 = unpack_weight(tab2_words, tab2_scales, "e4m3")[:, unstriped(offs2)]
    v3 = unpack_weight(tab3_words, tab3_scales, "e2m1")[:, unstriped(offs3)]
    a = mxq(f64(w1), 0, "e4m3").T @ v
    b = unpack_weight(w2_words, w2_scales, "e2m1").T @ v
    c = mxq(f64(w3), 0, "e4m3").T @ v2
    h = a / (1.0 + np.exp(-a)) * b + c
    y = unpack_weight(w4_words, w4_scales, "e4m3").T @ mxq(h, 0, "e4m3")
    d = mxq(f64(w5), 0, "e4m3").T @ v3
    return y * d

@@ -1,0 +1,237 @@
+from contextlib import ExitStack
+
+import concourse.mybir as mybir
+from concourse.masks import make_identity
+
+K, M, H, N, T, T2, T3, S = 1024, 512, 1024, 512, 2048, 2048, 1024, 512
+FLOPS = 2 * S * (2 * K * H + M * H + H * N + M * N)
+
+F32 = mybir.dt.float32
+BF16 = mybir.dt.bfloat16
+I32 = mybir.dt.int32
+U32 = mybir.dt.uint32
+U16 = mybir.dt.uint16
+U8 = mybir.dt.uint8
+FP8X4 = mybir.dt.float8_e4m3fn_x4
+FP4X4 = mybir.dt.float4_e2m1fn_x4
+SILU = mybir.ActivationFunctionType.Silu
+MULT = mybir.AluOpType.mult
+ADD = mybir.AluOpType.add
+
+P = 128
+PACK = 4
+QW = 256
+LOAD_ORDER = ["offs","offs2","offs3","w1q0p0","tabp0","s:tab","w1q0p1","tabp1","w2h0","s:w2","w1q1p0","tab2","s:tab2","w1q1p1","w3q0","w3q1","w2h1","w1q2p0","w1q2p1","w1q3p0","w1q3p1","w3q2","w3q3","tab3","w5h0","w5h1","w4","s:tab3","s:w4"]
+SCALE_ORDER = [["tab","sync"],["w2","sync"],["tab2","sync"],["tab3","gpsimd"],["w4","gpsimd"]]
+V_CASTS = ["w3q1","w3q3"]
+STEPS = [["g","gw0"],["g","gs0"],["g","gs1"],["g","gw1"],["cast","w1q0p0"],["cast","w1q0p1"],["quant","w1q0p0"],["quant","w1q0p1"],["a",0,0],["a",0,1],["b",0,0],["b",0,1],["silu",0,0],["silu",0,1],["gate",0,0],["gate",0,1],["cast","w1q1p0"],["cast","w1q1p1"],["quant","w1q1p0"],["quant","w1q1p1"],["a",1,0],["a",1,1],["b",1,0],["b",1,1],["silu",1,0],["silu",1,1],["gate",1,0],["gate",1,1],["cast","w1q2p0"],["cast","w1q2p1"],["quant","w1q2p0"],["quant","w1q2p1"],["a",2,0],["a",2,1],["b",2,0],["b",2,1],["silu",2,0],["silu",2,1],["gate",2,0],["gate",2,1],["g","g2s"],["g","g2w"],["cast","w1q3p0"],["cast","w1q3p1"],["quant","w1q3p0"],["quant","w1q3p1"],["a",3,0],["a",3,1],["b",3,0],["b",3,1],["silu",3,0],["silu",3,1],["gate",3,0],["gate",3,1],["cast","w3q0"],["quant","w3q0"],["c",0,0],["c",0,1],["plus",0,0],["plus",0,1],["cast","w3q1"],["quant","w3q1"],["c",1,0],["c",1,1],["plus",1,0],["plus",1,1],["cast","w3q2"],["quant","w3q2"],["c",2,0],["c",2,1],["plus",2,0],["plus",2,1],["cast","w3q3"],["quant","w3q3"],["c",3,0],["c",3,1],["plus",3,0],["plus",3,1],["turn",0,0],["turn",0,1],["turn_out",0,0],["turn_out",0,1],["qh",0,0],["qh",0,1],["y",0,0,0],["y",0,0,1],["y",0,1,0],["y",0,1,1],["turn",1,0],["turn_out",1,0],["turn",1,1],["turn_out",1,1],["g","g3s"],["g","g3w"],["cast","w5h0"],["cast","w5h1"],["quant","w5h0"],["quant","w5h1"],["d",0],["d",1],["d",2],["d",3],["qh",1,0],["y",1,0,0],["y",1,0,1],["qh",1,1],["fin",0,0],["fin",0,1],["y",1,1,0],["y",1,1,1],["fin",1,0],["fin",1,1]]
+
+
+def tile_list_abbreviation_expansion_features_kernel(
+    tc, tab_words, tab_scales, tab2_words, tab2_scales, tab3_words, tab3_scales, offs, offs2, offs3,
+    w1, w2_words, w2_scales, w3, w4_words, w4_scales, w5, out,
+):
+    nc = tc.nc
+    with ExitStack() as ctx:
+        keep = ctx.enter_context(tc.tile_pool(name="keep", bufs=1))
+        psum = ctx.enter_context(tc.psum_pool(name="psum", bufs=1))
+
+        def sb(name, shape, dtype):
+            return keep.tile(shape, dtype, name=name, align_bytes=64)
+
+        lists = {"offs": keep.tile([P, S // 16], U16, name="list1"), "offs2": keep.tile([P, S // 16], U16, name="list2"),
+                 "offs3": keep.tile([P, S // 16], U16, name="list3")}
+        list_src = {"offs": offs, "offs2": offs2, "offs3": offs3}
+        banks = [psum.tile([P, 512], F32, name=f"bank{i}") for i in range(8)]
+
+        tab_w = [sb(f"tab_w{a}", [P, T], U32) for a in range(2)]
+        tab2_w = sb("tab2_w", [P, T2], U32)
+        tab3_w = sb("tab3_w", [P, T3], U16)
+        planes = {
+            "tab": (sb("tab_s", [P, 2 * T], U8), tab_scales),
+            "tab2": (sb("tab2_s", [P, T2], U8), tab2_scales),
+            "tab3": (sb("tab3_s", [P, T3], U8), tab3_scales),
+            "w2": (sb("w2_s", [P, 2 * H], U8), w2_scales),
+            "w4": (sb("w4_s", [P, 2 * N], U8), w4_scales),
+        }
+        w2_w = [sb(f"w2_w{h}", [P, 2, H], U8) for h in range(2)]
+        w4_w = sb("w4_w", [P, 2, N], U32)
+        raw = {}
+        for q in range(4):
+            for a in range(2):
+                raw[f"w1q{q}p{a}"] = (sb(f"w1raw{q}{a}", [P, PACK, QW], F32), w1[512 * a : 512 * (a + 1), QW * q : QW * (q + 1)])
+            raw[f"w3q{q}"] = (sb(f"w3raw{q}", [P, PACK, QW], F32), w3[:, QW * q : QW * (q + 1)])
+        for q in range(2):
+            raw[f"w5h{q}"] = (sb(f"w5raw{q}", [P, PACK, QW], F32), w5[:, QW * q : QW * (q + 1)])
+
+        for name, queue in SCALE_ORDER:
+            nc.vector.memset(planes[name][0][:].bitcast(I32), 0)
+
+        def load_scales(name, queue):
+            tile, src = planes[name]
+            passes = src.shape[0]
+            eng = {"sync": nc.sync, "scalar": nc.scalar, "gpsimd": nc.gpsimd}[queue]
+            for quad in range(4):
+                eng.dma_start(
+                    out=tile[32 * quad : 32 * quad + 4, :].bitcast(I32).rearrange("r (a t) -> r a t", a=passes),
+                    in_=src[:, 4 * quad : 4 * quad + 4, :].bitcast(I32).rearrange("a r t -> r a t"),
+                )
+
+        def load(name):
+            if name in lists:
+                nc.sync.dma_start(lists[name][:], list_src[name])
+            elif name in raw:
+                tile, src = raw[name]
+                nc.sync.dma_start(out=tile[:], in_=src.rearrange("(p i) c -> p i c", i=PACK))
+            elif name.startswith("tabp"):
+                a = int(name[4])
+                nc.sync.dma_start(out=tab_w[a][:].bitcast(I32), in_=tab_words[a].rearrange("p t i -> p (t i)").bitcast(I32))
+            elif name == "tab2":
+                nc.sync.dma_start(out=tab2_w[:].bitcast(I32), in_=tab2_words[0].rearrange("p t i -> p (t i)").bitcast(I32))
+            elif name == "tab3":
+                nc.sync.dma_start(out=tab3_w[:].bitcast(I32), in_=tab3_words[0].bitcast(I32))
+            elif name.startswith("w2h"):
+                h = int(name[3])
+                nc.sync.dma_start(out=w2_w[h][:].bitcast(I32),
+                                  in_=w2_words[:, :, H * h : H * (h + 1)].bitcast(I32).rearrange("a p b -> p a b"))
+            elif name == "w4":
+                nc.sync.dma_start(out=w4_w[:].bitcast(I32),
+                                  in_=w4_words.rearrange("a p e i -> a p (e i)").bitcast(I32).rearrange("a p e -> p a e"))
+            elif name.startswith("s:"):
+                load_scales(name[2:], dict(SCALE_ORDER)[name[2:]])
+
+        for name in LOAD_ORDER:
+            load(name)
+
+        ident = sb("ident", [P, P], F32)
+        make_identity(nc, ident[:])
+
+        v_w = [sb(f"v_w{a}", [P, S], U32) for a in range(2)]
+        v_s = [sb(f"v_s{a}", [P, S], U8) for a in range(2)]
+        v2_w = sb("v2_w", [P, S], U32)
+        v2_s = sb("v2_s", [P, S], U8)
+        v3_w = sb("v3_w", [P, S], U16)
+        v3_s = sb("v3_s", [P, S], U8)
+        gathers = {
+            "gs0": (v_s[0], planes["tab"][0][:, 0:T], "offs"),
+            "gs1": (v_s[1], planes["tab"][0][:, T : 2 * T], "offs"),
+            "gw0": (v_w[0], tab_w[0][:], "offs"),
+            "gw1": (v_w[1], tab_w[1][:], "offs"),
+            "g2s": (v2_s, planes["tab2"][0][:], "offs2"),
+            "g2w": (v2_w, tab2_w[:], "offs2"),
+            "g3s": (v3_s, planes["tab3"][0][:], "offs3"),
+            "g3w": (v3_w, tab3_w[:], "offs3"),
+        }
+
+        grouped = {name: sb("g_" + name, [P, QW * PACK], BF16) for name in raw}
+        codes = {name: sb("c_" + name, [P, QW], U32) for name in raw}
+        scales = {name: sb("s_" + name, [P, QW], U8) for name in raw}
+
+        def cast(name):
+            src = raw[name][0][:].rearrange("p i (c k) -> p c i k", k=4)
+            dst = grouped[name][:].rearrange("p (c k i) -> p c i k", k=4, i=PACK)
+            if name in V_CASTS:
+                nc.vector.tensor_copy(out=dst, in_=src)
+            else:
+                nc.scalar.copy(out=dst, in_=src)
+
+        def quant(name):
+            nc.vector.quantize_mx(out=codes[name][:].bitcast(FP8X4), scales=scales[name][:], in_=grouped[name][:])
+
+        sil = [[sb(f"sil{q}{g}", [P, 512], F32) for g in range(2)] for q in range(4)]
+        gated = [[sb(f"gated{q}{g}", [P, 512], F32) for g in range(2)] for q in range(4)]
+        h_rows = [[sb(f"h_rows{h}{g}", [P, 2, 512], BF16) for g in range(2)] for h in range(2)]
+        h_cols = [[sb(f"h_cols{h}{g}", [P, 256 * PACK], BF16) for g in range(2)] for h in range(2)]
+        h_w = [[sb(f"h_w{h}{g}", [P, 256], U32) for g in range(2)] for h in range(2)]
+        h_s = [[sb(f"h_s{h}{g}", [P, 256], U8) for g in range(2)] for h in range(2)]
+        d_sb = sb("d_sb", [P, 4, S], F32)
+        res = [[sb(f"res{g}{m}", [P, 2, 256], F32) for m in range(2)] for g in range(2)]
+        w2_s = planes["w2"][0]
+        w4_s = planes["w4"][0]
+
+        def mm_a(q, g):
+            for i in range(2):
+                js = slice(128 * (2 * g + i), 128 * (2 * g + i + 1))
+                for a in range(2):
+                    name = f"w1q{q}p{a}"
+                    nc.tensor.matmul_mx(out=banks[g][:, 256 * i : 256 * (i + 1)], lhsT=v_w[a][:, js].bitcast(FP8X4), lhsT_scale=v_s[a][:, js],
+                                        rhs=codes[name][:].bitcast(FP8X4), rhs_scale=scales[name][:], start=(a == 0), stop=(a == 1))
+
+        def mm_b(q, g):
+            for i in range(2):
+                js = slice(128 * (2 * g + i), 128 * (2 * g + i + 1))
+                for e in range(2):
+                    c0 = (q % 2) * 256 + 128 * e
+                    r0 = q * 256 + 128 * e
+                    for a in range(2):
+                        nc.tensor.matmul_mx(out=banks[2 + g][:, 256 * i + 128 * e : 256 * i + 128 * (e + 1)],
+                                            lhsT=v_w[a][:, js].bitcast(FP8X4), lhsT_scale=v_s[a][:, js],
+                                            rhs=w2_w[q // 2][:, a, 2 * c0 : 2 * c0 + 256].bitcast(FP4X4),
+                                            rhs_scale=w2_s[:, H * a + r0 : H * a + r0 + 128], start=(a == 0), stop=(a == 1))
+
+        def mm_c(q, g):
+            name = f"w3q{q}"
+            for i in range(2):
+                js = slice(128 * (2 * g + i), 128 * (2 * g + i + 1))
+                nc.tensor.matmul_mx(out=banks[4 + g][:, 256 * i : 256 * (i + 1)], lhsT=v2_w[:, js].bitcast(FP8X4), lhsT_scale=v2_s[:, js],
+                                    rhs=codes[name][:].bitcast(FP8X4), rhs_scale=scales[name][:], start=True, stop=True)
+
+        def silu(q, g):
+            nc.scalar.activation(out=sil[q][g][:], in_=banks[g][:], func=SILU)
+
+        def gate(q, g):
+            nc.vector.tensor_tensor(out=gated[q][g][:], in0=banks[2 + g][:], in1=sil[q][g][:], op=MULT)
+
+        def plus(q, g):
+            c0 = (q % 2) * 256
+            nc.vector.tensor_tensor(out=h_rows[q // 2][g][:, :, c0 : c0 + 256],
+                                    in0=banks[4 + g][:].rearrange("p (i c) -> p i c", i=2),
+                                    in1=gated[q][g][:].rearrange("p (i c) -> p i c", i=2), op=ADD)
+
+        def turn(h, g):
+            words = h_rows[h][g][:].rearrange("p i r -> p (i r)").bitcast(F32)
+            for i in range(2):
+                for u in range(2):
+                    nc.tensor.transpose(banks[6 + g][:, 256 * u + 128 * i : 256 * u + 128 * (i + 1)],
+                                        words[:, 256 * i + u : 256 * (i + 1) : 2], ident[:])
+
+        def turn_out(h, g):
+            nc.scalar.copy(out=h_cols[h][g][:].bitcast(F32).rearrange("p (j u) -> p j u", u=2),
+                           in_=banks[6 + g][:].rearrange("p (u j) -> p j u", u=2))
+
+        def quant_h(h, g):
+            nc.vector.quantize_mx(out=h_w[h][g][:].bitcast(FP8X4), scales=h_s[h][g][:], in_=h_cols[h][g][:])
+
+        def mm_d(nt):
+            name = f"w5h{nt // 2}"
+            ns = slice(128 * (nt % 2), 128 * (nt % 2 + 1))
+            nc.tensor.matmul_mx(out=banks[6 + nt % 2][:], lhsT=codes[name][:, ns].bitcast(FP8X4), lhsT_scale=scales[name][:, ns],
+                                rhs=v3_w[:].bitcast(FP4X4), rhs_scale=v3_s[:], start=True, stop=True)
+            nc.scalar.copy(out=d_sb[:, nt, :], in_=banks[6 + nt % 2][:])
+
+        def mm_y(h, g, m):
+            for i in range(2):
+                n0 = 128 * (2 * m + i)
+                nc.tensor.matmul_mx(out=banks[2 * g + m][:, 256 * i : 256 * (i + 1)],
+                                    lhsT=w4_w[:, h, n0 : n0 + 128].bitcast(FP8X4), lhsT_scale=w4_s[:, N * h + n0 : N * h + n0 + 128],
+                                    rhs=h_w[h][g][:].bitcast(FP8X4), rhs_scale=h_s[h][g][:],
+                                    start=(h == 0 and i == 0), stop=(h == 1 and i == 1))
+
+        def finish(g, m):
+            nc.vector.tensor_tensor(out=res[g][m][:], in0=banks[2 * g + m][:].rearrange("p (i j) -> p i j", i=2),
+                                    in1=d_sb[:, 2 * m : 2 * m + 2, 256 * g : 256 * (g + 1)], op=MULT)
+            nc.sync.dma_start(out=out[256 * m : 256 * (m + 1), 256 * g : 256 * (g + 1)].rearrange("(i p) j -> p i j", p=P),
+                              in_=res[g][m][:])
+
+        for step in STEPS:
+            kind = step[0]
+            if kind == "g":
+                dst, window, key = gathers[step[1]]
+                nc.vector.tensor_copy(dst[:], window.indirect(lists[key][:]))
+            elif kind == "cast":
+                cast(step[1])
+            elif kind == "quant":
+                quant(step[1])
+            else:
+                {"a": mm_a, "b": mm_b, "c": mm_c, "silu": silu, "gate": gate, "plus": plus, "turn": turn, "turn_out": turn_out,
+                 "qh": quant_h, "d": mm_d, "y": mm_y, "fin": finish}[kind](*step[1:])

@@ -20,11 +20,13 @@ ADD = mybir.AluOpType.add
 
 P = 128
 PACK = 4
-QW = 256
-LOAD_ORDER = ["offs","offs2","offs3","w1q0p0","tabp0","s:tab","w1q0p1","tabp1","w2h0","s:w2","w1q1p0","tab2","s:tab2","w1q1p1","w3q0","w3q1","w2h1","w1q2p0","w1q2p1","w1q3p0","w1q3p1","w3q2","w3q3","tab3","w5h0","w5h1","w4","s:tab3","s:w4"]
-SCALE_ORDER = [["tab","sync"],["w2","sync"],["tab2","sync"],["tab3","gpsimd"],["w4","gpsimd"]]
-V_CASTS = ["w3q1","w3q3"]
-STEPS = [["g","gw0"],["g","gs0"],["g","gs1"],["g","gw1"],["cast","w1q0p0"],["cast","w1q0p1"],["quant","w1q0p0"],["quant","w1q0p1"],["a",0,0],["a",0,1],["b",0,0],["b",0,1],["silu",0,0],["silu",0,1],["gate",0,0],["gate",0,1],["cast","w1q1p0"],["cast","w1q1p1"],["quant","w1q1p0"],["quant","w1q1p1"],["a",1,0],["a",1,1],["b",1,0],["b",1,1],["silu",1,0],["silu",1,1],["gate",1,0],["gate",1,1],["cast","w1q2p0"],["cast","w1q2p1"],["quant","w1q2p0"],["quant","w1q2p1"],["a",2,0],["a",2,1],["b",2,0],["b",2,1],["silu",2,0],["silu",2,1],["gate",2,0],["gate",2,1],["g","g2s"],["g","g2w"],["cast","w1q3p0"],["cast","w1q3p1"],["quant","w1q3p0"],["quant","w1q3p1"],["a",3,0],["a",3,1],["b",3,0],["b",3,1],["silu",3,0],["silu",3,1],["gate",3,0],["gate",3,1],["cast","w3q0"],["quant","w3q0"],["c",0,0],["c",0,1],["plus",0,0],["plus",0,1],["cast","w3q1"],["quant","w3q1"],["c",1,0],["c",1,1],["plus",1,0],["plus",1,1],["cast","w3q2"],["quant","w3q2"],["c",2,0],["c",2,1],["plus",2,0],["plus",2,1],["cast","w3q3"],["quant","w3q3"],["c",3,0],["c",3,1],["plus",3,0],["plus",3,1],["turn",0,0],["turn",0,1],["turn_out",0,0],["turn_out",0,1],["qh",0,0],["qh",0,1],["y",0,0,0],["y",0,0,1],["y",0,1,0],["y",0,1,1],["turn",1,0],["turn_out",1,0],["turn",1,1],["turn_out",1,1],["g","g3s"],["g","g3w"],["cast","w5h0"],["cast","w5h1"],["quant","w5h0"],["quant","w5h1"],["d",0],["d",1],["d",2],["d",3],["qh",1,0],["y",1,0,0],["y",1,0,1],["qh",1,1],["fin",0,0],["fin",0,1],["y",1,1,0],["y",1,1,1],["fin",1,0],["fin",1,1]]
+PASS = P * PACK
+BANK = 512
+PIECE = 256
+QUARTERS = H // PIECE
+PAIR = 2 * P
+TAB2_ROW0 = 8
+W4_ROW0 = 4
 
 
 def tile_list_abbreviation_expansion_features_kernel(
@@ -36,202 +38,276 @@ def tile_list_abbreviation_expansion_features_kernel(
         keep = ctx.enter_context(tc.tile_pool(name="keep", bufs=1))
         psum = ctx.enter_context(tc.psum_pool(name="psum", bufs=1))
 
-        def sb(name, shape, dtype):
+        def sbuf(name, shape, dtype):
             return keep.tile(shape, dtype, name=name, align_bytes=64)
 
-        lists = {"offs": keep.tile([P, S // 16], U16, name="list1"), "offs2": keep.tile([P, S // 16], U16, name="list2"),
-                 "offs3": keep.tile([P, S // 16], U16, name="list3")}
-        list_src = {"offs": offs, "offs2": offs2, "offs3": offs3}
-        banks = [psum.tile([P, 512], F32, name=f"bank{i}") for i in range(8)]
+        list1 = keep.tile([P, S // 16], U16, name="list1")
+        list2 = keep.tile([P, S // 16], U16, name="list2")
+        list3 = keep.tile([P, S // 16], U16, name="list3")
 
-        tab_w = [sb(f"tab_w{a}", [P, T], U32) for a in range(2)]
-        tab2_w = sb("tab2_w", [P, T2], U32)
-        tab3_w = sb("tab3_w", [P, T3], U16)
-        planes = {
-            "tab": (sb("tab_s", [P, 2 * T], U8), tab_scales),
-            "tab2": (sb("tab2_s", [P, T2], U8), tab2_scales),
-            "tab3": (sb("tab3_s", [P, T3], U8), tab3_scales),
-            "w2": (sb("w2_s", [P, 2 * H], U8), w2_scales),
-            "w4": (sb("w4_s", [P, 2 * N], U8), w4_scales),
-        }
-        w2_w = [sb(f"w2_w{h}", [P, 2, H], U8) for h in range(2)]
-        w4_w = sb("w4_w", [P, 2, N], U32)
-        raw = {}
-        for q in range(4):
-            for a in range(2):
-                raw[f"w1q{q}p{a}"] = (sb(f"w1raw{q}{a}", [P, PACK, QW], F32), w1[512 * a : 512 * (a + 1), QW * q : QW * (q + 1)])
-            raw[f"w3q{q}"] = (sb(f"w3raw{q}", [P, PACK, QW], F32), w3[:, QW * q : QW * (q + 1)])
-        for q in range(2):
-            raw[f"w5h{q}"] = (sb(f"w5raw{q}", [P, PACK, QW], F32), w5[:, QW * q : QW * (q + 1)])
+        banks = [psum.tile([P, BANK], F32, name=f"bank{i}") for i in range(8)]
+        a_bank, b_bank, c_bank, turn_bank = banks[0:2], banks[2:4], banks[4:6], banks[6:8]
+        y_bank = [[a_bank[g], b_bank[g]] for g in range(2)]
 
-        for name, queue in SCALE_ORDER:
-            nc.vector.memset(planes[name][0][:].bitcast(I32), 0)
+        tab_w = [sbuf(f"tab_w{a}", [P, T], U32) for a in range(2)]
+        tab2_w = sbuf("tab2_w", [P, T2], U32)
+        tab3_w = sbuf("tab3_w", [P, T3], U16)
+        tab_s = sbuf("tab_s", [P, 2 * T], U8)
+        tab2_s = sbuf("tab2_s", [P, T2], U8)
+        tab3_s = sbuf("tab3_s", [P, T3], U8)
+        w2_s = sbuf("w2_s", [P, 2 * H], U8)
+        w4_s = sbuf("w4_s", [P, 2 * N], U8)
+        w2_w = [sbuf(f"w2_w{half}", [P, 2, H], U8) for half in range(2)]
+        w4_w = sbuf("w4_w", [P, 2, N], U32)
 
-        def load_scales(name, queue):
-            tile, src = planes[name]
-            passes = src.shape[0]
-            eng = {"sync": nc.sync, "scalar": nc.scalar, "gpsimd": nc.gpsimd}[queue]
+        def piece(name, rows):
+            return {
+                "rows": rows,
+                "raw": sbuf("raw_" + name, [P, PACK * PIECE], F32),
+                "grouped": sbuf("grouped_" + name, [P, PIECE * PACK], BF16),
+                "codes": sbuf("codes_" + name, [P, PIECE], U32),
+                "plane": sbuf("plane_" + name, [P, PIECE], U8),
+            }
+
+        def columns(i):
+            return slice(PIECE * i, PIECE * (i + 1))
+
+        w1_piece = [[piece(f"w1_{q}{a}", w1[PASS * a : PASS * (a + 1), columns(q)]) for a in range(2)] for q in range(QUARTERS)]
+        w3_piece = [piece(f"w3_{q}", w3[:, columns(q)]) for q in range(QUARTERS)]
+        w5_piece = [piece(f"w5_{i}", w5[:, columns(i)]) for i in range(N // PIECE)]
+
+        nc.vector.memset(tab3_s[:].bitcast(I32), 0)
+        nc.gpsimd.memset(tab_s[:].bitcast(I32), 0)
+        for plane in (w2_s, w4_s, tab2_s):
+            nc.vector.memset(plane[:].bitcast(I32), 0)
+
+        def load_plane(queue, plane, scales, row0):
             for quad in range(4):
-                eng.dma_start(
-                    out=tile[32 * quad : 32 * quad + 4, :].bitcast(I32).rearrange("r (a t) -> r a t", a=passes),
-                    in_=src[:, 4 * quad : 4 * quad + 4, :].bitcast(I32).rearrange("a r t -> r a t"),
+                first = 32 * quad + row0
+                queue.dma_start(
+                    out=plane[first : first + 4, :].bitcast(I32).rearrange("r (a t) -> r a t", a=scales.shape[0]),
+                    in_=scales[:, 4 * quad : 4 * quad + 4, :].bitcast(I32).rearrange("a r t -> r a t"),
                 )
 
-        def load(name):
-            if name in lists:
-                nc.sync.dma_start(lists[name][:], list_src[name])
-            elif name in raw:
-                tile, src = raw[name]
-                nc.sync.dma_start(out=tile[:], in_=src.rearrange("(p i) c -> p i c", i=PACK))
-            elif name.startswith("tabp"):
-                a = int(name[4])
-                nc.sync.dma_start(out=tab_w[a][:].bitcast(I32), in_=tab_words[a].rearrange("p t i -> p (t i)").bitcast(I32))
-            elif name == "tab2":
-                nc.sync.dma_start(out=tab2_w[:].bitcast(I32), in_=tab2_words[0].rearrange("p t i -> p (t i)").bitcast(I32))
-            elif name == "tab3":
-                nc.sync.dma_start(out=tab3_w[:].bitcast(I32), in_=tab3_words[0].bitcast(I32))
-            elif name.startswith("w2h"):
-                h = int(name[3])
-                nc.sync.dma_start(out=w2_w[h][:].bitcast(I32),
-                                  in_=w2_words[:, :, H * h : H * (h + 1)].bitcast(I32).rearrange("a p b -> p a b"))
-            elif name == "w4":
-                nc.sync.dma_start(out=w4_w[:].bitcast(I32),
-                                  in_=w4_words.rearrange("a p e i -> a p (e i)").bitcast(I32).rearrange("a p e -> p a e"))
-            elif name.startswith("s:"):
-                load_scales(name[2:], dict(SCALE_ORDER)[name[2:]])
+        def load_piece(part):
+            nc.sync.dma_start(
+                out=part["raw"][:].rearrange("p (i c) -> p i c", i=PACK),
+                in_=part["rows"].rearrange("(p i) c -> p i c", i=PACK),
+            )
 
-        for name in LOAD_ORDER:
-            load(name)
+        def load_e4m3_words(tile, words):
+            nc.sync.dma_start(out=tile[:].bitcast(I32), in_=words.rearrange("p t i -> p (t i)").bitcast(I32))
 
-        ident = sb("ident", [P, P], F32)
+        def load_w2(half):
+            nc.sync.dma_start(
+                out=w2_w[half][:].bitcast(I32),
+                in_=w2_words[:, :, H * half : H * (half + 1)].bitcast(I32).rearrange("a p b -> p a b"),
+            )
+
+        load_piece(w1_piece[0][0])
+        nc.sync.dma_start(list3[:], offs3)
+        nc.sync.dma_start(out=tab3_w[:].bitcast(I32), in_=tab3_words[0].bitcast(I32))
+        load_plane(nc.sync, tab3_s, tab3_scales, 0)
+        load_e4m3_words(tab_w[0], tab_words[0])
+        nc.sync.dma_start(list1[:], offs)
+        load_piece(w1_piece[0][1])
+        load_e4m3_words(tab_w[1], tab_words[1])
+        load_w2(0)
+        nc.sync.dma_start(list2[:], offs2)
+        load_e4m3_words(tab2_w, tab2_words[0])
+        load_piece(w3_piece[0])
+        load_plane(nc.sync, tab2_s, tab2_scales, TAB2_ROW0)
+        for q in range(1, QUARTERS):
+            if q == QUARTERS // 2:
+                load_w2(1)
+            load_piece(w1_piece[q][0])
+            load_piece(w1_piece[q][1])
+            load_piece(w3_piece[q])
+        nc.sync.dma_start(
+            out=w4_w[:].bitcast(I32),
+            in_=w4_words.rearrange("a p e i -> a p (e i)").bitcast(I32).rearrange("a p e -> p a e"),
+        )
+        for part in w5_piece:
+            load_piece(part)
+        load_plane(nc.gpsimd, tab_s, tab_scales, 0)
+        load_plane(nc.gpsimd, w2_s, w2_scales, 0)
+        load_plane(nc.gpsimd, w4_s, w4_scales, W4_ROW0)
+
+        ident = sbuf("ident", [P, P], F32)
         make_identity(nc, ident[:])
 
-        v_w = [sb(f"v_w{a}", [P, S], U32) for a in range(2)]
-        v_s = [sb(f"v_s{a}", [P, S], U8) for a in range(2)]
-        v2_w = sb("v2_w", [P, S], U32)
-        v2_s = sb("v2_s", [P, S], U8)
-        v3_w = sb("v3_w", [P, S], U16)
-        v3_s = sb("v3_s", [P, S], U8)
-        gathers = {
-            "gs0": (v_s[0], planes["tab"][0][:, 0:T], "offs"),
-            "gs1": (v_s[1], planes["tab"][0][:, T : 2 * T], "offs"),
-            "gw0": (v_w[0], tab_w[0][:], "offs"),
-            "gw1": (v_w[1], tab_w[1][:], "offs"),
-            "g2s": (v2_s, planes["tab2"][0][:], "offs2"),
-            "g2w": (v2_w, tab2_w[:], "offs2"),
-            "g3s": (v3_s, planes["tab3"][0][:], "offs3"),
-            "g3w": (v3_w, tab3_w[:], "offs3"),
-        }
+        v_w = [sbuf(f"v_w{a}", [P, S], U32) for a in range(2)]
+        v_s = [sbuf(f"v_s{a}", [P, S], U8) for a in range(2)]
+        v2_w = sbuf("v2_w", [P, S], U32)
+        v2_s = sbuf("v2_s", [P, S], U8)
+        v3_w = sbuf("v3_w", [P, S], U16)
+        v3_s = sbuf("v3_s", [P, S], U8)
 
-        grouped = {name: sb("g_" + name, [P, QW * PACK], BF16) for name in raw}
-        codes = {name: sb("c_" + name, [P, QW], U32) for name in raw}
-        scales = {name: sb("s_" + name, [P, QW], U8) for name in raw}
+        def gather(picked, window, entries):
+            nc.vector.tensor_copy(picked[:], window.indirect(entries[:]))
 
-        def cast(name):
-            src = raw[name][0][:].rearrange("p i (c k) -> p c i k", k=4)
-            dst = grouped[name][:].rearrange("p (c k i) -> p c i k", k=4, i=PACK)
-            if name in V_CASTS:
+        def round_piece(part, on_vector):
+            src = part["raw"][:].rearrange("p (i c e) -> p c i e", i=PACK, e=4)
+            dst = part["grouped"][:].rearrange("p (c e i) -> p c i e", e=4, i=PACK)
+            if on_vector:
                 nc.vector.tensor_copy(out=dst, in_=src)
             else:
                 nc.scalar.copy(out=dst, in_=src)
 
-        def quant(name):
-            nc.vector.quantize_mx(out=codes[name][:].bitcast(FP8X4), scales=scales[name][:], in_=grouped[name][:])
+        def quantise_piece(part):
+            nc.vector.quantize_mx(out=part["codes"][:].bitcast(FP8X4), scales=part["plane"][:], in_=part["grouped"][:])
 
-        sil = [[sb(f"sil{q}{g}", [P, 512], F32) for g in range(2)] for q in range(4)]
-        gated = [[sb(f"gated{q}{g}", [P, 512], F32) for g in range(2)] for q in range(4)]
-        h_rows = [[sb(f"h_rows{h}{g}", [P, 2, 512], BF16) for g in range(2)] for h in range(2)]
-        h_cols = [[sb(f"h_cols{h}{g}", [P, 256 * PACK], BF16) for g in range(2)] for h in range(2)]
-        h_w = [[sb(f"h_w{h}{g}", [P, 256], U32) for g in range(2)] for h in range(2)]
-        h_s = [[sb(f"h_s{h}{g}", [P, 256], U8) for g in range(2)] for h in range(2)]
-        d_sb = sb("d_sb", [P, 4, S], F32)
-        res = [[sb(f"res{g}{m}", [P, 2, 256], F32) for m in range(2)] for g in range(2)]
-        w2_s = planes["w2"][0]
-        w4_s = planes["w4"][0]
+        def prepare(parts, on_vector):
+            for part, flag in zip(parts, on_vector):
+                round_piece(part, flag)
+            for part in parts:
+                quantise_piece(part)
 
-        def mm_a(q, g):
+        last = QUARTERS - 1
+        silu_a = [[w1_piece[q + 1][0]["raw"][:, BANK * g : BANK * (g + 1)] for g in range(2)] for q in range(last)]
+        silu_a.append([sbuf(f"silu_last{g}", [P, BANK], F32)[:] for g in range(2)])
+        gated = [[sbuf(f"gated{q}{g}", [P, BANK], F32) for g in range(2)] for q in range(QUARTERS)]
+        h_rows = [[sbuf(f"h_rows{a}{g}", [P, 2, PASS], BF16) for g in range(2)] for a in range(2)]
+        h_cols = [sbuf(f"h_cols{a}", [P, S * PACK], BF16) for a in range(2)]
+        h_w = [sbuf(f"h_w{a}", [P, S], U32) for a in range(2)]
+        h_s = [sbuf(f"h_s{a}", [P, S], U8) for a in range(2)]
+        d_sb = sbuf("d_sb", [P, N // P, S], F32)
+        result = [[sbuf(f"result{g}{m}", [P, 2, PAIR], F32) for m in range(2)] for g in range(2)]
+
+        def positions(g, i):
+            return slice(PAIR * g + P * i, PAIR * g + P * (i + 1))
+
+        def gated_product(q, g):
             for i in range(2):
-                js = slice(128 * (2 * g + i), 128 * (2 * g + i + 1))
+                js = positions(g, i)
                 for a in range(2):
-                    name = f"w1q{q}p{a}"
-                    nc.tensor.matmul_mx(out=banks[g][:, 256 * i : 256 * (i + 1)], lhsT=v_w[a][:, js].bitcast(FP8X4), lhsT_scale=v_s[a][:, js],
-                                        rhs=codes[name][:].bitcast(FP8X4), rhs_scale=scales[name][:], start=(a == 0), stop=(a == 1))
-
-        def mm_b(q, g):
+                    nc.tensor.matmul_mx(
+                        out=a_bank[g][:, columns(i)], lhsT=v_w[a][:, js].bitcast(FP8X4), lhsT_scale=v_s[a][:, js],
+                        rhs=w1_piece[q][a]["codes"][:].bitcast(FP8X4), rhs_scale=w1_piece[q][a]["plane"][:],
+                        start=(a == 0), stop=(a == 1),
+                    )
             for i in range(2):
-                js = slice(128 * (2 * g + i), 128 * (2 * g + i + 1))
-                for e in range(2):
-                    c0 = (q % 2) * 256 + 128 * e
-                    r0 = q * 256 + 128 * e
+                js = positions(g, i)
+                for e in range(PIECE // P):
+                    r0 = PIECE * q + P * e
+                    byte0 = 2 * (r0 % PASS)
                     for a in range(2):
-                        nc.tensor.matmul_mx(out=banks[2 + g][:, 256 * i + 128 * e : 256 * i + 128 * (e + 1)],
-                                            lhsT=v_w[a][:, js].bitcast(FP8X4), lhsT_scale=v_s[a][:, js],
-                                            rhs=w2_w[q // 2][:, a, 2 * c0 : 2 * c0 + 256].bitcast(FP4X4),
-                                            rhs_scale=w2_s[:, H * a + r0 : H * a + r0 + 128], start=(a == 0), stop=(a == 1))
+                        nc.tensor.matmul_mx(
+                            out=b_bank[g][:, PIECE * i + P * e : PIECE * i + P * (e + 1)],
+                            lhsT=v_w[a][:, js].bitcast(FP8X4), lhsT_scale=v_s[a][:, js],
+                            rhs=w2_w[r0 // PASS][:, a, byte0 : byte0 + 2 * P].bitcast(FP4X4),
+                            rhs_scale=w2_s[:, H * a + r0 : H * a + r0 + P],
+                            start=(a == 0), stop=(a == 1),
+                        )
+            nc.scalar.activation(out=silu_a[q][g], in_=a_bank[g][:], func=SILU)
+            nc.vector.tensor_tensor(out=gated[q][g][:], in0=b_bank[g][:], in1=silu_a[q][g], op=MULT)
 
-        def mm_c(q, g):
-            name = f"w3q{q}"
+        def add_sense(q, g):
             for i in range(2):
-                js = slice(128 * (2 * g + i), 128 * (2 * g + i + 1))
-                nc.tensor.matmul_mx(out=banks[4 + g][:, 256 * i : 256 * (i + 1)], lhsT=v2_w[:, js].bitcast(FP8X4), lhsT_scale=v2_s[:, js],
-                                    rhs=codes[name][:].bitcast(FP8X4), rhs_scale=scales[name][:], start=True, stop=True)
+                js = positions(g, i)
+                nc.tensor.matmul_mx(
+                    out=c_bank[g][:, columns(i)], lhsT=v2_w[:, js].bitcast(FP8X4), lhsT_scale=v2_s[TAB2_ROW0:, js],
+                    rhs=w3_piece[q]["codes"][:].bitcast(FP8X4), rhs_scale=w3_piece[q]["plane"][:], start=True, stop=True,
+                )
+            nc.vector.tensor_tensor(
+                out=h_rows[q // 2][g][:, :, columns(q % 2)],
+                in0=c_bank[g][:].rearrange("p (i c) -> p i c", i=2),
+                in1=gated[q][g][:].rearrange("p (i c) -> p i c", i=2), op=ADD,
+            )
 
-        def silu(q, g):
-            nc.scalar.activation(out=sil[q][g][:], in_=banks[g][:], func=SILU)
-
-        def gate(q, g):
-            nc.vector.tensor_tensor(out=gated[q][g][:], in0=banks[2 + g][:], in1=sil[q][g][:], op=MULT)
-
-        def plus(q, g):
-            c0 = (q % 2) * 256
-            nc.vector.tensor_tensor(out=h_rows[q // 2][g][:, :, c0 : c0 + 256],
-                                    in0=banks[4 + g][:].rearrange("p (i c) -> p i c", i=2),
-                                    in1=gated[q][g][:].rearrange("p (i c) -> p i c", i=2), op=ADD)
-
-        def turn(h, g):
-            words = h_rows[h][g][:].rearrange("p i r -> p (i r)").bitcast(F32)
+        def turn_h(a, g):
+            words = h_rows[a][g][:].rearrange("p i r -> p (i r)").bitcast(F32)
             for i in range(2):
                 for u in range(2):
-                    nc.tensor.transpose(banks[6 + g][:, 256 * u + 128 * i : 256 * u + 128 * (i + 1)],
-                                        words[:, 256 * i + u : 256 * (i + 1) : 2], ident[:])
+                    nc.tensor.transpose(
+                        turn_bank[g][:, PAIR * u + P * i : PAIR * u + P * (i + 1)],
+                        words[:, 2 * P * i + u : 2 * P * (i + 1) : 2], ident[:],
+                    )
+            nc.scalar.copy(
+                out=h_cols[a][:, PACK * PAIR * g : PACK * PAIR * (g + 1)].bitcast(F32).rearrange("p (j u) -> p j u", u=2),
+                in_=turn_bank[g][:].rearrange("p (u j) -> p j u", u=2),
+            )
 
-        def turn_out(h, g):
-            nc.scalar.copy(out=h_cols[h][g][:].bitcast(F32).rearrange("p (j u) -> p j u", u=2),
-                           in_=banks[6 + g][:].rearrange("p (u j) -> p j u", u=2))
+        def quantise_h(a, g):
+            js = slice(PAIR * g, PAIR * (g + 1))
+            nc.vector.quantize_mx(
+                out=h_w[a][:, js].bitcast(FP8X4), scales=h_s[a][:, js], in_=h_cols[a][:, PACK * PAIR * g : PACK * PAIR * (g + 1)],
+            )
 
-        def quant_h(h, g):
-            nc.vector.quantize_mx(out=h_w[h][g][:].bitcast(FP8X4), scales=h_s[h][g][:], in_=h_cols[h][g][:])
+        def mix(a, g):
+            js = slice(PAIR * g, PAIR * (g + 1))
+            for m in range(2):
+                for i in range(2):
+                    n0 = P * (2 * m + i)
+                    nc.tensor.matmul_mx(
+                        out=y_bank[g][m][:, PAIR * i : PAIR * (i + 1)], lhsT=w4_w[:, a, n0 : n0 + P].bitcast(FP8X4),
+                        lhsT_scale=w4_s[W4_ROW0:, N * a + n0 : N * a + n0 + P],
+                        rhs=h_w[a][:, js].bitcast(FP8X4), rhs_scale=h_s[a][:, js],
+                        start=(a == 0 and i == 0), stop=(a == 1 and i == 1),
+                    )
 
-        def mm_d(nt):
-            name = f"w5h{nt // 2}"
-            ns = slice(128 * (nt % 2), 128 * (nt % 2 + 1))
-            nc.tensor.matmul_mx(out=banks[6 + nt % 2][:], lhsT=codes[name][:, ns].bitcast(FP8X4), lhsT_scale=scales[name][:, ns],
-                                rhs=v3_w[:].bitcast(FP4X4), rhs_scale=v3_s[:], start=True, stop=True)
-            nc.scalar.copy(out=d_sb[:, nt, :], in_=banks[6 + nt % 2][:])
-
-        def mm_y(h, g, m):
-            for i in range(2):
-                n0 = 128 * (2 * m + i)
-                nc.tensor.matmul_mx(out=banks[2 * g + m][:, 256 * i : 256 * (i + 1)],
-                                    lhsT=w4_w[:, h, n0 : n0 + 128].bitcast(FP8X4), lhsT_scale=w4_s[:, N * h + n0 : N * h + n0 + 128],
-                                    rhs=h_w[h][g][:].bitcast(FP8X4), rhs_scale=h_s[h][g][:],
-                                    start=(h == 0 and i == 0), stop=(h == 1 and i == 1))
+        def domain(tile):
+            part = w5_piece[tile // 2]
+            ns = slice(P * (tile % 2), P * (tile % 2 + 1))
+            bank = c_bank[tile % 2]
+            nc.tensor.matmul_mx(
+                out=bank[:], lhsT=part["codes"][:, ns].bitcast(FP8X4), lhsT_scale=part["plane"][:, ns],
+                rhs=v3_w[:].bitcast(FP4X4), rhs_scale=v3_s[:], start=True, stop=True,
+            )
+            if tile == 0:
+                nc.vector.tensor_copy(out=d_sb[:, tile, :], in_=bank[:])
+            else:
+                nc.scalar.copy(out=d_sb[:, tile, :], in_=bank[:])
 
         def finish(g, m):
-            nc.vector.tensor_tensor(out=res[g][m][:], in0=banks[2 * g + m][:].rearrange("p (i j) -> p i j", i=2),
-                                    in1=d_sb[:, 2 * m : 2 * m + 2, 256 * g : 256 * (g + 1)], op=MULT)
-            nc.sync.dma_start(out=out[256 * m : 256 * (m + 1), 256 * g : 256 * (g + 1)].rearrange("(i p) j -> p i j", p=P),
-                              in_=res[g][m][:])
+            js = slice(PAIR * g, PAIR * (g + 1))
+            nc.vector.tensor_tensor(
+                out=result[g][m][:], in0=y_bank[g][m][:].rearrange("p (i j) -> p i j", i=2),
+                in1=d_sb[:, 2 * m : 2 * m + 2, js], op=MULT,
+            )
+            nc.sync.dma_start(out=out[2 * P * m : 2 * P * (m + 1), js].rearrange("(i p) j -> p i j", p=P), in_=result[g][m][:])
 
-        for step in STEPS:
-            kind = step[0]
-            if kind == "g":
-                dst, window, key = gathers[step[1]]
-                nc.vector.tensor_copy(dst[:], window.indirect(lists[key][:]))
-            elif kind == "cast":
-                cast(step[1])
-            elif kind == "quant":
-                quant(step[1])
+        gather(v3_s, tab3_s[:], list3)
+        gather(v3_w, tab3_w[:], list3)
+        gather(v_w[0], tab_w[0][:], list1)
+        gather(v_s[0], tab_s[:, 0:T], list1)
+        gather(v_s[1], tab_s[:, T : 2 * T], list1)
+        gather(v_w[1], tab_w[1][:], list1)
+
+        for q in range(QUARTERS):
+            prepare(w1_piece[q], [False, q > 0])
+            if q == 0:
+                gather(v2_s, tab2_s[:], list2)
+                gather(v2_w, tab2_w[:], list2)
             else:
-                {"a": mm_a, "b": mm_b, "c": mm_c, "silu": silu, "gate": gate, "plus": plus, "turn": turn, "turn_out": turn_out,
-                 "qh": quant_h, "d": mm_d, "y": mm_y, "fin": finish}[kind](*step[1:])
+                for g in range(2):
+                    gated_product(q - 1, g)
+                for g in range(2):
+                    add_sense(q - 1, g)
+            prepare([w3_piece[q]], [False])
+        for g in range(2):
+            turn_h(0, g)
+        for g in range(2):
+            quantise_h(0, g)
+
+        gated_product(last, 0)
+        add_sense(last, 0)
+        turn_h(1, 0)
+        prepare(w5_piece, [False, False])
+        mix(0, 0)
+        gated_product(last, 1)
+        add_sense(last, 1)
+        turn_h(1, 1)
+        domain(0)
+        domain(1)
+        mix(0, 1)
+        quantise_h(1, 0)
+        mix(1, 0)
+        domain(2)
+        domain(3)
+        finish(0, 0)
+        quantise_h(1, 1)
+        mix(1, 1)
+        finish(1, 0)
+        finish(0, 1)
+        finish(1, 1)

@@ -25,8 +25,8 @@ BANK = 512
 PIECE = 256
 QUARTERS = H // PIECE
 PAIR = 2 * P
-TAB2_ROW0 = 8
 W4_ROW0 = 4
+ROWS = 16
 
 
 def tile_list_abbreviation_expansion_features_kernel(
@@ -46,8 +46,9 @@ def tile_list_abbreviation_expansion_features_kernel(
         list3 = keep.tile([P, S // 16], U16, name="list3")
 
         banks = [psum.tile([P, BANK], F32, name=f"bank{i}") for i in range(8)]
-        a_bank, b_bank, c_bank, turn_bank = banks[0:2], banks[2:4], banks[4:6], banks[6:8]
-        y_bank = [[a_bank[g], b_bank[g]] for g in range(2)]
+        a_bank, b_bank, c_bank = banks[0:2], banks[2:4], banks[4:6]
+        turn_bank = [banks[6:8], c_bank]
+        y_bank = [banks[6:8], b_bank]
 
         tab_w = [sbuf(f"tab_w{a}", [P, T], U32) for a in range(2)]
         tab2_w = sbuf("tab2_w", [P, T2], U32)
@@ -76,18 +77,31 @@ def tile_list_abbreviation_expansion_features_kernel(
         w3_piece = [piece(f"w3_{q}", w3[:, columns(q)]) for q in range(QUARTERS)]
         w5_piece = [piece(f"w5_{i}", w5[:, columns(i)]) for i in range(N // PIECE)]
 
-        nc.vector.memset(tab3_s[:].bitcast(I32), 0)
-        nc.gpsimd.memset(tab_s[:].bitcast(I32), 0)
-        for plane in (w2_s, w4_s, tab2_s):
+        picked1_s = sbuf("picked1_s", [P, 4 * S], U8)
+        planes1 = sbuf("planes1", [P, 4 * S], U8)
+        warm = sbuf("warm", [P, 16], F32)
+        nc.vector.memset(warm[:, 0:8], 0.0)
+        nc.scalar.activation(out=warm[:, 8:9], in_=warm[:, 0:1], func=SILU)
+        for plane in (tab_s, tab2_s, tab3_s, planes1, w4_s):
             nc.vector.memset(plane[:].bitcast(I32), 0)
+        nc.gpsimd.memset(w2_s[:].bitcast(I32), 0)
 
-        def load_plane(queue, plane, scales, row0):
-            for quad in range(4):
-                first = 32 * quad + row0
+        def load_plane(queue, plane, scales, row0, rows):
+            for r in rows:
                 queue.dma_start(
-                    out=plane[first : first + 4, :].bitcast(I32).rearrange("r (a t) -> r a t", a=scales.shape[0]),
-                    in_=scales[:, 4 * quad : 4 * quad + 4, :].bitcast(I32).rearrange("a r t -> r a t"),
+                    out=plane[row0 + r : P : 32, :].bitcast(I32).rearrange("q (a t) -> q a t", a=scales.shape[0]),
+                    in_=scales[:, r:ROWS:4, :].bitcast(I32).rearrange("a q t -> q a t"),
                 )
+
+        def load_rows(tile, scales):
+            nc.sync.dma_start(
+                out=tile[0:P:8, :].bitcast(I32).rearrange("s (a t) -> s a t", a=scales.shape[0]),
+                in_=scales.bitcast(I32).rearrange("a s t -> s a t"),
+            )
+
+        def place_rows(planes, picked):
+            for r in range(4):
+                nc.sync.dma_start(out=planes[r:P:32, :].bitcast(I32), in_=picked[8 * r : P : 32, :].bitcast(I32))
 
         def load_piece(part):
             nc.sync.dma_start(
@@ -104,47 +118,56 @@ def tile_list_abbreviation_expansion_features_kernel(
                 in_=w2_words[:, :, H * half : H * (half + 1)].bitcast(I32).rearrange("a p b -> p a b"),
             )
 
-        load_piece(w1_piece[0][0])
-        nc.sync.dma_start(list3[:], offs3)
-        nc.sync.dma_start(out=tab3_w[:].bitcast(I32), in_=tab3_words[0].bitcast(I32))
-        load_plane(nc.sync, tab3_s, tab3_scales, 0)
-        load_e4m3_words(tab_w[0], tab_words[0])
+        v_w = [sbuf(f"v_w{a}", [P, S], U32) for a in range(2)]
+        v2_w = sbuf("v2_w", [P, S], U32)
+        v3_w = sbuf("v3_w", [P, S], U16)
+        v_s = [planes1[:, 0:S], planes1[:, S : 2 * S]]
+        v2_s = planes1[:, 2 * S : 3 * S]
+        v3_s = planes1[:, 3 * S : 4 * S]
+
+        def gather(picked, window, entries):
+            nc.vector.tensor_copy(picked, window.indirect(entries[:]))
+
         nc.sync.dma_start(list1[:], offs)
+        load_piece(w1_piece[0][0])
+        load_rows(tab_s, tab_scales)
+        nc.sync.dma_start(list2[:], offs2)
+        load_rows(tab2_s, tab2_scales)
+        nc.sync.dma_start(list3[:], offs3)
+        load_rows(tab3_s, tab3_scales)
+        load_e4m3_words(tab_w[0], tab_words[0])
         load_piece(w1_piece[0][1])
         load_e4m3_words(tab_w[1], tab_words[1])
+        gather(picked1_s[:, 0:S], tab_s[:, 0:T], list1)
+        gather(picked1_s[:, S : 2 * S], tab_s[:, T : 2 * T], list1)
+        gather(picked1_s[:, 2 * S : 3 * S], tab2_s[:], list2)
+        gather(picked1_s[:, 3 * S : 4 * S], tab3_s[:], list3)
         load_w2(0)
-        nc.sync.dma_start(list2[:], offs2)
+        place_rows(planes1, picked1_s)
+        nc.sync.dma_start(out=tab3_w[:].bitcast(I32), in_=tab3_words[0].bitcast(I32))
+        load_piece(w1_piece[1][0])
         load_e4m3_words(tab2_w, tab2_words[0])
         load_piece(w3_piece[0])
-        load_plane(nc.sync, tab2_s, tab2_scales, TAB2_ROW0)
-        for q in range(1, QUARTERS):
-            if q == QUARTERS // 2:
-                load_w2(1)
-            load_piece(w1_piece[q][0])
-            load_piece(w1_piece[q][1])
-            load_piece(w3_piece[q])
+        load_piece(w1_piece[1][1])
+        load_piece(w3_piece[1])
+        load_piece(w1_piece[2][0])
+        load_w2(1)
+        load_piece(w1_piece[2][1])
+        load_piece(w3_piece[2])
+        load_piece(w1_piece[3][0])
+        load_piece(w1_piece[3][1])
+        load_piece(w3_piece[3])
         nc.sync.dma_start(
             out=w4_w[:].bitcast(I32),
             in_=w4_words.rearrange("a p e i -> a p (e i)").bitcast(I32).rearrange("a p e -> p a e"),
         )
-        for part in w5_piece:
-            load_piece(part)
-        load_plane(nc.gpsimd, tab_s, tab_scales, 0)
-        load_plane(nc.gpsimd, w2_s, w2_scales, 0)
-        load_plane(nc.gpsimd, w4_s, w4_scales, W4_ROW0)
+        load_piece(w5_piece[0])
+        load_piece(w5_piece[1])
+        load_plane(nc.gpsimd, w2_s, w2_scales, 0, range(4))
+        load_plane(nc.gpsimd, w4_s, w4_scales, W4_ROW0, range(4))
 
         ident = sbuf("ident", [P, P], F32)
         make_identity(nc, ident[:])
-
-        v_w = [sbuf(f"v_w{a}", [P, S], U32) for a in range(2)]
-        v_s = [sbuf(f"v_s{a}", [P, S], U8) for a in range(2)]
-        v2_w = sbuf("v2_w", [P, S], U32)
-        v2_s = sbuf("v2_s", [P, S], U8)
-        v3_w = sbuf("v3_w", [P, S], U16)
-        v3_s = sbuf("v3_s", [P, S], U8)
-
-        def gather(picked, window, entries):
-            nc.vector.tensor_copy(picked[:], window.indirect(entries[:]))
 
         def round_piece(part, on_vector):
             src = part["raw"][:].rearrange("p (i c e) -> p c i e", i=PACK, e=4)
@@ -164,11 +187,10 @@ def tile_list_abbreviation_expansion_features_kernel(
                 quantise_piece(part)
 
         last = QUARTERS - 1
-        silu_a = [[w1_piece[q + 1][0]["raw"][:, BANK * g : BANK * (g + 1)] for g in range(2)] for q in range(last)]
-        silu_a.append([sbuf(f"silu_last{g}", [P, BANK], F32)[:] for g in range(2)])
-        gated = [[sbuf(f"gated{q}{g}", [P, BANK], F32) for g in range(2)] for q in range(QUARTERS)]
+        silu_a = [[sbuf(f"silu0{g}", [P, BANK], F32)[:] for g in range(2)], [w1_piece[2][0]["raw"][:, BANK * g : BANK * (g + 1)] for g in range(2)], [w1_piece[3][0]["raw"][:, BANK * g : BANK * (g + 1)] for g in range(2)], [sbuf(f"silu3{g}", [P, BANK], F32)[:] for g in range(2)]]
+        gated = [[sbuf(f"gated0{g}", [P, BANK], F32)[:] for g in range(2)], [sbuf(f"gated1{g}", [P, BANK], F32)[:] for g in range(2)], [sbuf(f"gated2{g}", [P, BANK], F32)[:] for g in range(2)], [sbuf(f"gated3{g}", [P, BANK], F32)[:] for g in range(2)]]
         h_rows = [[sbuf(f"h_rows{a}{g}", [P, 2, PASS], BF16) for g in range(2)] for a in range(2)]
-        h_cols = [sbuf(f"h_cols{a}", [P, S * PACK], BF16) for a in range(2)]
+        h_cols = [w3_piece[3]["raw"][:].bitcast(BF16), sbuf("h_cols1", [P, S * PACK], BF16)[:]]
         h_w = [sbuf(f"h_w{a}", [P, S], U32) for a in range(2)]
         h_s = [sbuf(f"h_s{a}", [P, S], U8) for a in range(2)]
         d_sb = sbuf("d_sb", [P, N // P, S], F32)
@@ -178,41 +200,41 @@ def tile_list_abbreviation_expansion_features_kernel(
             return slice(PAIR * g + P * i, PAIR * g + P * (i + 1))
 
         def gated_product(q, g):
-            for i in range(2):
-                js = positions(g, i)
-                for a in range(2):
+            for a in range(2):
+                for i in range(2):
+                    js = positions(g, i)
                     nc.tensor.matmul_mx(
                         out=a_bank[g][:, columns(i)], lhsT=v_w[a][:, js].bitcast(FP8X4), lhsT_scale=v_s[a][:, js],
                         rhs=w1_piece[q][a]["codes"][:].bitcast(FP8X4), rhs_scale=w1_piece[q][a]["plane"][:],
-                        start=(a == 0), stop=(a == 1),
+                        start=(a == 0 and i == 0), stop=(a == 1 and i == 1),
                     )
-            for i in range(2):
-                js = positions(g, i)
-                for e in range(PIECE // P):
-                    r0 = PIECE * q + P * e
-                    byte0 = 2 * (r0 % PASS)
-                    for a in range(2):
+            for a in range(2):
+                for i in range(2):
+                    js = positions(g, i)
+                    for e in range(PIECE // P):
+                        r0 = PIECE * q + P * e
+                        byte0 = 2 * (r0 % PASS)
                         nc.tensor.matmul_mx(
                             out=b_bank[g][:, PIECE * i + P * e : PIECE * i + P * (e + 1)],
                             lhsT=v_w[a][:, js].bitcast(FP8X4), lhsT_scale=v_s[a][:, js],
                             rhs=w2_w[r0 // PASS][:, a, byte0 : byte0 + 2 * P].bitcast(FP4X4),
                             rhs_scale=w2_s[:, H * a + r0 : H * a + r0 + P],
-                            start=(a == 0), stop=(a == 1),
+                            start=(a == 0 and i == 0 and e == 0), stop=(a == 1 and i == 1 and e == 1),
                         )
             nc.scalar.activation(out=silu_a[q][g], in_=a_bank[g][:], func=SILU)
-            nc.vector.tensor_tensor(out=gated[q][g][:], in0=b_bank[g][:], in1=silu_a[q][g], op=MULT)
+            nc.vector.tensor_tensor(out=gated[q][g], in0=b_bank[g][:], in1=silu_a[q][g], op=MULT)
 
         def add_sense(q, g):
             for i in range(2):
                 js = positions(g, i)
                 nc.tensor.matmul_mx(
-                    out=c_bank[g][:, columns(i)], lhsT=v2_w[:, js].bitcast(FP8X4), lhsT_scale=v2_s[TAB2_ROW0:, js],
+                    out=c_bank[g][:, columns(i)], lhsT=v2_w[:, js].bitcast(FP8X4), lhsT_scale=v2_s[:, js],
                     rhs=w3_piece[q]["codes"][:].bitcast(FP8X4), rhs_scale=w3_piece[q]["plane"][:], start=True, stop=True,
                 )
             nc.vector.tensor_tensor(
                 out=h_rows[q // 2][g][:, :, columns(q % 2)],
                 in0=c_bank[g][:].rearrange("p (i c) -> p i c", i=2),
-                in1=gated[q][g][:].rearrange("p (i c) -> p i c", i=2), op=ADD,
+                in1=gated[q][g].rearrange("p (i c) -> p i c", i=2), op=ADD,
             )
 
         def turn_h(a, g):
@@ -220,12 +242,12 @@ def tile_list_abbreviation_expansion_features_kernel(
             for i in range(2):
                 for u in range(2):
                     nc.tensor.transpose(
-                        turn_bank[g][:, PAIR * u + P * i : PAIR * u + P * (i + 1)],
+                        turn_bank[a][g][:, PAIR * u + P * i : PAIR * u + P * (i + 1)],
                         words[:, 2 * P * i + u : 2 * P * (i + 1) : 2], ident[:],
                     )
             nc.scalar.copy(
                 out=h_cols[a][:, PACK * PAIR * g : PACK * PAIR * (g + 1)].bitcast(F32).rearrange("p (j u) -> p j u", u=2),
-                in_=turn_bank[g][:].rearrange("p (u j) -> p j u", u=2),
+                in_=turn_bank[a][g][:].rearrange("p (u j) -> p j u", u=2),
             )
 
         def quantise_h(a, g):
@@ -249,15 +271,12 @@ def tile_list_abbreviation_expansion_features_kernel(
         def domain(tile):
             part = w5_piece[tile // 2]
             ns = slice(P * (tile % 2), P * (tile % 2 + 1))
-            bank = c_bank[tile % 2]
+            bank = a_bank[tile % 2]
             nc.tensor.matmul_mx(
                 out=bank[:], lhsT=part["codes"][:, ns].bitcast(FP8X4), lhsT_scale=part["plane"][:, ns],
-                rhs=v3_w[:].bitcast(FP4X4), rhs_scale=v3_s[:], start=True, stop=True,
+                rhs=v3_w[:].bitcast(FP4X4), rhs_scale=v3_s, start=True, stop=True,
             )
-            if tile == 0:
-                nc.vector.tensor_copy(out=d_sb[:, tile, :], in_=bank[:])
-            else:
-                nc.scalar.copy(out=d_sb[:, tile, :], in_=bank[:])
+            nc.scalar.copy(out=d_sb[:, tile, :], in_=bank[:])
 
         def finish(g, m):
             js = slice(PAIR * g, PAIR * (g + 1))
@@ -267,47 +286,58 @@ def tile_list_abbreviation_expansion_features_kernel(
             )
             nc.sync.dma_start(out=out[2 * P * m : 2 * P * (m + 1), js].rearrange("(i p) j -> p i j", p=P), in_=result[g][m][:])
 
-        gather(v3_s, tab3_s[:], list3)
-        gather(v3_w, tab3_w[:], list3)
-        gather(v_w[0], tab_w[0][:], list1)
-        gather(v_s[0], tab_s[:, 0:T], list1)
-        gather(v_s[1], tab_s[:, T : 2 * T], list1)
-        gather(v_w[1], tab_w[1][:], list1)
+        gather(v_w[0][:], tab_w[0][:], list1)
+        gather(v_w[1][:], tab_w[1][:], list1)
 
-        for q in range(QUARTERS):
-            prepare(w1_piece[q], [False, q > 0])
-            if q == 0:
-                gather(v2_s, tab2_s[:], list2)
-                gather(v2_w, tab2_w[:], list2)
-            else:
-                for g in range(2):
-                    gated_product(q - 1, g)
-                for g in range(2):
-                    add_sense(q - 1, g)
-            prepare([w3_piece[q]], [False])
-        for g in range(2):
-            turn_h(0, g)
-        for g in range(2):
-            quantise_h(0, g)
-
-        gated_product(last, 0)
-        add_sense(last, 0)
-        turn_h(1, 0)
-        prepare(w5_piece, [False, False])
+        prepare([w1_piece[0][0]], [False])
+        prepare([w1_piece[0][1]], [False])
+        gather(v3_w[:], tab3_w[:], list3)
+        gated_product(0, 0)
+        gated_product(0, 1)
+        prepare([w1_piece[1][0]], [False])
+        gather(v2_w[:], tab2_w[:], list2)
+        prepare([w3_piece[0]], [False])
+        add_sense(0, 0)
+        add_sense(0, 1)
+        prepare([w1_piece[1][1]], [False])
+        prepare([w3_piece[1]], [True])
+        prepare([w1_piece[2][0]], [False])
+        gated_product(1, 0)
+        gated_product(1, 1)
+        add_sense(1, 0)
+        add_sense(1, 1)
+        prepare([w1_piece[2][1]], [True])
+        prepare([w3_piece[2]], [False])
+        prepare([w1_piece[3][0]], [False])
+        gated_product(2, 0)
+        gated_product(2, 1)
+        add_sense(2, 0)
+        add_sense(2, 1)
+        prepare([w1_piece[3][1]], [True])
+        prepare([w3_piece[3]], [False])
+        turn_h(0, 0)
+        turn_h(0, 1)
+        quantise_h(0, 0)
+        quantise_h(0, 1)
         mix(0, 0)
-        gated_product(last, 1)
-        add_sense(last, 1)
+        gated_product(3, 0)
+        gated_product(3, 1)
+        mix(0, 1)
+        add_sense(3, 0)
+        add_sense(3, 1)
+        prepare([w5_piece[0]], [False])
+        turn_h(1, 0)
         turn_h(1, 1)
         domain(0)
         domain(1)
-        mix(0, 1)
         quantise_h(1, 0)
+        prepare([w5_piece[1]], [True])
         mix(1, 0)
+        quantise_h(1, 1)
+        mix(1, 1)
         domain(2)
         domain(3)
         finish(0, 0)
-        quantise_h(1, 1)
-        mix(1, 1)
         finish(1, 0)
         finish(0, 1)
         finish(1, 1)

@@ -46,9 +46,10 @@ def tile_list_abbreviation_expansion_features_kernel(
         list3 = keep.tile([P, S // 16], U16, name="list3")
 
         banks = [psum.tile([P, BANK], F32, name=f"bank{i}") for i in range(8)]
-        a_bank, b_bank, c_bank = banks[0:2], banks[2:4], banks[4:6]
-        turn_bank = [banks[6:8], c_bank]
-        y_bank = [banks[6:8], b_bank]
+        a_bank, b_bank, c_bank = banks[0:2], banks[2:4], banks[4:8]
+        turn_bank = [a_bank, [c_bank[0], c_bank[2]]]
+        y_bank = [b_bank, a_bank]
+        d_bank = [c_bank[1], c_bank[3]]
 
         tab_w = [sbuf(f"tab_w{a}", [P, T], U32) for a in range(2)]
         tab2_w = sbuf("tab2_w", [P, T2], U32)
@@ -61,10 +62,10 @@ def tile_list_abbreviation_expansion_features_kernel(
         w2_w = [sbuf(f"w2_w{half}", [P, 2, H], U8) for half in range(2)]
         w4_w = sbuf("w4_w", [P, 2, N], U32)
 
-        def piece(name, rows):
+        def piece(name, rows, raw=None):
             return {
                 "rows": rows,
-                "raw": sbuf("raw_" + name, [P, PACK * PIECE], F32),
+                "raw": sbuf("raw_" + name, [P, PACK * PIECE], F32)[:] if raw is None else raw,
                 "grouped": sbuf("grouped_" + name, [P, PIECE * PACK], BF16),
                 "codes": sbuf("codes_" + name, [P, PIECE], U32),
                 "plane": sbuf("plane_" + name, [P, PIECE], U8),
@@ -73,7 +74,12 @@ def tile_list_abbreviation_expansion_features_kernel(
         def columns(i):
             return slice(PIECE * i, PIECE * (i + 1))
 
-        w1_piece = [[piece(f"w1_{q}{a}", w1[PASS * a : PASS * (a + 1), columns(q)]) for a in range(2)] for q in range(QUARTERS)]
+        slot = PACK * PIECE
+        shared = sbuf("shared", [P, (QUARTERS + 1) * slot], F32)
+        w1_piece = [
+            [piece(f"w1_{q}0", w1[0:PASS, columns(q)]), piece(f"w1_{q}1", w1[PASS:K, columns(q)], shared[:, slot * q : slot * (q + 1)])]
+            for q in range(QUARTERS)
+        ]
         w3_piece = [piece(f"w3_{q}", w3[:, columns(q)]) for q in range(QUARTERS)]
         w5_piece = [piece(f"w5_{i}", w5[:, columns(i)]) for i in range(N // PIECE)]
 
@@ -82,9 +88,9 @@ def tile_list_abbreviation_expansion_features_kernel(
         warm = sbuf("warm", [P, 16], F32)
         nc.vector.memset(warm[:, 0:8], 0.0)
         nc.scalar.activation(out=warm[:, 8:9], in_=warm[:, 0:1], func=SILU)
-        for plane in (tab_s, tab2_s, tab3_s, planes1, w4_s):
+        for plane in (tab_s, tab2_s, tab3_s, w2_s, planes1):
             nc.vector.memset(plane[:].bitcast(I32), 0)
-        nc.gpsimd.memset(w2_s[:].bitcast(I32), 0)
+        nc.gpsimd.memset(w4_s[:].bitcast(I32), 0)
 
         def load_plane(queue, plane, scales, row0, rows):
             for r in rows:
@@ -105,7 +111,7 @@ def tile_list_abbreviation_expansion_features_kernel(
 
         def load_piece(part):
             nc.sync.dma_start(
-                out=part["raw"][:].rearrange("p (i c) -> p i c", i=PACK),
+                out=part["raw"].rearrange("p (i c) -> p i c", i=PACK),
                 in_=part["rows"].rearrange("(p i) c -> p i c", i=PACK),
             )
 
@@ -138,40 +144,42 @@ def tile_list_abbreviation_expansion_features_kernel(
         load_e4m3_words(tab_w[0], tab_words[0])
         load_piece(w1_piece[0][1])
         load_e4m3_words(tab_w[1], tab_words[1])
+        load_piece(w1_piece[1][0])
         gather(picked1_s[:, 0:S], tab_s[:, 0:T], list1)
         gather(picked1_s[:, S : 2 * S], tab_s[:, T : 2 * T], list1)
         gather(picked1_s[:, 2 * S : 3 * S], tab2_s[:], list2)
         gather(picked1_s[:, 3 * S : 4 * S], tab3_s[:], list3)
-        load_w2(0)
         place_rows(planes1, picked1_s)
-        nc.sync.dma_start(out=tab3_w[:].bitcast(I32), in_=tab3_words[0].bitcast(I32))
-        load_piece(w1_piece[1][0])
-        load_e4m3_words(tab2_w, tab2_words[0])
-        load_piece(w3_piece[0])
         load_piece(w1_piece[1][1])
-        load_piece(w3_piece[1])
+        load_plane(nc.sync, w2_s, w2_scales, 0, range(0, 2))
+        load_w2(0)
+        load_plane(nc.sync, w2_s, w2_scales, 0, range(2, 4))
+        nc.sync.dma_start(out=tab3_w[:].bitcast(I32), in_=tab3_words[0].bitcast(I32))
         load_piece(w1_piece[2][0])
         load_w2(1)
         load_piece(w1_piece[2][1])
-        load_piece(w3_piece[2])
         load_piece(w1_piece[3][0])
+        load_e4m3_words(tab2_w, tab2_words[0])
         load_piece(w1_piece[3][1])
+        load_piece(w3_piece[0])
+        load_piece(w3_piece[1])
+        load_piece(w3_piece[2])
         load_piece(w3_piece[3])
+        load_piece(w5_piece[0])
         nc.sync.dma_start(
             out=w4_w[:].bitcast(I32),
             in_=w4_words.rearrange("a p e i -> a p (e i)").bitcast(I32).rearrange("a p e -> p a e"),
         )
-        load_piece(w5_piece[0])
         load_piece(w5_piece[1])
-        load_plane(nc.gpsimd, w2_s, w2_scales, 0, range(4))
         load_plane(nc.gpsimd, w4_s, w4_scales, W4_ROW0, range(4))
 
         ident = sbuf("ident", [P, P], F32)
         make_identity(nc, ident[:])
 
         def round_piece(part, on_vector):
-            src = part["raw"][:].rearrange("p (i c e) -> p c i e", i=PACK, e=4)
-            dst = part["grouped"][:].rearrange("p (c e i) -> p c i e", e=4, i=PACK)
+            run = 2 if on_vector else 4
+            src = part["raw"].rearrange("p (i c e) -> p c i e", i=PACK, e=run)
+            dst = part["grouped"][:].rearrange("p (c e i) -> p c i e", e=run, i=PACK)
             if on_vector:
                 nc.vector.tensor_copy(out=dst, in_=src)
             else:
@@ -187,10 +195,12 @@ def tile_list_abbreviation_expansion_features_kernel(
                 quantise_piece(part)
 
         last = QUARTERS - 1
-        silu_a = [[sbuf(f"silu0{g}", [P, BANK], F32)[:] for g in range(2)], [w1_piece[2][0]["raw"][:, BANK * g : BANK * (g + 1)] for g in range(2)], [w1_piece[3][0]["raw"][:, BANK * g : BANK * (g + 1)] for g in range(2)], [sbuf(f"silu3{g}", [P, BANK], F32)[:] for g in range(2)]]
-        gated = [[sbuf(f"gated0{g}", [P, BANK], F32)[:] for g in range(2)], [sbuf(f"gated1{g}", [P, BANK], F32)[:] for g in range(2)], [sbuf(f"gated2{g}", [P, BANK], F32)[:] for g in range(2)], [sbuf(f"gated3{g}", [P, BANK], F32)[:] for g in range(2)]]
-        h_rows = [[sbuf(f"h_rows{a}{g}", [P, 2, PASS], BF16) for g in range(2)] for a in range(2)]
-        h_cols = [w3_piece[3]["raw"][:].bitcast(BF16), sbuf("h_cols1", [P, S * PACK], BF16)[:]]
+        silu_a = [[w1_piece[q + 1][0]["raw"][:, BANK * g : BANK * (g + 1)] for g in range(2)] for q in range(last)]
+        silu_a.append([w3_piece[0]["raw"][:, BANK * g : BANK * (g + 1)] for g in range(2)])
+        gated = [[shared[:, slot * (q + 1) + BANK * g : slot * (q + 1) + BANK * (g + 1)] for g in range(2)] for q in range(QUARTERS)]
+        h_rows = [[sbuf(f"h_rows{a}{g}", [P, 2, PASS], BF16)[:] for g in range(2)] for a in range(2)]
+        h_rows[0][1] = w3_piece[last]["grouped"][:].rearrange("p (i r) -> p i r", i=2)
+        h_cols = [w5_piece[0]["raw"].bitcast(BF16), sbuf("h_cols1", [P, S * PACK], BF16)[:]]
         h_w = [sbuf(f"h_w{a}", [P, S], U32) for a in range(2)]
         h_s = [sbuf(f"h_s{a}", [P, S], U8) for a in range(2)]
         d_sb = sbuf("d_sb", [P, N // P, S], F32)
@@ -224,17 +234,19 @@ def tile_list_abbreviation_expansion_features_kernel(
             nc.scalar.activation(out=silu_a[q][g], in_=a_bank[g][:], func=SILU)
             nc.vector.tensor_tensor(out=gated[q][g], in0=b_bank[g][:], in1=silu_a[q][g], op=MULT)
 
-        def add_sense(q, g):
-            for i in range(2):
-                js = positions(g, i)
+        def add_sense(a, tile):
+            js = slice(P * tile, P * (tile + 1))
+            for e in range(2):
+                part = w3_piece[2 * a + e]
                 nc.tensor.matmul_mx(
-                    out=c_bank[g][:, columns(i)], lhsT=v2_w[:, js].bitcast(FP8X4), lhsT_scale=v2_s[:, js],
-                    rhs=w3_piece[q]["codes"][:].bitcast(FP8X4), rhs_scale=w3_piece[q]["plane"][:], start=True, stop=True,
+                    out=c_bank[tile][:, columns(e)], lhsT=v2_w[:, js].bitcast(FP8X4), lhsT_scale=v2_s[:, js],
+                    rhs=part["codes"][:].bitcast(FP8X4), rhs_scale=part["plane"][:], start=True, stop=True,
                 )
+            both = shared[:, slot * (2 * a + 1) : slot * (2 * a + 3)].rearrange("p (e c) -> p e c", e=2)
             nc.vector.tensor_tensor(
-                out=h_rows[q // 2][g][:, :, columns(q % 2)],
-                in0=c_bank[g][:].rearrange("p (i c) -> p i c", i=2),
-                in1=gated[q][g].rearrange("p (i c) -> p i c", i=2), op=ADD,
+                out=h_rows[a][tile // 2][:, tile % 2, :].rearrange("p (e c) -> p e c", e=2),
+                in0=c_bank[tile][:].rearrange("p (e c) -> p e c", e=2),
+                in1=both[:, :, columns(tile)], op=ADD,
             )
 
         def turn_h(a, g):
@@ -271,7 +283,7 @@ def tile_list_abbreviation_expansion_features_kernel(
         def domain(tile):
             part = w5_piece[tile // 2]
             ns = slice(P * (tile % 2), P * (tile % 2 + 1))
-            bank = a_bank[tile % 2]
+            bank = d_bank[tile % 2]
             nc.tensor.matmul_mx(
                 out=bank[:], lhsT=part["codes"][:, ns].bitcast(FP8X4), lhsT_scale=part["plane"][:, ns],
                 rhs=v3_w[:].bitcast(FP4X4), rhs_scale=v3_s, start=True, stop=True,
@@ -291,48 +303,52 @@ def tile_list_abbreviation_expansion_features_kernel(
 
         prepare([w1_piece[0][0]], [False])
         prepare([w1_piece[0][1]], [False])
-        gather(v3_w[:], tab3_w[:], list3)
-        gated_product(0, 0)
-        gated_product(0, 1)
         prepare([w1_piece[1][0]], [False])
+        gather(v3_w[:], tab3_w[:], list3)
+        round_piece(w1_piece[1][1], True)
+        gated_product(0, 0)
+        quantise_piece(w1_piece[1][1])
+        gated_product(0, 1)
+        prepare([w1_piece[2][0]], [False])
+        round_piece(w1_piece[2][1], True)
+        gated_product(1, 0)
+        quantise_piece(w1_piece[2][1])
+        gated_product(1, 1)
+        prepare([w1_piece[3][0]], [False])
         gather(v2_w[:], tab2_w[:], list2)
+        round_piece(w1_piece[3][1], True)
+        gated_product(2, 0)
+        quantise_piece(w1_piece[3][1])
+        gated_product(2, 1)
         prepare([w3_piece[0]], [False])
+        round_piece(w3_piece[1], True)
+        gated_product(3, 0)
+        quantise_piece(w3_piece[1])
+        gated_product(3, 1)
         add_sense(0, 0)
         add_sense(0, 1)
-        prepare([w1_piece[1][1]], [False])
-        prepare([w3_piece[1]], [True])
-        prepare([w1_piece[2][0]], [False])
-        gated_product(1, 0)
-        gated_product(1, 1)
-        add_sense(1, 0)
-        add_sense(1, 1)
-        prepare([w1_piece[2][1]], [True])
         prepare([w3_piece[2]], [False])
-        prepare([w1_piece[3][0]], [False])
-        gated_product(2, 0)
-        gated_product(2, 1)
-        add_sense(2, 0)
-        add_sense(2, 1)
-        prepare([w1_piece[3][1]], [True])
         prepare([w3_piece[3]], [False])
+        add_sense(0, 2)
+        add_sense(0, 3)
+        prepare([w5_piece[0]], [False])
         turn_h(0, 0)
         turn_h(0, 1)
         quantise_h(0, 0)
-        quantise_h(0, 1)
         mix(0, 0)
-        gated_product(3, 0)
-        gated_product(3, 1)
+        quantise_h(0, 1)
         mix(0, 1)
-        add_sense(3, 0)
-        add_sense(3, 1)
-        prepare([w5_piece[0]], [False])
+        add_sense(1, 0)
+        add_sense(1, 1)
         turn_h(1, 0)
-        turn_h(1, 1)
         domain(0)
-        domain(1)
+        add_sense(1, 2)
+        add_sense(1, 3)
+        turn_h(1, 1)
+        prepare([w5_piece[1]], [False])
         quantise_h(1, 0)
-        prepare([w5_piece[1]], [True])
         mix(1, 0)
+        domain(1)
         quantise_h(1, 1)
         mix(1, 1)
         domain(2)

@@ -49,7 +49,7 @@ def tile_list_abbreviation_expansion_features_kernel(
         a_bank, b_bank, c_bank = banks[0:2], banks[2:4], banks[4:8]
         turn_bank = [a_bank, [c_bank[0], c_bank[2]]]
         y_bank = [b_bank, a_bank]
-        d_bank = [c_bank[1], c_bank[3]]
+        d_bank = [a_bank[0], a_bank[1], c_bank[1], c_bank[3]]
 
         tab_w = [sbuf(f"tab_w{a}", [P, T], U32) for a in range(2)]
         tab2_w = sbuf("tab2_w", [P, T2], U32)
@@ -166,24 +166,26 @@ def tile_list_abbreviation_expansion_features_kernel(
         load_piece(w3_piece[2])
         load_piece(w3_piece[3])
         load_piece(w5_piece[0])
+        load_piece(w5_piece[1])
         nc.sync.dma_start(
             out=w4_w[:].bitcast(I32),
             in_=w4_words.rearrange("a p e i -> a p (e i)").bitcast(I32).rearrange("a p e -> p a e"),
         )
-        load_piece(w5_piece[1])
         load_plane(nc.gpsimd, w4_s, w4_scales, W4_ROW0, range(4))
 
         ident = sbuf("ident", [P, P], F32)
         make_identity(nc, ident[:])
 
         def round_piece(part, on_vector):
-            run = 2 if on_vector else 4
-            src = part["raw"].rearrange("p (i c e) -> p c i e", i=PACK, e=run)
-            dst = part["grouped"][:].rearrange("p (c e i) -> p c i e", e=run, i=PACK)
             if on_vector:
-                nc.vector.tensor_copy(out=dst, in_=src)
+                nc.vector.tensor_copy(
+                    out=part["grouped"][:].rearrange("p (c i) -> p c i", i=PACK), in_=part["raw"].rearrange("p (i c) -> p c i", i=PACK),
+                )
             else:
-                nc.scalar.copy(out=dst, in_=src)
+                nc.scalar.copy(
+                    out=part["grouped"][:].rearrange("p (c e i) -> p c i e", e=4, i=PACK),
+                    in_=part["raw"].rearrange("p (i c e) -> p c i e", i=PACK, e=4),
+                )
 
         def quantise_piece(part):
             nc.vector.quantize_mx(out=part["codes"][:].bitcast(FP8X4), scales=part["plane"][:], in_=part["grouped"][:])
@@ -200,7 +202,7 @@ def tile_list_abbreviation_expansion_features_kernel(
         gated = [[shared[:, slot * (q + 1) + BANK * g : slot * (q + 1) + BANK * (g + 1)] for g in range(2)] for q in range(QUARTERS)]
         h_rows = [[sbuf(f"h_rows{a}{g}", [P, 2, PASS], BF16)[:] for g in range(2)] for a in range(2)]
         h_rows[0][1] = w3_piece[last]["grouped"][:].rearrange("p (i r) -> p i r", i=2)
-        h_cols = [w5_piece[0]["raw"].bitcast(BF16), sbuf("h_cols1", [P, S * PACK], BF16)[:]]
+        h_cols = [[w5_piece[g]["raw"][:, 0:BANK].bitcast(BF16) for g in range(2)], [sbuf(f"h_cols1{g}", [P, PAIR * PACK], BF16)[:] for g in range(2)]]
         h_w = [sbuf(f"h_w{a}", [P, S], U32) for a in range(2)]
         h_s = [sbuf(f"h_s{a}", [P, S], U8) for a in range(2)]
         d_sb = sbuf("d_sb", [P, N // P, S], F32)
@@ -258,14 +260,14 @@ def tile_list_abbreviation_expansion_features_kernel(
                         words[:, 2 * P * i + u : 2 * P * (i + 1) : 2], ident[:],
                     )
             nc.scalar.copy(
-                out=h_cols[a][:, PACK * PAIR * g : PACK * PAIR * (g + 1)].bitcast(F32).rearrange("p (j u) -> p j u", u=2),
+                out=h_cols[a][g].bitcast(F32).rearrange("p (j u) -> p j u", u=2),
                 in_=turn_bank[a][g][:].rearrange("p (u j) -> p j u", u=2),
             )
 
         def quantise_h(a, g):
             js = slice(PAIR * g, PAIR * (g + 1))
             nc.vector.quantize_mx(
-                out=h_w[a][:, js].bitcast(FP8X4), scales=h_s[a][:, js], in_=h_cols[a][:, PACK * PAIR * g : PACK * PAIR * (g + 1)],
+                out=h_w[a][:, js].bitcast(FP8X4), scales=h_s[a][:, js], in_=h_cols[a][g],
             )
 
         def mix(a, g):
@@ -283,7 +285,7 @@ def tile_list_abbreviation_expansion_features_kernel(
         def domain(tile):
             part = w5_piece[tile // 2]
             ns = slice(P * (tile % 2), P * (tile % 2 + 1))
-            bank = d_bank[tile % 2]
+            bank = d_bank[tile]
             nc.tensor.matmul_mx(
                 out=bank[:], lhsT=part["codes"][:, ns].bitcast(FP8X4), lhsT_scale=part["plane"][:, ns],
                 rhs=v3_w[:].bitcast(FP4X4), rhs_scale=v3_s, start=True, stop=True,
@@ -333,27 +335,27 @@ def tile_list_abbreviation_expansion_features_kernel(
         add_sense(0, 3)
         prepare([w5_piece[0]], [False])
         turn_h(0, 0)
+        prepare([w5_piece[1]], [False])
         turn_h(0, 1)
         quantise_h(0, 0)
         mix(0, 0)
+        domain(0)
         quantise_h(0, 1)
-        mix(0, 1)
         add_sense(1, 0)
         add_sense(1, 1)
         turn_h(1, 0)
-        domain(0)
+        domain(1)
         add_sense(1, 2)
+        domain(2)
         add_sense(1, 3)
         turn_h(1, 1)
-        prepare([w5_piece[1]], [False])
         quantise_h(1, 0)
         mix(1, 0)
-        domain(1)
+        domain(3)
+        mix(0, 1)
         quantise_h(1, 1)
         mix(1, 1)
-        domain(2)
-        domain(3)
         finish(0, 0)
-        finish(1, 0)
         finish(0, 1)
+        finish(1, 0)
         finish(1, 1)

@@ -25,8 +25,8 @@ BANK = 512
 PIECE = 256
 QUARTERS = H // PIECE
 PAIR = 2 * P
-W4_ROW0 = 4
 ROWS = 16
+W4_ROW0 = 4
 
 
 def tile_list_abbreviation_expansion_features_kernel(
@@ -46,10 +46,6 @@ def tile_list_abbreviation_expansion_features_kernel(
         list3 = keep.tile([P, S // 16], U16, name="list3")
 
         banks = [psum.tile([P, BANK], F32, name=f"bank{i}") for i in range(8)]
-        a_bank, b_bank, c_bank = banks[0:2], banks[2:4], banks[4:8]
-        turn_bank = [a_bank, [c_bank[0], c_bank[2]]]
-        y_bank = [b_bank, a_bank]
-        d_bank = [a_bank[0], a_bank[1], c_bank[1], c_bank[3]]
 
         tab_w = [sbuf(f"tab_w{a}", [P, T], U32) for a in range(2)]
         tab2_w = sbuf("tab2_w", [P, T2], U32)
@@ -59,57 +55,37 @@ def tile_list_abbreviation_expansion_features_kernel(
         tab3_s = sbuf("tab3_s", [P, T3], U8)
         w2_s = sbuf("w2_s", [P, 2 * H], U8)
         w4_s = sbuf("w4_s", [P, 2 * N], U8)
-        w2_w = [sbuf(f"w2_w{half}", [P, 2, H], U8) for half in range(2)]
+        w2_w = [sbuf(f"w2_w{half}", [P, 2 * PASS], U16) for half in range(2)]
+        w2_dealt = [sbuf(f"w2_dealt{half}", [P, 2 * PASS], U16) for half in range(2)]
+        w2_s_dealt = [w2_w[half][:].bitcast(U8)[:, 0 : 2 * PASS] for half in range(2)]
         w4_w = sbuf("w4_w", [P, 2, N], U32)
 
-        def piece(name, rows, raw=None):
+        def operand(name, rows, lead=0):
+            room = sbuf("raw_" + name, [P, lead + PACK * PASS], F32)
             return {
                 "rows": rows,
-                "raw": sbuf("raw_" + name, [P, PACK * PIECE], F32)[:] if raw is None else raw,
-                "grouped": sbuf("grouped_" + name, [P, PIECE * PACK], BF16),
-                "codes": sbuf("codes_" + name, [P, PIECE], U32),
-                "plane": sbuf("plane_" + name, [P, PIECE], U8),
+                "room": room,
+                "raw": room[:, lead : lead + PACK * PASS],
+                "grouped": sbuf("grouped_" + name, [P, PASS * PACK], BF16)[:],
+                "codes": sbuf("codes_" + name, [P, PASS], U32),
+                "plane": sbuf("plane_" + name, [P, PASS], U8),
             }
 
         def columns(i):
             return slice(PIECE * i, PIECE * (i + 1))
 
-        slot = PACK * PIECE
-        shared = sbuf("shared", [P, (QUARTERS + 1) * slot], F32)
-        w1_piece = [
-            [piece(f"w1_{q}0", w1[0:PASS, columns(q)]), piece(f"w1_{q}1", w1[PASS:K, columns(q)], shared[:, slot * q : slot * (q + 1)])]
-            for q in range(QUARTERS)
-        ]
-        w3_piece = [piece(f"w3_{q}", w3[:, columns(q)]) for q in range(QUARTERS)]
-        w5_piece = [piece(f"w5_{i}", w5[:, columns(i)]) for i in range(N // PIECE)]
+        w1_q = [[operand(f"w1_{half}{a}", w1[PASS * a : PASS * (a + 1), PASS * half : PASS * (half + 1)]) for a in range(2)] for half in range(2)]
+        w3_q = [operand("w3_0", w3[:, 0:PASS]), operand("w3_1", w3[:, PASS:H], 3 * PIECE)]
+        w5_q = operand("w5", w5, PIECE)
 
-        picked1_s = sbuf("picked1_s", [P, 4 * S], U8)
-        planes1 = sbuf("planes1", [P, 4 * S], U8)
-        warm = sbuf("warm", [P, 16], F32)
-        nc.vector.memset(warm[:, 0:8], 0.0)
-        nc.scalar.activation(out=warm[:, 8:9], in_=warm[:, 0:1], func=SILU)
-        for plane in (tab_s, tab2_s, tab3_s, w2_s, planes1):
-            nc.vector.memset(plane[:].bitcast(I32), 0)
-        nc.gpsimd.memset(w4_s[:].bitcast(I32), 0)
-
-        def load_plane(queue, plane, scales, row0, rows):
-            for r in rows:
+        def load_plane(queue, plane, scales, row0):
+            for r in range(4):
                 queue.dma_start(
                     out=plane[row0 + r : P : 32, :].bitcast(I32).rearrange("q (a t) -> q a t", a=scales.shape[0]),
                     in_=scales[:, r:ROWS:4, :].bitcast(I32).rearrange("a q t -> q a t"),
                 )
 
-        def load_rows(tile, scales):
-            nc.sync.dma_start(
-                out=tile[0:P:8, :].bitcast(I32).rearrange("s (a t) -> s a t", a=scales.shape[0]),
-                in_=scales.bitcast(I32).rearrange("a s t -> s a t"),
-            )
-
-        def place_rows(planes, picked):
-            for r in range(4):
-                nc.sync.dma_start(out=planes[r:P:32, :].bitcast(I32), in_=picked[8 * r : P : 32, :].bitcast(I32))
-
-        def load_piece(part):
+        def load_block(part):
             nc.sync.dma_start(
                 out=part["raw"].rearrange("p (i c) -> p i c", i=PACK),
                 in_=part["rows"].rearrange("(p i) c -> p i c", i=PACK),
@@ -120,155 +96,167 @@ def tile_list_abbreviation_expansion_features_kernel(
 
         def load_w2(half):
             nc.sync.dma_start(
-                out=w2_w[half][:].bitcast(I32),
+                out=w2_w[half][:].bitcast(I32).rearrange("p (a b) -> p a b", a=2),
                 in_=w2_words[:, :, H * half : H * (half + 1)].bitcast(I32).rearrange("a p b -> p a b"),
+            )
+
+        def load_w4():
+            nc.sync.dma_start(
+                out=w4_w[:].bitcast(I32),
+                in_=w4_words.rearrange("a p e i -> a p (e i)").bitcast(I32).rearrange("a p e -> p a e"),
             )
 
         v_w = [sbuf(f"v_w{a}", [P, S], U32) for a in range(2)]
         v2_w = sbuf("v2_w", [P, S], U32)
         v3_w = sbuf("v3_w", [P, S], U16)
-        v_s = [planes1[:, 0:S], planes1[:, S : 2 * S]]
-        v2_s = planes1[:, 2 * S : 3 * S]
-        v3_s = planes1[:, 3 * S : 4 * S]
+        picked_s = sbuf("picked_s", [P, 4 * S], U8)
+        planes = sbuf("planes", [P, 4 * S], U8)
+        v_s = [planes[:, 0:S], planes[:, S : 2 * S]]
+        v2_s = planes[:, 2 * S : 3 * S]
+        v3_s = planes[:, 3 * S : 4 * S]
+
+        def load_rows(tile, scales):
+            nc.sync.dma_start(
+                out=tile[0:P:8, :].bitcast(I32).rearrange("s (a t) -> s a t", a=scales.shape[0]),
+                in_=scales.bitcast(I32).rearrange("a s t -> s a t"),
+            )
+
+        def place_rows(queue, cols):
+            for r in range(4):
+                queue.dma_start(out=planes[r:P:32, cols].bitcast(I32), in_=picked_s[8 * r : P : 32, cols].bitcast(I32))
 
         def gather(picked, window, entries):
             nc.vector.tensor_copy(picked, window.indirect(entries[:]))
 
-        nc.sync.dma_start(list1[:], offs)
-        load_piece(w1_piece[0][0])
-        load_rows(tab_s, tab_scales)
-        nc.sync.dma_start(list2[:], offs2)
-        load_rows(tab2_s, tab2_scales)
-        nc.sync.dma_start(list3[:], offs3)
-        load_rows(tab3_s, tab3_scales)
-        load_e4m3_words(tab_w[0], tab_words[0])
-        load_piece(w1_piece[0][1])
-        load_e4m3_words(tab_w[1], tab_words[1])
-        load_piece(w1_piece[1][0])
-        gather(picked1_s[:, 0:S], tab_s[:, 0:T], list1)
-        gather(picked1_s[:, S : 2 * S], tab_s[:, T : 2 * T], list1)
-        gather(picked1_s[:, 2 * S : 3 * S], tab2_s[:], list2)
-        gather(picked1_s[:, 3 * S : 4 * S], tab3_s[:], list3)
-        place_rows(planes1, picked1_s)
-        load_piece(w1_piece[1][1])
-        load_plane(nc.sync, w2_s, w2_scales, 0, range(0, 2))
-        load_w2(0)
-        load_plane(nc.sync, w2_s, w2_scales, 0, range(2, 4))
-        nc.sync.dma_start(out=tab3_w[:].bitcast(I32), in_=tab3_words[0].bitcast(I32))
-        load_piece(w1_piece[2][0])
-        load_w2(1)
-        load_piece(w1_piece[2][1])
-        load_piece(w1_piece[3][0])
-        load_e4m3_words(tab2_w, tab2_words[0])
-        load_piece(w1_piece[3][1])
-        load_piece(w3_piece[0])
-        load_piece(w3_piece[1])
-        load_piece(w3_piece[2])
-        load_piece(w3_piece[3])
-        load_piece(w5_piece[0])
-        load_piece(w5_piece[1])
-        nc.sync.dma_start(
-            out=w4_w[:].bitcast(I32),
-            in_=w4_words.rearrange("a p e i -> a p (e i)").bitcast(I32).rearrange("a p e -> p a e"),
-        )
-        load_plane(nc.gpsimd, w4_s, w4_scales, W4_ROW0, range(4))
+        def deal_w2_words(half):
+            nc.vector.tensor_copy(
+                out=w2_dealt[half][:].rearrange("p (a t m) -> p a t m", a=2, t=PACK),
+                in_=w2_w[half][:].rearrange("p (a m t) -> p a t m", a=2, t=PACK),
+            )
 
-        ident = sbuf("ident", [P, P], F32)
-        make_identity(nc, ident[:])
+        def deal_w2_scales(half):
+            nc.vector.tensor_copy(
+                out=w2_s_dealt[half].rearrange("p (a t m) -> p a t m", a=2, t=PACK),
+                in_=w2_s[:].rearrange("p (a r) -> p a r", a=2)[:, :, PASS * half : PASS * (half + 1)].rearrange("p a (m t) -> p a t m", t=PACK),
+            )
 
-        def round_piece(part, on_vector):
-            if on_vector:
-                nc.vector.tensor_copy(
-                    out=part["grouped"][:].rearrange("p (c i) -> p c i", i=PACK), in_=part["raw"].rearrange("p (i c) -> p c i", i=PACK),
-                )
+        def round_piece(part, m0, m1, engine, dealt=True):
+            if dealt:
+                dst = part["grouped"].rearrange("p (t m i) -> p m i t", t=PACK, i=PACK)[:, m0:m1, :, :]
             else:
-                nc.scalar.copy(
-                    out=part["grouped"][:].rearrange("p (c e i) -> p c i e", e=4, i=PACK),
-                    in_=part["raw"].rearrange("p (i c e) -> p c i e", i=PACK, e=4),
-                )
+                dst = part["grouped"].rearrange("p (m t i) -> p m i t", t=PACK, i=PACK)[:, m0:m1, :, :]
+            src = part["raw"].rearrange("p (i m t) -> p m i t", i=PACK, t=PACK)[:, m0:m1, :, :]
+            if engine == "v":
+                nc.vector.tensor_copy(out=dst, in_=src)
+            elif engine == "g":
+                nc.gpsimd.tensor_scalar(out=dst, in0=src, scalar1=1.0, scalar2=0.0, op0=MULT, op1=ADD)
+            else:
+                nc.scalar.copy(out=dst, in_=src)
 
-        def quantise_piece(part):
-            nc.vector.quantize_mx(out=part["codes"][:].bitcast(FP8X4), scales=part["plane"][:], in_=part["grouped"][:])
+        def quantise(part):
+            nc.vector.quantize_mx(out=part["codes"][:].bitcast(FP8X4), scales=part["plane"][:], in_=part["grouped"])
 
-        def prepare(parts, on_vector):
-            for part, flag in zip(parts, on_vector):
-                round_piece(part, flag)
-            for part in parts:
-                quantise_piece(part)
+        def quantise_half(part, e):
+            nc.vector.quantize_mx(
+                out=part["codes"][:, columns(e)].bitcast(FP8X4), scales=part["plane"][:, columns(e)],
+                in_=part["grouped"][:, PACK * PIECE * e : PACK * PIECE * (e + 1)],
+            )
 
-        last = QUARTERS - 1
-        silu_a = [[w1_piece[q + 1][0]["raw"][:, BANK * g : BANK * (g + 1)] for g in range(2)] for q in range(last)]
-        silu_a.append([w3_piece[0]["raw"][:, BANK * g : BANK * (g + 1)] for g in range(2)])
-        gated = [[shared[:, slot * (q + 1) + BANK * g : slot * (q + 1) + BANK * (g + 1)] for g in range(2)] for q in range(QUARTERS)]
-        h_rows = [[sbuf(f"h_rows{a}{g}", [P, 2, PASS], BF16)[:] for g in range(2)] for a in range(2)]
-        h_rows[0][1] = w3_piece[last]["grouped"][:].rearrange("p (i r) -> p i r", i=2)
-        h_cols = [[w5_piece[g]["raw"][:, 0:BANK].bitcast(BF16) for g in range(2)], [sbuf(f"h_cols1{g}", [P, PAIR * PACK], BF16)[:] for g in range(2)]]
-        h_w = [sbuf(f"h_w{a}", [P, S], U32) for a in range(2)]
-        h_s = [sbuf(f"h_s{a}", [P, S], U8) for a in range(2)]
+        a_bank = [banks[0:4], banks[0:4]]
+        b_bank = [banks[4:8], banks[4:8]]
+        c_bank = [[banks[0], banks[1], banks[2], banks[4]], [banks[5], banks[6], banks[0], banks[1]]]
+        d_bank = [banks[2], banks[4], banks[3], banks[7]]
+        y_bank = [banks[5:7], banks[0:2]]
+
+        def fresh(name):
+            return sbuf(name, [P, BANK], F32)[:]
+
+        def over(part, slot):
+            return part["raw"][:, BANK * slot : BANK * (slot + 1)]
+
+        def over_left(part, slot):
+            return part["raw"].rearrange("p (i c) -> p i c", i=PACK)[:, 2 * slot : 2 * slot + 2, 0:PIECE]
+
+        def over_right(part, slot):
+            return part["raw"].rearrange("p (i c) -> p i c", i=PACK)[:, 2 * slot : 2 * slot + 2, PIECE:PASS]
+
+        silu_a = [
+            [fresh(f"silu0{t}") for t in range(4)],
+            [fresh("silu10"), over_left(w3_q[0], 0), over_left(w3_q[0], 1), over(w3_q[1], 1)],
+        ]
+        gated = [
+            [fresh(f"gated0{t}") for t in range(4)],
+            [over_right(w3_q[0], 0), fresh("gated11"), fresh("gated12"), fresh("gated13")],
+        ]
+        h_first = w3_q[1]["room"][:, 0 : 2 * BANK].bitcast(BF16)
+        h_pair = [
+            [h_first[:, 0 : 2 * PASS], h_first[:, 2 * PASS : 4 * PASS]],
+            [w5_q["room"][:, 0:BANK].bitcast(BF16), over(w5_q, 1).bitcast(BF16)],
+        ]
+        h_cols = [[h_pair[half][t // 2][:, PASS * (t % 2) : PASS * (t % 2 + 1)] for t in range(4)] for half in range(2)]
         d_sb = sbuf("d_sb", [P, N // P, S], F32)
         result = [[sbuf(f"result{g}{m}", [P, 2, PAIR], F32) for m in range(2)] for g in range(2)]
+        h_w = [sbuf(f"h_w{a}", [P, S], U32) for a in range(2)]
+        h_s = [sbuf(f"h_s{a}", [P, S], U8) for a in range(2)]
 
-        def positions(g, i):
-            return slice(PAIR * g + P * i, PAIR * g + P * (i + 1))
+        def cols(t):
+            return slice(P * t, P * (t + 1))
 
-        def gated_product(q, g):
+        def woven(bank):
+            return bank[:].rearrange("p (t u j) -> p u j t", t=PACK, u=2)
+
+        def flat(ap):
+            if len(ap.shape) == 2:
+                return ap.rearrange("p (u j t) -> p u j t", t=PACK, u=2)
+            return ap.rearrange("p u (j t) -> p u j t", t=PACK)
+
+        def gate(half, tile):
+            js = cols(tile)
             for a in range(2):
-                for i in range(2):
-                    js = positions(g, i)
+                for t in range(PACK):
                     nc.tensor.matmul_mx(
-                        out=a_bank[g][:, columns(i)], lhsT=v_w[a][:, js].bitcast(FP8X4), lhsT_scale=v_s[a][:, js],
-                        rhs=w1_piece[q][a]["codes"][:].bitcast(FP8X4), rhs_scale=w1_piece[q][a]["plane"][:],
-                        start=(a == 0 and i == 0), stop=(a == 1 and i == 1),
+                        out=a_bank[half][tile][:, cols(t)], lhsT=w1_q[half][a]["codes"][:, cols(t)].bitcast(FP8X4),
+                        lhsT_scale=w1_q[half][a]["plane"][:, cols(t)],
+                        rhs=v_w[a][:, js].bitcast(FP8X4), rhs_scale=v_s[a][:, js],
+                        start=(a == 0 and t == 0), stop=(a == 1 and t == PACK - 1),
                     )
+
+        def silu(half, tile):
+            nc.scalar.activation(out=flat(silu_a[half][tile]), in_=woven(a_bank[half][tile]), func=SILU)
+
+        def value(half, tile):
+            js = cols(tile)
             for a in range(2):
-                for i in range(2):
-                    js = positions(g, i)
-                    for e in range(PIECE // P):
-                        r0 = PIECE * q + P * e
-                        byte0 = 2 * (r0 % PASS)
-                        nc.tensor.matmul_mx(
-                            out=b_bank[g][:, PIECE * i + P * e : PIECE * i + P * (e + 1)],
-                            lhsT=v_w[a][:, js].bitcast(FP8X4), lhsT_scale=v_s[a][:, js],
-                            rhs=w2_w[r0 // PASS][:, a, byte0 : byte0 + 2 * P].bitcast(FP4X4),
-                            rhs_scale=w2_s[:, H * a + r0 : H * a + r0 + P],
-                            start=(a == 0 and i == 0 and e == 0), stop=(a == 1 and i == 1 and e == 1),
-                        )
-            nc.scalar.activation(out=silu_a[q][g], in_=a_bank[g][:], func=SILU)
-            nc.vector.tensor_tensor(out=gated[q][g], in0=b_bank[g][:], in1=silu_a[q][g], op=MULT)
-
-        def add_sense(a, tile):
-            js = slice(P * tile, P * (tile + 1))
-            for e in range(2):
-                part = w3_piece[2 * a + e]
-                nc.tensor.matmul_mx(
-                    out=c_bank[tile][:, columns(e)], lhsT=v2_w[:, js].bitcast(FP8X4), lhsT_scale=v2_s[:, js],
-                    rhs=part["codes"][:].bitcast(FP8X4), rhs_scale=part["plane"][:], start=True, stop=True,
-                )
-            both = shared[:, slot * (2 * a + 1) : slot * (2 * a + 3)].rearrange("p (e c) -> p e c", e=2)
-            nc.vector.tensor_tensor(
-                out=h_rows[a][tile // 2][:, tile % 2, :].rearrange("p (e c) -> p e c", e=2),
-                in0=c_bank[tile][:].rearrange("p (e c) -> p e c", e=2),
-                in1=both[:, :, columns(tile)], op=ADD,
-            )
-
-        def turn_h(a, g):
-            words = h_rows[a][g][:].rearrange("p i r -> p (i r)").bitcast(F32)
-            for i in range(2):
-                for u in range(2):
-                    nc.tensor.transpose(
-                        turn_bank[a][g][:, PAIR * u + P * i : PAIR * u + P * (i + 1)],
-                        words[:, 2 * P * i + u : 2 * P * (i + 1) : 2], ident[:],
+                for t in range(PACK):
+                    ws = cols(PACK * a + t)
+                    nc.tensor.matmul_mx(
+                        out=b_bank[half][tile][:, cols(t)], lhsT=w2_dealt[half][:, ws].bitcast(FP4X4),
+                        lhsT_scale=w2_s_dealt[half][:, ws],
+                        rhs=v_w[a][:, js].bitcast(FP8X4), rhs_scale=v_s[a][:, js],
+                        start=(a == 0 and t == 0), stop=(a == 1 and t == PACK - 1),
                     )
-            nc.scalar.copy(
-                out=h_cols[a][g].bitcast(F32).rearrange("p (j u) -> p j u", u=2),
-                in_=turn_bank[a][g][:].rearrange("p (u j) -> p j u", u=2),
-            )
 
-        def quantise_h(a, g):
+        def multiply(half, tile):
+            nc.vector.tensor_tensor(out=flat(gated[half][tile]), in0=woven(b_bank[half][tile]), in1=flat(silu_a[half][tile]), op=MULT)
+
+        def sense(half, tile):
+            js = cols(tile)
+            for t in range(PACK):
+                nc.tensor.matmul_mx(
+                    out=c_bank[half][tile][:, cols(t)], lhsT=w3_q[half]["codes"][:, cols(t)].bitcast(FP8X4),
+                    lhsT_scale=w3_q[half]["plane"][:, cols(t)],
+                    rhs=v2_w[:, js].bitcast(FP8X4), rhs_scale=v2_s[:, js], start=True, stop=True,
+                )
+
+        def add(half, tile):
+            nc.vector.tensor_tensor(out=flat(h_cols[half][tile]), in0=woven(c_bank[half][tile]), in1=flat(gated[half][tile]), op=ADD)
+
+        def quantise_h(half, g):
             js = slice(PAIR * g, PAIR * (g + 1))
-            nc.vector.quantize_mx(
-                out=h_w[a][:, js].bitcast(FP8X4), scales=h_s[a][:, js], in_=h_cols[a][g],
-            )
+            nc.vector.quantize_mx(out=h_w[half][:, js].bitcast(FP8X4), scales=h_s[half][:, js], in_=h_pair[half][g])
+
+        def quantise_first_half():
+            nc.vector.quantize_mx(out=h_w[0][:].bitcast(FP8X4), scales=h_s[0][:], in_=h_first)
 
         def mix(a, g):
             js = slice(PAIR * g, PAIR * (g + 1))
@@ -282,15 +270,16 @@ def tile_list_abbreviation_expansion_features_kernel(
                         start=(a == 0 and i == 0), stop=(a == 1 and i == 1),
                     )
 
-        def domain(tile):
-            part = w5_piece[tile // 2]
-            ns = slice(P * (tile % 2), P * (tile % 2 + 1))
+        def domain(tile, engine="s"):
             bank = d_bank[tile]
             nc.tensor.matmul_mx(
-                out=bank[:], lhsT=part["codes"][:, ns].bitcast(FP8X4), lhsT_scale=part["plane"][:, ns],
+                out=bank[:], lhsT=w5_q["codes"][:, cols(tile)].bitcast(FP8X4), lhsT_scale=w5_q["plane"][:, cols(tile)],
                 rhs=v3_w[:].bitcast(FP4X4), rhs_scale=v3_s, start=True, stop=True,
             )
-            nc.scalar.copy(out=d_sb[:, tile, :], in_=bank[:])
+            if engine == "v":
+                nc.vector.tensor_copy(out=d_sb[:, tile, :], in_=bank[:])
+            else:
+                nc.scalar.copy(out=d_sb[:, tile, :], in_=bank[:])
 
         def finish(g, m):
             js = slice(PAIR * g, PAIR * (g + 1))
@@ -300,60 +289,128 @@ def tile_list_abbreviation_expansion_features_kernel(
             )
             nc.sync.dma_start(out=out[2 * P * m : 2 * P * (m + 1), js].rearrange("(i p) j -> p i j", p=P), in_=result[g][m][:])
 
-        gather(v_w[0][:], tab_w[0][:], list1)
-        gather(v_w[1][:], tab_w[1][:], list1)
+        warm = sbuf("warm", [P, 16], F32)
+        for plane in (tab_s, w2_s, tab2_s, tab3_s, planes, w4_s):
+            nc.vector.memset(plane[:].bitcast(I32), 0)
+        nc.vector.memset(warm[:, 0:8], 0.0)
+        nc.scalar.activation(out=warm[:, 8:9], in_=warm[:, 0:1], func=SILU)
 
-        prepare([w1_piece[0][0]], [False])
-        prepare([w1_piece[0][1]], [False])
-        prepare([w1_piece[1][0]], [False])
+        nc.sync.dma_start(list3[:], offs3)
+        nc.sync.dma_start(out=tab3_w[:].bitcast(I32), in_=tab3_words[0].bitcast(I32))
+        nc.sync.dma_start(list1[:], offs)
+        load_rows(tab_s, tab_scales)
+        load_rows(tab2_s, tab2_scales)
+        nc.sync.dma_start(list2[:], offs2)
+        load_rows(tab3_s, tab3_scales)
+        load_block(w1_q[0][0])
+        load_plane(nc.sync, w2_s, w2_scales, 0)
+        load_w2(0)
+        load_e4m3_words(tab_w[0], tab_words[0])
+        load_block(w1_q[0][1])
         gather(v3_w[:], tab3_w[:], list3)
-        round_piece(w1_piece[1][1], True)
-        gated_product(0, 0)
-        quantise_piece(w1_piece[1][1])
-        gated_product(0, 1)
-        prepare([w1_piece[2][0]], [False])
-        round_piece(w1_piece[2][1], True)
-        gated_product(1, 0)
-        quantise_piece(w1_piece[2][1])
-        gated_product(1, 1)
-        prepare([w1_piece[3][0]], [False])
+        gather(picked_s[:, 0:S], tab_s[:, 0:T], list1)
+        gather(picked_s[:, S : 2 * S], tab_s[:, T : 2 * T], list1)
+        gather(picked_s[:, 2 * S : 3 * S], tab2_s[:], list2)
+        gather(picked_s[:, 3 * S : 4 * S], tab3_s[:], list3)
+        place_rows(nc.sync, slice(0, 4 * S))
+        load_e4m3_words(tab_w[1], tab_words[1])
+        load_w2(1)
+        load_block(w1_q[1][0])
+        load_block(w1_q[1][1])
+        load_e4m3_words(tab2_w, tab2_words[0])
+        load_block(w3_q[0])
+        load_block(w3_q[1])
+        load_block(w5_q)
+        load_w4()
+        load_plane(nc.sync, w4_s, w4_scales, W4_ROW0)
+
+        round_piece(w1_q[0][0], 0, 64, "s")
+        round_piece(w1_q[0][0], 64, 128, "s")
+        deal_w2_words(0)
+        deal_w2_scales(0)
+        quantise(w1_q[0][0])
+        gather(v_w[0][:], tab_w[0][:], list1)
+        round_piece(w1_q[0][1], 0, 64, "s")
+        round_piece(w1_q[0][1], 64, 128, "s")
+        quantise(w1_q[0][1])
+        gather(v_w[1][:], tab_w[1][:], list1)
+        deal_w2_words(1)
+        deal_w2_scales(1)
+        gate(0, 0)
+        value(0, 0)
+        gate(0, 1)
+        value(0, 1)
+        gate(0, 2)
+        value(0, 2)
+        gate(0, 3)
+        value(0, 3)
+        silu(0, 0)
+        multiply(0, 0)
+        silu(0, 1)
+        multiply(0, 1)
+        silu(0, 2)
+        multiply(0, 2)
+        silu(0, 3)
+        multiply(0, 3)
+        round_piece(w1_q[1][0], 0, 76, "s")
+        round_piece(w1_q[1][0], 76, 128, "v")
+        quantise(w1_q[1][0])
+        round_piece(w1_q[1][1], 0, 76, "s")
+        round_piece(w1_q[1][1], 76, 128, "v")
+        quantise(w1_q[1][1])
         gather(v2_w[:], tab2_w[:], list2)
-        round_piece(w1_piece[3][1], True)
-        gated_product(2, 0)
-        quantise_piece(w1_piece[3][1])
-        gated_product(2, 1)
-        prepare([w3_piece[0]], [False])
-        round_piece(w3_piece[1], True)
-        gated_product(3, 0)
-        quantise_piece(w3_piece[1])
-        gated_product(3, 1)
-        add_sense(0, 0)
-        add_sense(0, 1)
-        prepare([w3_piece[2]], [False])
-        prepare([w3_piece[3]], [False])
-        add_sense(0, 2)
-        add_sense(0, 3)
-        prepare([w5_piece[0]], [False])
-        turn_h(0, 0)
-        prepare([w5_piece[1]], [False])
-        turn_h(0, 1)
-        quantise_h(0, 0)
-        mix(0, 0)
-        domain(0)
-        quantise_h(0, 1)
-        add_sense(1, 0)
-        add_sense(1, 1)
-        turn_h(1, 0)
-        domain(1)
-        add_sense(1, 2)
-        domain(2)
-        add_sense(1, 3)
-        turn_h(1, 1)
+        gate(1, 0)
+        value(1, 0)
+        gate(1, 1)
+        value(1, 1)
+        gate(1, 2)
+        value(1, 2)
+        gate(1, 3)
+        value(1, 3)
+        silu(1, 0)
+        round_piece(w3_q[0], 0, 64, "s")
+        round_piece(w3_q[0], 64, 128, "v")
+        quantise(w3_q[0])
+        multiply(1, 0)
+        silu(1, 1)
+        silu(1, 2)
+        multiply(1, 1)
+        multiply(1, 2)
+        round_piece(w3_q[1], 64, 128, "s")
+        round_piece(w3_q[1], 0, 64, "s")
+        sense(0, 0)
+        sense(0, 1)
+        sense(0, 2)
+        sense(0, 3)
+        add(0, 0)
+        add(0, 1)
+        add(0, 2)
+        quantise(w3_q[1])
+        add(0, 3)
+        silu(1, 3)
+        multiply(1, 3)
+        quantise_first_half()
+        sense(1, 0)
+        sense(1, 1)
+        sense(1, 2)
+        sense(1, 3)
+        round_piece(w5_q, 0, 64, "s", False)
+        round_piece(w5_q, 64, 128, "s", False)
+        add(1, 0)
+        quantise_half(w5_q, 0)
+        domain(0, "s")
+        domain(1, "s")
+        add(1, 1)
+        quantise_half(w5_q, 1)
+        domain(2, "s")
+        domain(3, "s")
+        add(1, 2)
         quantise_h(1, 0)
+        add(1, 3)
+        mix(0, 0)
         mix(1, 0)
-        domain(3)
-        mix(0, 1)
         quantise_h(1, 1)
+        mix(0, 1)
         mix(1, 1)
         finish(0, 0)
         finish(0, 1)

@@ -185,13 +185,13 @@ def tile_list_abbreviation_expansion_features_kernel(
             [fresh("silu10"), over_left(w3_q[0], 0), over_left(w3_q[0], 1), over(w3_q[1], 1)],
         ]
         gated = [
-            [fresh(f"gated0{t}") for t in range(4)],
+            [fresh("gated00"), fresh("gated01"), over(w1_q[1][1], 0), over(w1_q[1][1], 1)],
             [over_right(w3_q[0], 0), fresh("gated11"), fresh("gated12"), fresh("gated13")],
         ]
         h_first = w3_q[1]["room"][:, 0 : 2 * BANK].bitcast(BF16)
         h_pair = [
             [h_first[:, 0 : 2 * PASS], h_first[:, 2 * PASS : 4 * PASS]],
-            [w5_q["room"][:, 0:BANK].bitcast(BF16), over(w5_q, 1).bitcast(BF16)],
+            [w5_q["room"][:, 0:BANK].bitcast(BF16), w5_q["raw"][:, PIECE : PIECE + BANK].bitcast(BF16)],
         ]
         h_cols = [[h_pair[half][t // 2][:, PASS * (t % 2) : PASS * (t % 2 + 1)] for t in range(4)] for half in range(2)]
         d_sb = sbuf("d_sb", [P, N // P, S], F32)
@@ -210,9 +210,9 @@ def tile_list_abbreviation_expansion_features_kernel(
                 return ap.rearrange("p (u j t) -> p u j t", t=PACK, u=2)
             return ap.rearrange("p u (j t) -> p u j t", t=PACK)
 
-        def gate(half, tile):
+        def gate(half, tile, passes=(0, 1)):
             js = cols(tile)
-            for a in range(2):
+            for a in passes:
                 for t in range(PACK):
                     nc.tensor.matmul_mx(
                         out=a_bank[half][tile][:, cols(t)], lhsT=w1_q[half][a]["codes"][:, cols(t)].bitcast(FP8X4),
@@ -224,9 +224,9 @@ def tile_list_abbreviation_expansion_features_kernel(
         def silu(half, tile):
             nc.scalar.activation(out=flat(silu_a[half][tile]), in_=woven(a_bank[half][tile]), func=SILU)
 
-        def value(half, tile):
+        def value(half, tile, passes=(0, 1)):
             js = cols(tile)
-            for a in range(2):
+            for a in passes:
                 for t in range(PACK):
                     ws = cols(PACK * a + t)
                     nc.tensor.matmul_mx(
@@ -257,6 +257,9 @@ def tile_list_abbreviation_expansion_features_kernel(
 
         def quantise_first_half():
             nc.vector.quantize_mx(out=h_w[0][:].bitcast(FP8X4), scales=h_s[0][:], in_=h_first)
+
+        def quantise_tile(tile):
+            nc.vector.quantize_mx(out=h_w[1][:, cols(tile)].bitcast(FP8X4), scales=h_s[1][:, cols(tile)], in_=h_cols[1][tile])
 
         def mix(a, g):
             js = slice(PAIR * g, PAIR * (g + 1))
@@ -289,30 +292,39 @@ def tile_list_abbreviation_expansion_features_kernel(
             )
             nc.sync.dma_start(out=out[2 * P * m : 2 * P * (m + 1), js].rearrange("(i p) j -> p i j", p=P), in_=result[g][m][:])
 
+        def finish_tile(g, tile):
+            m, i = divmod(tile, 2)
+            js = slice(PAIR * g, PAIR * (g + 1))
+            nc.vector.tensor_tensor(
+                out=result[g][m][:, i, :], in0=y_bank[g][m][:, PAIR * i : PAIR * (i + 1)], in1=d_sb[:, tile, js], op=MULT,
+            )
+            nc.sync.dma_start(out=out[cols(tile), js], in_=result[g][m][:, i, :])
+
         warm = sbuf("warm", [P, 16], F32)
         for plane in (tab_s, w2_s, tab2_s, tab3_s, planes, w4_s):
             nc.vector.memset(plane[:].bitcast(I32), 0)
         nc.vector.memset(warm[:, 0:8], 0.0)
         nc.scalar.activation(out=warm[:, 8:9], in_=warm[:, 0:1], func=SILU)
+        load_plane(nc.gpsimd, w2_s, w2_scales, 0)
 
         nc.sync.dma_start(list3[:], offs3)
         nc.sync.dma_start(out=tab3_w[:].bitcast(I32), in_=tab3_words[0].bitcast(I32))
-        nc.sync.dma_start(list1[:], offs)
+        load_w2(0)
         load_rows(tab_s, tab_scales)
+        nc.sync.dma_start(list1[:], offs)
         load_rows(tab2_s, tab2_scales)
         nc.sync.dma_start(list2[:], offs2)
         load_rows(tab3_s, tab3_scales)
         load_block(w1_q[0][0])
-        load_plane(nc.sync, w2_s, w2_scales, 0)
-        load_w2(0)
         load_e4m3_words(tab_w[0], tab_words[0])
-        load_block(w1_q[0][1])
-        gather(v3_w[:], tab3_w[:], list3)
         gather(picked_s[:, 0:S], tab_s[:, 0:T], list1)
         gather(picked_s[:, S : 2 * S], tab_s[:, T : 2 * T], list1)
+        place_rows(nc.sync, slice(0, 2 * S))
+        load_block(w1_q[0][1])
+        gather(v3_w[:], tab3_w[:], list3)
         gather(picked_s[:, 2 * S : 3 * S], tab2_s[:], list2)
         gather(picked_s[:, 3 * S : 4 * S], tab3_s[:], list3)
-        place_rows(nc.sync, slice(0, 4 * S))
+        place_rows(nc.gpsimd, slice(2 * S, 4 * S))
         load_e4m3_words(tab_w[1], tab_words[1])
         load_w2(1)
         load_block(w1_q[1][0])
@@ -327,45 +339,53 @@ def tile_list_abbreviation_expansion_features_kernel(
         round_piece(w1_q[0][0], 0, 64, "s")
         round_piece(w1_q[0][0], 64, 128, "s")
         deal_w2_words(0)
-        deal_w2_scales(0)
         quantise(w1_q[0][0])
         gather(v_w[0][:], tab_w[0][:], list1)
+        deal_w2_scales(0)
         round_piece(w1_q[0][1], 0, 64, "s")
-        round_piece(w1_q[0][1], 64, 128, "s")
+        round_piece(w1_q[0][1], 64, 128, "v")
         quantise(w1_q[0][1])
         gather(v_w[1][:], tab_w[1][:], list1)
         deal_w2_words(1)
         deal_w2_scales(1)
-        gate(0, 0)
-        value(0, 0)
-        gate(0, 1)
-        value(0, 1)
-        gate(0, 2)
-        value(0, 2)
-        gate(0, 3)
-        value(0, 3)
+        gate(0, 0, (0,))
+        gate(0, 1, (0,))
+        gate(0, 2, (0,))
+        gate(0, 3, (0,))
+        gate(0, 0, (1,))
+        gate(0, 1, (1,))
+        gate(0, 2, (1,))
+        gate(0, 3, (1,))
+        value(0, 0, (0,))
+        value(0, 0, (1,))
+        value(0, 1, (0,))
+        value(0, 1, (1,))
+        value(0, 2, (0,))
+        value(0, 2, (1,))
+        value(0, 3, (0,))
+        value(0, 3, (1,))
         silu(0, 0)
-        multiply(0, 0)
         silu(0, 1)
-        multiply(0, 1)
         silu(0, 2)
-        multiply(0, 2)
         silu(0, 3)
-        multiply(0, 3)
-        round_piece(w1_q[1][0], 0, 76, "s")
-        round_piece(w1_q[1][0], 76, 128, "v")
+        multiply(0, 0)
+        multiply(0, 1)
+        round_piece(w1_q[1][0], 0, 56, "s")
+        round_piece(w1_q[1][0], 56, 128, "v")
         quantise(w1_q[1][0])
         round_piece(w1_q[1][1], 0, 76, "s")
         round_piece(w1_q[1][1], 76, 128, "v")
         quantise(w1_q[1][1])
+        multiply(0, 2)
+        multiply(0, 3)
         gather(v2_w[:], tab2_w[:], list2)
         gate(1, 0)
-        value(1, 0)
         gate(1, 1)
-        value(1, 1)
         gate(1, 2)
-        value(1, 2)
         gate(1, 3)
+        value(1, 0)
+        value(1, 1)
+        value(1, 2)
         value(1, 3)
         silu(1, 0)
         round_piece(w3_q[0], 0, 64, "s")
@@ -404,15 +424,17 @@ def tile_list_abbreviation_expansion_features_kernel(
         quantise_half(w5_q, 1)
         domain(2, "s")
         domain(3, "s")
-        add(1, 2)
         quantise_h(1, 0)
+        add(1, 2)
         add(1, 3)
         mix(0, 0)
         mix(1, 0)
-        quantise_h(1, 1)
+        quantise_tile(2)
+        quantise_tile(3)
         mix(0, 1)
         mix(1, 1)
         finish(0, 0)
         finish(0, 1)
         finish(1, 0)
-        finish(1, 1)
+        finish_tile(1, 2)
+        finish_tile(1, 3)

@@ -109,11 +109,11 @@ def tile_list_abbreviation_expansion_features_kernel(
         v_w = [sbuf(f"v_w{a}", [P, S], U32) for a in range(2)]
         v2_w = sbuf("v2_w", [P, S], U32)
         v3_w = sbuf("v3_w", [P, S], U16)
-        picked_s = sbuf("picked_s", [P, 4 * S], U8)
-        planes = sbuf("planes", [P, 4 * S], U8)
-        v_s = [planes[:, 0:S], planes[:, S : 2 * S]]
-        v2_s = planes[:, 2 * S : 3 * S]
-        v3_s = planes[:, 3 * S : 4 * S]
+        picked_s = [sbuf(f"picked_s{k}", [P, 2 * S], U8) for k in range(2)]
+        planes = [sbuf(f"planes{k}", [P, 2 * S], U8) for k in range(2)]
+        v_s = [planes[0][:, 0:S], planes[0][:, S : 2 * S]]
+        v2_s = planes[1][:, 0:S]
+        v3_s = planes[1][:, S : 2 * S]
 
         def load_rows(tile, scales):
             nc.sync.dma_start(
@@ -121,9 +121,9 @@ def tile_list_abbreviation_expansion_features_kernel(
                 in_=scales.bitcast(I32).rearrange("a s t -> s a t"),
             )
 
-        def place_rows(queue, cols):
+        def place_rows(queue, k):
             for r in range(4):
-                queue.dma_start(out=planes[r:P:32, cols].bitcast(I32), in_=picked_s[8 * r : P : 32, cols].bitcast(I32))
+                queue.dma_start(out=planes[k][r:P:32, :].bitcast(I32), in_=picked_s[k][8 * r : P : 32, :].bitcast(I32))
 
         def gather(picked, window, entries):
             nc.vector.tensor_copy(picked, window.indirect(entries[:]))
@@ -301,11 +301,10 @@ def tile_list_abbreviation_expansion_features_kernel(
             nc.sync.dma_start(out=out[cols(tile), js], in_=result[g][m][:, i, :])
 
         warm = sbuf("warm", [P, 16], F32)
-        for plane in (tab_s, w2_s, tab2_s, tab3_s, planes, w4_s):
+        for plane in (tab_s, w2_s, tab2_s, tab3_s, planes[0], planes[1], w4_s):
             nc.vector.memset(plane[:].bitcast(I32), 0)
         nc.vector.memset(warm[:, 0:8], 0.0)
         nc.scalar.activation(out=warm[:, 8:9], in_=warm[:, 0:1], func=SILU)
-        load_plane(nc.gpsimd, w2_s, w2_scales, 0)
 
         nc.sync.dma_start(list3[:], offs3)
         nc.sync.dma_start(out=tab3_w[:].bitcast(I32), in_=tab3_words[0].bitcast(I32))
@@ -317,20 +316,21 @@ def tile_list_abbreviation_expansion_features_kernel(
         load_rows(tab3_s, tab3_scales)
         load_block(w1_q[0][0])
         load_e4m3_words(tab_w[0], tab_words[0])
-        gather(picked_s[:, 0:S], tab_s[:, 0:T], list1)
-        gather(picked_s[:, S : 2 * S], tab_s[:, T : 2 * T], list1)
-        place_rows(nc.sync, slice(0, 2 * S))
         load_block(w1_q[0][1])
         gather(v3_w[:], tab3_w[:], list3)
-        gather(picked_s[:, 2 * S : 3 * S], tab2_s[:], list2)
-        gather(picked_s[:, 3 * S : 4 * S], tab3_s[:], list3)
-        place_rows(nc.gpsimd, slice(2 * S, 4 * S))
+        gather(picked_s[0][:, 0:S], tab_s[:, 0:T], list1)
+        gather(picked_s[0][:, S : 2 * S], tab_s[:, T : 2 * T], list1)
+        place_rows(nc.sync, 0)
+        gather(picked_s[1][:, 0:S], tab2_s[:], list2)
+        gather(picked_s[1][:, S : 2 * S], tab3_s[:], list3)
         load_e4m3_words(tab_w[1], tab_words[1])
+        load_plane(nc.sync, w2_s, w2_scales, 0)
         load_w2(1)
         load_block(w1_q[1][0])
         load_block(w1_q[1][1])
         load_e4m3_words(tab2_w, tab2_words[0])
         load_block(w3_q[0])
+        place_rows(nc.sync, 1)
         load_block(w3_q[1])
         load_block(w5_q)
         load_w4()
@@ -341,11 +341,11 @@ def tile_list_abbreviation_expansion_features_kernel(
         deal_w2_words(0)
         quantise(w1_q[0][0])
         gather(v_w[0][:], tab_w[0][:], list1)
-        deal_w2_scales(0)
         round_piece(w1_q[0][1], 0, 64, "s")
         round_piece(w1_q[0][1], 64, 128, "v")
         quantise(w1_q[0][1])
         gather(v_w[1][:], tab_w[1][:], list1)
+        deal_w2_scales(0)
         deal_w2_words(1)
         deal_w2_scales(1)
         gate(0, 0, (0,))

@@ -50,14 +50,14 @@ def tile_list_abbreviation_expansion_features_kernel(
         tab_w = [sbuf(f"tab_w{a}", [P, T], U32) for a in range(2)]
         tab2_w = sbuf("tab2_w", [P, T2], U32)
         tab3_w = sbuf("tab3_w", [P, T3], U16)
-        tab_s = sbuf("tab_s", [P, 2 * T], U8)
+        tab_s = sbuf("tab_s", [P, T], U8)
         tab2_s = sbuf("tab2_s", [P, T2], U8)
         tab3_s = sbuf("tab3_s", [P, T3], U8)
         w2_s = sbuf("w2_s", [P, 2 * H], U8)
         w4_s = sbuf("w4_s", [P, 2 * N], U8)
         w2_w = [sbuf(f"w2_w{half}", [P, 2 * PASS], U16) for half in range(2)]
         w2_dealt = [sbuf(f"w2_dealt{half}", [P, 2 * PASS], U16) for half in range(2)]
-        w2_s_dealt = [w2_w[half][:].bitcast(U8)[:, 0 : 2 * PASS] for half in range(2)]
+        w2_s_dealt = [w2_w[0][:].bitcast(U8)[:, 2 * PASS * half : 2 * PASS * (half + 1)] for half in range(2)]
         w4_w = sbuf("w4_w", [P, 2, N], U32)
 
         def operand(name, rows, lead=0):
@@ -109,7 +109,7 @@ def tile_list_abbreviation_expansion_features_kernel(
         v_w = [sbuf(f"v_w{a}", [P, S], U32) for a in range(2)]
         v2_w = sbuf("v2_w", [P, S], U32)
         v3_w = sbuf("v3_w", [P, S], U16)
-        picked_s = [sbuf(f"picked_s{k}", [P, 2 * S], U8) for k in range(2)]
+        picked_s = [sbuf("picked_s0", [P, S], U8), sbuf("picked_s1", [P, 2 * S], U8)]
         planes = [sbuf(f"planes{k}", [P, 2 * S], U8) for k in range(2)]
         v_s = [planes[0][:, 0:S], planes[0][:, S : 2 * S]]
         v2_s = planes[1][:, 0:S]
@@ -120,6 +120,16 @@ def tile_list_abbreviation_expansion_features_kernel(
                 out=tile[0:P:8, :].bitcast(I32).rearrange("s (a t) -> s a t", a=scales.shape[0]),
                 in_=scales.bitcast(I32).rearrange("a s t -> s a t"),
             )
+
+        def load_both_passes():
+            nc.sync.dma_start(out=tab_s[0 : 2 * ROWS, :].bitcast(I32), in_=tab_scales.rearrange("a s t -> (a s) t").bitcast(I32))
+
+        def place_pass(a):
+            for r in range(4):
+                nc.sync.dma_start(
+                    out=planes[0][r:P:32, S * a : S * (a + 1)].bitcast(I32),
+                    in_=picked_s[0][ROWS * a + r : ROWS * (a + 1) : 4, :].bitcast(I32),
+                )
 
         def place_rows(queue, k):
             for r in range(4):
@@ -301,26 +311,28 @@ def tile_list_abbreviation_expansion_features_kernel(
             nc.sync.dma_start(out=out[cols(tile), js], in_=result[g][m][:, i, :])
 
         warm = sbuf("warm", [P, 16], F32)
-        for plane in (tab_s, w2_s, tab2_s, tab3_s, planes[0], planes[1], w4_s):
+        nc.vector.memset(tab_s[32:64, :].bitcast(I32), 0)
+        nc.vector.memset(tab_s[64:P, :].bitcast(I32), 0)
+        for plane in (tab2_s, tab3_s, planes[0], planes[1], w4_s, w2_s):
             nc.vector.memset(plane[:].bitcast(I32), 0)
         nc.vector.memset(warm[:, 0:8], 0.0)
         nc.scalar.activation(out=warm[:, 8:9], in_=warm[:, 0:1], func=SILU)
 
+        nc.sync.dma_start(list1[:], offs)
+        load_both_passes()
         nc.sync.dma_start(list3[:], offs3)
         nc.sync.dma_start(out=tab3_w[:].bitcast(I32), in_=tab3_words[0].bitcast(I32))
         load_w2(0)
-        load_rows(tab_s, tab_scales)
-        nc.sync.dma_start(list1[:], offs)
         load_rows(tab2_s, tab2_scales)
         nc.sync.dma_start(list2[:], offs2)
         load_rows(tab3_s, tab3_scales)
         load_block(w1_q[0][0])
+        gather(picked_s[0][:], tab_s[:], list1)
         load_e4m3_words(tab_w[0], tab_words[0])
+        place_pass(0)
         load_block(w1_q[0][1])
+        place_pass(1)
         gather(v3_w[:], tab3_w[:], list3)
-        gather(picked_s[0][:, 0:S], tab_s[:, 0:T], list1)
-        gather(picked_s[0][:, S : 2 * S], tab_s[:, T : 2 * T], list1)
-        place_rows(nc.sync, 0)
         gather(picked_s[1][:, 0:S], tab2_s[:], list2)
         gather(picked_s[1][:, S : 2 * S], tab3_s[:], list3)
         load_e4m3_words(tab_w[1], tab_words[1])
@@ -333,8 +345,8 @@ def tile_list_abbreviation_expansion_features_kernel(
         place_rows(nc.sync, 1)
         load_block(w3_q[1])
         load_block(w5_q)
-        load_w4()
         load_plane(nc.sync, w4_s, w4_scales, W4_ROW0)
+        load_w4()
 
         round_piece(w1_q[0][0], 0, 64, "s")
         round_piece(w1_q[0][0], 64, 128, "s")
@@ -346,8 +358,8 @@ def tile_list_abbreviation_expansion_features_kernel(
         quantise(w1_q[0][1])
         gather(v_w[1][:], tab_w[1][:], list1)
         deal_w2_scales(0)
-        deal_w2_words(1)
         deal_w2_scales(1)
+        deal_w2_words(1)
         gate(0, 0, (0,))
         gate(0, 1, (0,))
         gate(0, 2, (0,))

@@ -310,13 +310,10 @@ def tile_list_abbreviation_expansion_features_kernel(
             )
             nc.sync.dma_start(out=out[cols(tile), js], in_=result[g][m][:, i, :])
 
-        warm = sbuf("warm", [P, 16], F32)
         nc.vector.memset(tab_s[32:64, :].bitcast(I32), 0)
         nc.vector.memset(tab_s[64:P, :].bitcast(I32), 0)
         for plane in (tab2_s, tab3_s, planes[0], planes[1], w4_s, w2_s):
             nc.vector.memset(plane[:].bitcast(I32), 0)
-        nc.vector.memset(warm[:, 0:8], 0.0)
-        nc.scalar.activation(out=warm[:, 8:9], in_=warm[:, 0:1], func=SILU)
 
         nc.sync.dma_start(list1[:], offs)
         load_both_passes()

@@ -1,7 +1,6 @@
 from contextlib import ExitStack
 
 import concourse.mybir as mybir
-from concourse.masks import make_identity
 
 K, M, H, N, T, T2, T3, S = 1024, 512, 1024, 512, 2048, 2048, 1024, 512
 FLOPS = 2 * S * (2 * K * H + M * H + H * N + M * N)
@@ -22,8 +21,6 @@ P = 128
 PACK = 4
 PASS = P * PACK
 BANK = 512
-PIECE = 256
-QUARTERS = H // PIECE
 PAIR = 2 * P
 ROWS = 16
 W4_ROW0 = 4
@@ -38,14 +35,15 @@ def tile_list_abbreviation_expansion_features_kernel(
         keep = ctx.enter_context(tc.tile_pool(name="keep", bufs=1))
         psum = ctx.enter_context(tc.psum_pool(name="psum", bufs=1))
 
-        def sbuf(name, shape, dtype):
-            return keep.tile(shape, dtype, name=name, align_bytes=64)
+        def sbuf(name, shape, dtype, tag=None):
+            return keep.tile(shape, dtype, name=name, tag=tag or name, align_bytes=64)
 
         list1 = keep.tile([P, S // 16], U16, name="list1")
         list2 = keep.tile([P, S // 16], U16, name="list2")
         list3 = keep.tile([P, S // 16], U16, name="list3")
 
         banks = [psum.tile([P, BANK], F32, name=f"bank{i}") for i in range(8)]
+        low, high = banks[0:4], banks[4:8]
 
         tab_w = [sbuf(f"tab_w{a}", [P, T], U32) for a in range(2)]
         tab2_w = sbuf("tab2_w", [P, T2], U32)
@@ -53,397 +51,330 @@ def tile_list_abbreviation_expansion_features_kernel(
         tab_s = sbuf("tab_s", [P, T], U8)
         tab2_s = sbuf("tab2_s", [P, T2], U8)
         tab3_s = sbuf("tab3_s", [P, T3], U8)
+        w2_w = sbuf("w2_w", [P, 2 * H], U16)
         w2_s = sbuf("w2_s", [P, 2 * H], U8)
+        w2_dealt = sbuf("w2_dealt", [P, 2 * H], U16)
+        w2_s_dealt = sbuf("w2_s_dealt", [P, 2 * H], U8)
+        w4_w = [sbuf(f"w4_w{a}", [P, N], U32) for a in range(2)]
         w4_s = sbuf("w4_s", [P, 2 * N], U8)
-        w2_w = [sbuf(f"w2_w{half}", [P, 2 * PASS], U16) for half in range(2)]
-        w2_dealt = [sbuf(f"w2_dealt{half}", [P, 2 * PASS], U16) for half in range(2)]
-        w2_s_dealt = [w2_w[0][:].bitcast(U8)[:, 2 * PASS * half : 2 * PASS * (half + 1)] for half in range(2)]
-        w4_w = sbuf("w4_w", [P, 2, N], U32)
 
-        def operand(name, rows, lead=0):
-            room = sbuf("raw_" + name, [P, lead + PACK * PASS], F32)
+        def operand(name, rows, lead=0, halved=False):
+            room = sbuf("grouped_" + name, [P, lead + PACK * PASS], BF16)
             return {
                 "rows": rows,
+                "raw": [sbuf(f"raw_{name}{e}", [P, PACK, PAIR], F32) for e in range(2)] if halved else sbuf("raw_" + name, [P, PACK * PASS], F32),
                 "room": room,
-                "raw": room[:, lead : lead + PACK * PASS],
-                "grouped": sbuf("grouped_" + name, [P, PASS * PACK], BF16)[:],
+                "grouped": room[:, lead : lead + PACK * PASS],
                 "codes": sbuf("codes_" + name, [P, PASS], U32),
                 "plane": sbuf("plane_" + name, [P, PASS], U8),
             }
 
-        def columns(i):
-            return slice(PIECE * i, PIECE * (i + 1))
-
         w1_q = [[operand(f"w1_{half}{a}", w1[PASS * a : PASS * (a + 1), PASS * half : PASS * (half + 1)]) for a in range(2)] for half in range(2)]
-        w3_q = [operand("w3_0", w3[:, 0:PASS]), operand("w3_1", w3[:, PASS:H], 3 * PIECE)]
-        w5_q = operand("w5", w5, PIECE)
+        w3_q = [operand("w3_0", w3[:, 0:PASS]), operand("w3_1", w3[:, PASS:H], 3 * PASS, True)]
+        w5_q = operand("w5", w5, PASS, True)
 
-        def load_plane(queue, plane, scales, row0):
+        v_w = [sbuf(f"v_w{a}", [P, S], U32) for a in range(2)]
+        v2_w = sbuf("v2_w", [P, S], U32)
+        v3_w = sbuf("v3_w", [P, S], U16)
+        picked1 = sbuf("picked1", [P, S], U8)
+        picked23 = sbuf("picked23", [P, 2 * S], U8)
+        v_s = [sbuf(f"v_s{a}", [P, S], U8) for a in range(2)]
+        planes23 = sbuf("planes23", [P, 2 * S], U8)
+        v2_s = planes23[:, 0:S]
+        v3_s = planes23[:, S : 2 * S]
+
+        silu_tiles = [sbuf(f"silu{k}", [P, BANK], F32)[:] for k in range(4)]
+        silu_a = [silu_tiles, [w3_q[0]["raw"][:, BANK * k : BANK * (k + 1)] for k in range(4)]]
+        gated = [[sbuf(f"gated0{g}", [P, 2, BANK], F32)[:] for g in range(2)], [sbuf("gated10", [P, 2, BANK], F32)[:]]]
+        b_aside = [w1_q[1][1]["raw"][:].rearrange("p (i c) -> p i c", i=PACK)[:, 2 * g : 2 * g + 2, 0:PAIR] for g in range(2)]
+        h_first = w3_q[1]["room"][:, 0 : PACK * S]
+        h_second = w5_q["room"][:, 0 : PACK * S]
+        h_cols = [[h[:, PASS * j : PASS * (j + 1)] for j in range(4)] for h in (h_first, h_second)]
+        h_w = [sbuf(f"h_w{a}", [P, S], U32) for a in range(2)]
+        h_s = [sbuf(f"h_s{a}", [P, S], U8) for a in range(2)]
+        d_sb = [[sbuf(f"d{g}{m}", [P, BANK], F32) for m in range(2)] for g in range(2)]
+        result = [[sbuf(f"result{g}{m}", [P, BANK], F32) for m in range(2)] for g in range(2)]
+
+        def cols(t):
+            return slice(P * t, P * (t + 1))
+
+        def pair(g):
+            return slice(PAIR * g, PAIR * (g + 1))
+
+        def load_plane(plane, scales, row0):
             for r in range(4):
-                queue.dma_start(
+                nc.sync.dma_start(
                     out=plane[row0 + r : P : 32, :].bitcast(I32).rearrange("q (a t) -> q a t", a=scales.shape[0]),
                     in_=scales[:, r:ROWS:4, :].bitcast(I32).rearrange("a q t -> q a t"),
                 )
 
         def load_block(part):
             nc.sync.dma_start(
-                out=part["raw"].rearrange("p (i c) -> p i c", i=PACK),
+                out=part["raw"][:].rearrange("p (i c) -> p i c", i=PACK),
                 in_=part["rows"].rearrange("(p i) c -> p i c", i=PACK),
             )
+
+        def load_halves(part):
+            for e in range(2):
+                nc.sync.dma_start(out=part["raw"][e][:], in_=part["rows"][:, pair(e)].rearrange("(p i) c -> p i c", i=PACK))
 
         def load_e4m3_words(tile, words):
             nc.sync.dma_start(out=tile[:].bitcast(I32), in_=words.rearrange("p t i -> p (t i)").bitcast(I32))
 
-        def load_w2(half):
-            nc.sync.dma_start(
-                out=w2_w[half][:].bitcast(I32).rearrange("p (a b) -> p a b", a=2),
-                in_=w2_words[:, :, H * half : H * (half + 1)].bitcast(I32).rearrange("a p b -> p a b"),
-            )
-
-        def load_w4():
-            nc.sync.dma_start(
-                out=w4_w[:].bitcast(I32),
-                in_=w4_words.rearrange("a p e i -> a p (e i)").bitcast(I32).rearrange("a p e -> p a e"),
-            )
-
-        v_w = [sbuf(f"v_w{a}", [P, S], U32) for a in range(2)]
-        v2_w = sbuf("v2_w", [P, S], U32)
-        v3_w = sbuf("v3_w", [P, S], U16)
-        picked_s = [sbuf("picked_s0", [P, S], U8), sbuf("picked_s1", [P, 2 * S], U8)]
-        planes = [sbuf(f"planes{k}", [P, 2 * S], U8) for k in range(2)]
-        v_s = [planes[0][:, 0:S], planes[0][:, S : 2 * S]]
-        v2_s = planes[1][:, 0:S]
-        v3_s = planes[1][:, S : 2 * S]
-
         def load_rows(tile, scales):
-            nc.sync.dma_start(
-                out=tile[0:P:8, :].bitcast(I32).rearrange("s (a t) -> s a t", a=scales.shape[0]),
-                in_=scales.bitcast(I32).rearrange("a s t -> s a t"),
-            )
-
-        def load_both_passes():
-            nc.sync.dma_start(out=tab_s[0 : 2 * ROWS, :].bitcast(I32), in_=tab_scales.rearrange("a s t -> (a s) t").bitcast(I32))
+            nc.sync.dma_start(out=tile[0:P:8, :].bitcast(I32), in_=scales[0].bitcast(I32))
 
         def place_pass(a):
             for r in range(4):
-                nc.sync.dma_start(
-                    out=planes[0][r:P:32, S * a : S * (a + 1)].bitcast(I32),
-                    in_=picked_s[0][ROWS * a + r : ROWS * (a + 1) : 4, :].bitcast(I32),
-                )
+                nc.sync.dma_start(out=v_s[a][r:P:32, :].bitcast(I32), in_=picked1[ROWS * a + r : ROWS * (a + 1) : 4, :].bitcast(I32))
 
-        def place_rows(queue, k):
+        def place_rows23():
             for r in range(4):
-                queue.dma_start(out=planes[k][r:P:32, :].bitcast(I32), in_=picked_s[k][8 * r : P : 32, :].bitcast(I32))
+                nc.sync.dma_start(out=planes23[r:P:32, :].bitcast(I32), in_=picked23[8 * r : P : 32, :].bitcast(I32))
 
-        def gather(picked, window, entries):
-            nc.vector.tensor_copy(picked, window.indirect(entries[:]))
+        def gather(picked, window, entries, j0=0, j1=S):
+            nc.vector.tensor_copy(picked[:, j0:j1], window[:].indirect(entries[:, j0 // 16 : j1 // 16]))
 
-        def deal_w2_words(half):
+        def deal(dealt, natural):
             nc.vector.tensor_copy(
-                out=w2_dealt[half][:].rearrange("p (a t m) -> p a t m", a=2, t=PACK),
-                in_=w2_w[half][:].rearrange("p (a m t) -> p a t m", a=2, t=PACK),
-            )
-
-        def deal_w2_scales(half):
-            nc.vector.tensor_copy(
-                out=w2_s_dealt[half].rearrange("p (a t m) -> p a t m", a=2, t=PACK),
-                in_=w2_s[:].rearrange("p (a r) -> p a r", a=2)[:, :, PASS * half : PASS * (half + 1)].rearrange("p a (m t) -> p a t m", t=PACK),
+                out=dealt[:].rearrange("p (h a t m) -> p h a t m", h=2, a=2, t=PACK),
+                in_=natural[:].rearrange("p (a h m t) -> p h a t m", a=2, h=2, t=PACK),
             )
 
         def round_piece(part, m0, m1, engine, dealt=True):
-            if dealt:
-                dst = part["grouped"].rearrange("p (t m i) -> p m i t", t=PACK, i=PACK)[:, m0:m1, :, :]
-            else:
-                dst = part["grouped"].rearrange("p (m t i) -> p m i t", t=PACK, i=PACK)[:, m0:m1, :, :]
-            src = part["raw"].rearrange("p (i m t) -> p m i t", i=PACK, t=PACK)[:, m0:m1, :, :]
+            order = "p (t m i) -> p m i t" if dealt else "p (m t i) -> p m i t"
+            dst = part["grouped"].rearrange(order, t=PACK, i=PACK)[:, m0:m1, :, :]
+            src = part["raw"][:].rearrange("p (i m t) -> p m i t", i=PACK, t=PACK)[:, m0:m1, :, :]
             if engine == "v":
                 nc.vector.tensor_copy(out=dst, in_=src)
             elif engine == "g":
-                nc.gpsimd.tensor_scalar(out=dst, in0=src, scalar1=1.0, scalar2=0.0, op0=MULT, op1=ADD)
+                walk = "p m i t -> p t m i" if dealt else "p m i t -> p m t i"
+                nc.gpsimd.tensor_scalar(out=dst.rearrange(walk), in0=src.rearrange(walk), scalar1=1.0, scalar2=0.0, op0=MULT, op1=ADD)
             else:
                 nc.scalar.copy(out=dst, in_=src)
+
+        def round_block(part, share, other="g", dealt=True):
+            round_piece(part, 0, share, "s", dealt)
+            round_piece(part, share, P, other, dealt)
+
+        def round_halves(part, dealt):
+            order = "p (t m i) -> p m i t" if dealt else "p (m t i) -> p m i t"
+            for e in range(2):
+                nc.scalar.copy(
+                    out=part["grouped"].rearrange(order, t=PACK, i=PACK)[:, 64 * e : 64 * (e + 1), :, :],
+                    in_=part["raw"][e][:].rearrange("p i (m t) -> p m i t", t=PACK),
+                )
 
         def quantise(part):
             nc.vector.quantize_mx(out=part["codes"][:].bitcast(FP8X4), scales=part["plane"][:], in_=part["grouped"])
 
-        def quantise_half(part, e):
-            nc.vector.quantize_mx(
-                out=part["codes"][:, columns(e)].bitcast(FP8X4), scales=part["plane"][:, columns(e)],
-                in_=part["grouped"][:, PACK * PIECE * e : PACK * PIECE * (e + 1)],
-            )
+        a_bank, b_bank = low, high
+        c_bank = [low, high]
+        y_bank = [low[0:2], low[2:4]]
+        d_bank = [high[0:2], high[2:4]]
 
-        a_bank = [banks[0:4], banks[0:4]]
-        b_bank = [banks[4:8], banks[4:8]]
-        c_bank = [[banks[0], banks[1], banks[2], banks[4]], [banks[5], banks[6], banks[0], banks[1]]]
-        d_bank = [banks[2], banks[4], banks[3], banks[7]]
-        y_bank = [banks[5:7], banks[0:2]]
+        def woven(bank, ways):
+            return bank[:].rearrange("p (t j) -> p j t", t=ways)
 
-        def fresh(name):
-            return sbuf(name, [P, BANK], F32)[:]
+        def flat(ap, ways):
+            return ap.rearrange("p (j t) -> p j t", t=ways)
 
-        def over(part, slot):
-            return part["raw"][:, BANK * slot : BANK * (slot + 1)]
-
-        def over_left(part, slot):
-            return part["raw"].rearrange("p (i c) -> p i c", i=PACK)[:, 2 * slot : 2 * slot + 2, 0:PIECE]
-
-        def over_right(part, slot):
-            return part["raw"].rearrange("p (i c) -> p i c", i=PACK)[:, 2 * slot : 2 * slot + 2, PIECE:PASS]
-
-        silu_a = [
-            [fresh(f"silu0{t}") for t in range(4)],
-            [fresh("silu10"), over_left(w3_q[0], 0), over_left(w3_q[0], 1), over(w3_q[1], 1)],
-        ]
-        gated = [
-            [fresh("gated00"), fresh("gated01"), over(w1_q[1][1], 0), over(w1_q[1][1], 1)],
-            [over_right(w3_q[0], 0), fresh("gated11"), fresh("gated12"), fresh("gated13")],
-        ]
-        h_first = w3_q[1]["room"][:, 0 : 2 * BANK].bitcast(BF16)
-        h_pair = [
-            [h_first[:, 0 : 2 * PASS], h_first[:, 2 * PASS : 4 * PASS]],
-            [w5_q["room"][:, 0:BANK].bitcast(BF16), w5_q["raw"][:, PIECE : PIECE + BANK].bitcast(BF16)],
-        ]
-        h_cols = [[h_pair[half][t // 2][:, PASS * (t % 2) : PASS * (t % 2 + 1)] for t in range(4)] for half in range(2)]
-        d_sb = sbuf("d_sb", [P, N // P, S], F32)
-        result = [[sbuf(f"result{g}{m}", [P, 2, PAIR], F32) for m in range(2)] for g in range(2)]
-        h_w = [sbuf(f"h_w{a}", [P, S], U32) for a in range(2)]
-        h_s = [sbuf(f"h_s{a}", [P, S], U8) for a in range(2)]
-
-        def cols(t):
-            return slice(P * t, P * (t + 1))
-
-        def woven(bank):
-            return bank[:].rearrange("p (t u j) -> p u j t", t=PACK, u=2)
-
-        def flat(ap):
-            if len(ap.shape) == 2:
-                return ap.rearrange("p (u j t) -> p u j t", t=PACK, u=2)
-            return ap.rearrange("p u (j t) -> p u j t", t=PACK)
-
-        def gate(half, tile, passes=(0, 1)):
-            js = cols(tile)
-            for a in passes:
-                for t in range(PACK):
-                    nc.tensor.matmul_mx(
-                        out=a_bank[half][tile][:, cols(t)], lhsT=w1_q[half][a]["codes"][:, cols(t)].bitcast(FP8X4),
-                        lhsT_scale=w1_q[half][a]["plane"][:, cols(t)],
-                        rhs=v_w[a][:, js].bitcast(FP8X4), rhs_scale=v_s[a][:, js],
-                        start=(a == 0 and t == 0), stop=(a == 1 and t == PACK - 1),
-                    )
-
-        def silu(half, tile):
-            nc.scalar.activation(out=flat(silu_a[half][tile]), in_=woven(a_bank[half][tile]), func=SILU)
-
-        def value(half, tile, passes=(0, 1)):
-            js = cols(tile)
-            for a in passes:
-                for t in range(PACK):
-                    ws = cols(PACK * a + t)
-                    nc.tensor.matmul_mx(
-                        out=b_bank[half][tile][:, cols(t)], lhsT=w2_dealt[half][:, ws].bitcast(FP4X4),
-                        lhsT_scale=w2_s_dealt[half][:, ws],
-                        rhs=v_w[a][:, js].bitcast(FP8X4), rhs_scale=v_s[a][:, js],
-                        start=(a == 0 and t == 0), stop=(a == 1 and t == PACK - 1),
-                    )
-
-        def multiply(half, tile):
-            nc.vector.tensor_tensor(out=flat(gated[half][tile]), in0=woven(b_bank[half][tile]), in1=flat(silu_a[half][tile]), op=MULT)
-
-        def sense(half, tile):
-            js = cols(tile)
-            for t in range(PACK):
+        def gate(half, k, a):
+            g, u = divmod(k, 2)
+            part = w1_q[half][a]
+            for e in range(2):
+                ws = cols(2 * u + e)
                 nc.tensor.matmul_mx(
-                    out=c_bank[half][tile][:, cols(t)], lhsT=w3_q[half]["codes"][:, cols(t)].bitcast(FP8X4),
-                    lhsT_scale=w3_q[half]["plane"][:, cols(t)],
-                    rhs=v2_w[:, js].bitcast(FP8X4), rhs_scale=v2_s[:, js], start=True, stop=True,
+                    out=a_bank[k][:, pair(e)], lhsT=part["codes"][:, ws].bitcast(FP8X4), lhsT_scale=part["plane"][:, ws],
+                    rhs=v_w[a][:, pair(g)].bitcast(FP8X4), rhs_scale=v_s[a][:, pair(g)],
+                    start=(a == 0 and e == 0), stop=(a == 1 and e == 1),
                 )
 
-        def add(half, tile):
-            nc.vector.tensor_tensor(out=flat(h_cols[half][tile]), in0=woven(c_bank[half][tile]), in1=flat(gated[half][tile]), op=ADD)
+        def value(half, k, a):
+            g, u = divmod(k, 2)
+            for e in range(2):
+                ws = cols(PACK * (2 * half + a) + 2 * u + e)
+                nc.tensor.matmul_mx(
+                    out=b_bank[k][:, pair(e)], lhsT=w2_dealt[:, ws].bitcast(FP4X4), lhsT_scale=w2_s_dealt[:, ws],
+                    rhs=v_w[a][:, pair(g)].bitcast(FP8X4), rhs_scale=v_s[a][:, pair(g)],
+                    start=(a == 0 and e == 0), stop=(a == 1 and e == 1),
+                )
 
-        def quantise_h(half, g):
-            js = slice(PAIR * g, PAIR * (g + 1))
-            nc.vector.quantize_mx(out=h_w[half][:, js].bitcast(FP8X4), scales=h_s[half][:, js], in_=h_pair[half][g])
+        def sense(half, j):
+            part = w3_q[half]
+            for t in range(PACK):
+                nc.tensor.matmul_mx(
+                    out=c_bank[half][j][:, cols(t)], lhsT=part["codes"][:, cols(t)].bitcast(FP8X4), lhsT_scale=part["plane"][:, cols(t)],
+                    rhs=v2_w[:, cols(j)].bitcast(FP8X4), rhs_scale=v2_s[:, cols(j)], start=True, stop=True,
+                )
 
-        def quantise_first_half():
-            nc.vector.quantize_mx(out=h_w[0][:].bitcast(FP8X4), scales=h_s[0][:], in_=h_first)
+        def silu(half, k):
+            nc.scalar.activation(out=flat(silu_a[half][k], 2), in_=woven(a_bank[k], 2), func=SILU)
 
-        def quantise_tile(tile):
-            nc.vector.quantize_mx(out=h_w[1][:, cols(tile)].bitcast(FP8X4), scales=h_s[1][:, cols(tile)], in_=h_cols[1][tile])
+        def multiply(half, k):
+            g, u = divmod(k, 2)
+            nc.vector.tensor_tensor(out=flat(gated[half][g][:, u, :], 2), in0=woven(b_bank[k], 2), in1=flat(silu_a[half][k], 2), op=MULT)
+
+        def multiply_aside(half, k):
+            g, u = divmod(k, 2)
+            nc.gpsimd.tensor_tensor(
+                out=gated[half][g][:, u, :].rearrange("p (r c) -> p r c", r=2), in0=b_aside[g],
+                in1=silu_a[half][k].rearrange("p (r c) -> p r c", r=2), op=MULT,
+            )
+
+        def copy_aside(k):
+            nc.scalar.copy(
+                out=b_aside[k // 2].rearrange("p r (j e) -> p r j e", e=2), in_=b_bank[k][:].rearrange("p (e r j) -> p r j e", e=2, r=2),
+            )
+
+        def add(half, j):
+            g, e = divmod(j, 2)
+            nc.vector.tensor_tensor(
+                out=h_cols[half][j].rearrange("p (j u e) -> p j u e", u=2, e=2),
+                in0=c_bank[half][j][:].rearrange("p (u e j) -> p j u e", u=2, e=2),
+                in1=gated[half][g][:, :, pair(e)].rearrange("p u (j e) -> p j u e", e=2), op=ADD,
+            )
+
+        def quantise_h(half, js, values):
+            nc.vector.quantize_mx(out=h_w[half][:, js].bitcast(FP8X4), scales=h_s[half][:, js], in_=values)
 
         def mix(a, g):
-            js = slice(PAIR * g, PAIR * (g + 1))
             for m in range(2):
                 for i in range(2):
-                    n0 = P * (2 * m + i)
+                    ns = cols(2 * m + i)
                     nc.tensor.matmul_mx(
-                        out=y_bank[g][m][:, PAIR * i : PAIR * (i + 1)], lhsT=w4_w[:, a, n0 : n0 + P].bitcast(FP8X4),
-                        lhsT_scale=w4_s[W4_ROW0:, N * a + n0 : N * a + n0 + P],
-                        rhs=h_w[a][:, js].bitcast(FP8X4), rhs_scale=h_s[a][:, js],
+                        out=y_bank[g][m][:, pair(i)], lhsT=w4_w[a][:, ns].bitcast(FP8X4),
+                        lhsT_scale=w4_s[W4_ROW0:, cols(PACK * a + 2 * m + i)],
+                        rhs=h_w[a][:, pair(g)].bitcast(FP8X4), rhs_scale=h_s[a][:, pair(g)],
                         start=(a == 0 and i == 0), stop=(a == 1 and i == 1),
                     )
 
-        def domain(tile, engine="s"):
-            bank = d_bank[tile]
-            nc.tensor.matmul_mx(
-                out=bank[:], lhsT=w5_q["codes"][:, cols(tile)].bitcast(FP8X4), lhsT_scale=w5_q["plane"][:, cols(tile)],
-                rhs=v3_w[:].bitcast(FP4X4), rhs_scale=v3_s, start=True, stop=True,
-            )
-            if engine == "v":
-                nc.vector.tensor_copy(out=d_sb[:, tile, :], in_=bank[:])
-            else:
-                nc.scalar.copy(out=d_sb[:, tile, :], in_=bank[:])
+        def domain(g, m):
+            for i in range(2):
+                ns = cols(2 * m + i)
+                nc.tensor.matmul_mx(
+                    out=d_bank[g][m][:, pair(i)], lhsT=w5_q["codes"][:, ns].bitcast(FP8X4), lhsT_scale=w5_q["plane"][:, ns],
+                    rhs=v3_w[:, pair(g)].bitcast(FP4X4), rhs_scale=v3_s[:, pair(g)], start=True, stop=True,
+                )
+            nc.scalar.copy(out=d_sb[g][m][:], in_=d_bank[g][m][:])
 
         def finish(g, m):
-            js = slice(PAIR * g, PAIR * (g + 1))
-            nc.vector.tensor_tensor(
-                out=result[g][m][:], in0=y_bank[g][m][:].rearrange("p (i j) -> p i j", i=2),
-                in1=d_sb[:, 2 * m : 2 * m + 2, js], op=MULT,
+            nc.vector.tensor_tensor(out=result[g][m][:], in0=y_bank[g][m][:], in1=d_sb[g][m][:], op=MULT)
+            nc.sync.dma_start(
+                out=out[pair(m), pair(g)].rearrange("(i p) j -> p i j", p=P), in_=result[g][m][:].rearrange("p (i j) -> p i j", i=2),
             )
-            nc.sync.dma_start(out=out[2 * P * m : 2 * P * (m + 1), js].rearrange("(i p) j -> p i j", p=P), in_=result[g][m][:])
 
-        def finish_tile(g, tile):
-            m, i = divmod(tile, 2)
-            js = slice(PAIR * g, PAIR * (g + 1))
-            nc.vector.tensor_tensor(
-                out=result[g][m][:, i, :], in0=y_bank[g][m][:, PAIR * i : PAIR * (i + 1)], in1=d_sb[:, tile, js], op=MULT,
-            )
-            nc.sync.dma_start(out=out[cols(tile), js], in_=result[g][m][:, i, :])
+        def finish_half(g, m, i):
+            nc.vector.tensor_tensor(out=result[g][m][:, pair(i)], in0=y_bank[g][m][:, pair(i)], in1=d_sb[g][m][:, pair(i)], op=MULT)
+            nc.sync.dma_start(out=out[cols(2 * m + i), pair(g)], in_=result[g][m][:, pair(i)])
 
+        nc.vector.memset(w2_s[:].bitcast(I32), 0)
         nc.vector.memset(tab_s[32:64, :].bitcast(I32), 0)
         nc.vector.memset(tab_s[64:P, :].bitcast(I32), 0)
-        for plane in (tab2_s, tab3_s, planes[0], planes[1], w4_s, w2_s):
-            nc.vector.memset(plane[:].bitcast(I32), 0)
+        for plane in (tab3_s, v_s[0], v_s[1], tab2_s, planes23, w4_s):
+            nc.gpsimd.memset(plane[:].bitcast(I32), 0)
 
         nc.sync.dma_start(list1[:], offs)
-        load_both_passes()
-        nc.sync.dma_start(list3[:], offs3)
-        nc.sync.dma_start(out=tab3_w[:].bitcast(I32), in_=tab3_words[0].bitcast(I32))
-        load_w2(0)
-        load_rows(tab2_s, tab2_scales)
-        nc.sync.dma_start(list2[:], offs2)
-        load_rows(tab3_s, tab3_scales)
+        nc.sync.dma_start(out=tab_s[0 : 2 * ROWS, :].bitcast(I32), in_=tab_scales.rearrange("a s t -> (a s) t").bitcast(I32))
+        nc.sync.dma_start(out=w2_w[:].bitcast(I32).rearrange("p (a b) -> p a b", a=2), in_=w2_words.bitcast(I32).rearrange("a p b -> p a b"))
+        load_plane(w2_s, w2_scales, 0)
         load_block(w1_q[0][0])
-        gather(picked_s[0][:], tab_s[:], list1)
+        nc.sync.dma_start(list3[:], offs3)
+        load_rows(tab3_s, tab3_scales)
+        nc.sync.dma_start(out=tab3_w[:].bitcast(I32), in_=tab3_words[0].bitcast(I32))
         load_e4m3_words(tab_w[0], tab_words[0])
+        gather(picked1, tab_s, list1)
         place_pass(0)
+        nc.sync.dma_start(list2[:], offs2)
+        load_rows(tab2_s, tab2_scales)
         load_block(w1_q[0][1])
         place_pass(1)
-        gather(v3_w[:], tab3_w[:], list3)
-        gather(picked_s[1][:, 0:S], tab2_s[:], list2)
-        gather(picked_s[1][:, S : 2 * S], tab3_s[:], list3)
         load_e4m3_words(tab_w[1], tab_words[1])
-        load_plane(nc.sync, w2_s, w2_scales, 0)
-        load_w2(1)
         load_block(w1_q[1][0])
-        load_block(w1_q[1][1])
-        load_e4m3_words(tab2_w, tab2_words[0])
-        load_block(w3_q[0])
-        place_rows(nc.sync, 1)
-        load_block(w3_q[1])
-        load_block(w5_q)
-        load_plane(nc.sync, w4_s, w4_scales, W4_ROW0)
-        load_w4()
-
-        round_piece(w1_q[0][0], 0, 64, "s")
-        round_piece(w1_q[0][0], 64, 128, "s")
-        deal_w2_words(0)
+        deal(w2_dealt, w2_w)
+        deal(w2_s_dealt, w2_s)
+        nc.vector.tensor_copy(picked23[:, S : 2 * S], tab3_s[:].indirect(list3[:]))
+        gather(v3_w, tab3_w, list3)
+        round_block(w1_q[0][0], 88)
         quantise(w1_q[0][0])
-        gather(v_w[0][:], tab_w[0][:], list1)
-        round_piece(w1_q[0][1], 0, 64, "s")
-        round_piece(w1_q[0][1], 64, 128, "v")
+        gather(v_w[0], tab_w[0], list1)
+        nc.vector.tensor_copy(picked23[:, 0:S], tab2_s[:].indirect(list2[:]))
+        load_block(w1_q[1][1])
+        place_rows23()
+        load_block(w3_q[0])
+        load_e4m3_words(tab2_w, tab2_words[0])
+        load_halves(w3_q[1])
+        load_plane(w4_s, w4_scales, W4_ROW0)
+        load_e4m3_words(w4_w[0], w4_words[0])
+        load_halves(w5_q)
+        load_e4m3_words(w4_w[1], w4_words[1])
+
+        for k in range(4):
+            gate(0, k, 0)
+        for k in range(4):
+            value(0, k, 0)
+        round_block(w1_q[0][1], 48, "v")
         quantise(w1_q[0][1])
-        gather(v_w[1][:], tab_w[1][:], list1)
-        deal_w2_scales(0)
-        deal_w2_scales(1)
-        deal_w2_words(1)
-        gate(0, 0, (0,))
-        gate(0, 1, (0,))
-        gate(0, 2, (0,))
-        gate(0, 3, (0,))
-        gate(0, 0, (1,))
-        gate(0, 1, (1,))
-        gate(0, 2, (1,))
-        gate(0, 3, (1,))
-        value(0, 0, (0,))
-        value(0, 0, (1,))
-        value(0, 1, (0,))
-        value(0, 1, (1,))
-        value(0, 2, (0,))
-        value(0, 2, (1,))
-        value(0, 3, (0,))
-        value(0, 3, (1,))
-        silu(0, 0)
-        silu(0, 1)
-        silu(0, 2)
-        silu(0, 3)
-        multiply(0, 0)
-        multiply(0, 1)
-        round_piece(w1_q[1][0], 0, 56, "s")
-        round_piece(w1_q[1][0], 56, 128, "v")
+        for g in range(2):
+            gather(v_w[1], tab_w[1], list1, PAIR * g, PAIR * (g + 1))
+        for k in range(4):
+            gate(0, k, 1)
+            value(0, k, 1)
+            silu(0, k)
+            multiply(0, k)
+        round_piece(w1_q[1][0], 0, 40, "s")
+        round_piece(w1_q[1][0], 40, 96, "g")
+        round_piece(w1_q[1][0], 96, P, "v")
         quantise(w1_q[1][0])
-        round_piece(w1_q[1][1], 0, 76, "s")
-        round_piece(w1_q[1][1], 76, 128, "v")
+        round_block(w1_q[1][1], 64, "v")
         quantise(w1_q[1][1])
-        multiply(0, 2)
-        multiply(0, 3)
-        gather(v2_w[:], tab2_w[:], list2)
-        gate(1, 0)
-        gate(1, 1)
-        gate(1, 2)
-        gate(1, 3)
-        value(1, 0)
-        value(1, 1)
-        value(1, 2)
-        value(1, 3)
-        silu(1, 0)
-        round_piece(w3_q[0], 0, 64, "s")
-        round_piece(w3_q[0], 64, 128, "v")
+        for k in range(4):
+            value(1, k, 0)
+            value(1, k, 1)
+            gate(1, k, 0)
+        copy_aside(1)
+        copy_aside(3)
+        round_block(w3_q[0], 32, "v")
         quantise(w3_q[0])
+        for k in range(4):
+            gate(1, k, 1)
+            silu(1, k)
         multiply(1, 0)
-        silu(1, 1)
-        silu(1, 2)
-        multiply(1, 1)
+        multiply_aside(1, 1)
+        for j0, j1 in ((0, P), (P, S)):
+            gather(v2_w, tab2_w, list2, j0, j1)
+        gated[1].append(sbuf("gated11", [P, 2, BANK], F32, "tab2_w")[:])
         multiply(1, 2)
-        round_piece(w3_q[1], 64, 128, "s")
-        round_piece(w3_q[1], 0, 64, "s")
-        sense(0, 0)
-        sense(0, 1)
-        sense(0, 2)
-        sense(0, 3)
-        add(0, 0)
-        add(0, 1)
-        add(0, 2)
+        multiply_aside(1, 3)
+        round_halves(w3_q[1], True)
+        for j in range(4):
+            sense(0, j)
+        for j in range(3):
+            add(0, j)
         quantise(w3_q[1])
         add(0, 3)
-        silu(1, 3)
-        multiply(1, 3)
-        quantise_first_half()
-        sense(1, 0)
-        sense(1, 1)
-        sense(1, 2)
-        sense(1, 3)
-        round_piece(w5_q, 0, 64, "s", False)
-        round_piece(w5_q, 64, 128, "s", False)
+        for j in range(4):
+            sense(1, j)
+        round_halves(w5_q, False)
         add(1, 0)
-        quantise_half(w5_q, 0)
-        domain(0, "s")
-        domain(1, "s")
-        add(1, 1)
-        quantise_half(w5_q, 1)
-        domain(2, "s")
-        domain(3, "s")
-        quantise_h(1, 0)
-        add(1, 2)
-        add(1, 3)
+        quantise_h(0, slice(0, S), h_first)
         mix(0, 0)
-        mix(1, 0)
-        quantise_tile(2)
-        quantise_tile(3)
         mix(0, 1)
+        quantise(w5_q)
+        domain(0, 0)
+        add(1, 1)
+        domain(0, 1)
+        add(1, 2)
+        domain(1, 0)
+        quantise_h(1, pair(0), h_second[:, 0 : 2 * PASS])
+        mix(1, 0)
+        add(1, 3)
+        domain(1, 1)
+        quantise_h(1, cols(2), h_cols[1][2])
+        quantise_h(1, cols(3), h_cols[1][3])
         mix(1, 1)
         finish(0, 0)
         finish(0, 1)
         finish(1, 0)
-        finish_tile(1, 2)
-        finish_tile(1, 3)
+        finish_half(1, 1, 0)
+        finish_half(1, 1, 1)

@@ -85,7 +85,7 @@ def tile_list_abbreviation_expansion_features_kernel(
 
         silu_tiles = [sbuf(f"silu{k}", [P, BANK], F32)[:] for k in range(4)]
         silu_a = [silu_tiles, [w3_q[0]["raw"][:, BANK * k : BANK * (k + 1)] for k in range(4)]]
-        gated = [[sbuf(f"gated0{g}", [P, 2, BANK], F32)[:] for g in range(2)], [sbuf("gated10", [P, 2, BANK], F32)[:]]]
+        gated = [[sbuf(f"gated0{g}", [P, 2, BANK], F32)[:] for g in range(2)]]
         b_aside = [w1_q[1][1]["raw"][:].rearrange("p (i c) -> p i c", i=PACK)[:, 2 * g : 2 * g + 2, 0:PAIR] for g in range(2)]
         h_first = w3_q[1]["room"][:, 0 : PACK * S]
         h_second = w5_q["room"][:, 0 : PACK * S]
@@ -272,7 +272,7 @@ def tile_list_abbreviation_expansion_features_kernel(
         nc.vector.memset(tab_s[32:64, :].bitcast(I32), 0)
         nc.vector.memset(tab_s[64:P, :].bitcast(I32), 0)
         for plane in (tab3_s, v_s[0], v_s[1], tab2_s, planes23, w4_s):
-            nc.gpsimd.memset(plane[:].bitcast(I32), 0)
+            nc.vector.memset(plane[:].bitcast(I32), 0)
 
         nc.sync.dma_start(list1[:], offs)
         nc.sync.dma_start(out=tab_s[0 : 2 * ROWS, :].bitcast(I32), in_=tab_scales.rearrange("a s t -> (a s) t").bitcast(I32))
@@ -295,7 +295,7 @@ def tile_list_abbreviation_expansion_features_kernel(
         deal(w2_s_dealt, w2_s)
         nc.vector.tensor_copy(picked23[:, S : 2 * S], tab3_s[:].indirect(list3[:]))
         gather(v3_w, tab3_w, list3)
-        round_block(w1_q[0][0], 88)
+        round_piece(w1_q[0][0], 0, P, "s")
         quantise(w1_q[0][0])
         gather(v_w[0], tab_w[0], list1)
         nc.vector.tensor_copy(picked23[:, 0:S], tab2_s[:].indirect(list2[:]))
@@ -322,9 +322,7 @@ def tile_list_abbreviation_expansion_features_kernel(
             value(0, k, 1)
             silu(0, k)
             multiply(0, k)
-        round_piece(w1_q[1][0], 0, 40, "s")
-        round_piece(w1_q[1][0], 40, 96, "g")
-        round_piece(w1_q[1][0], 96, P, "v")
+        round_block(w1_q[1][0], 64, "v")
         quantise(w1_q[1][0])
         round_block(w1_q[1][1], 64, "v")
         quantise(w1_q[1][1])
@@ -339,11 +337,11 @@ def tile_list_abbreviation_expansion_features_kernel(
         for k in range(4):
             gate(1, k, 1)
             silu(1, k)
+        gather(v2_w, tab2_w, list2)
+        gated_second = sbuf("gated1", [P, 2, 2, BANK], F32, "tab2_w")
+        gated.append([gated_second[:, g, :, :] for g in range(2)])
         multiply(1, 0)
         multiply_aside(1, 1)
-        for j0, j1 in ((0, P), (P, S)):
-            gather(v2_w, tab2_w, list2, j0, j1)
-        gated[1].append(sbuf("gated11", [P, 2, BANK], F32, "tab2_w")[:])
         multiply(1, 2)
         multiply_aside(1, 3)
         round_halves(w3_q[1], True)

@@ -213,7 +213,7 @@ def tile_list_abbreviation_expansion_features_kernel(
 
         def multiply(half, k):
             g, u = divmod(k, 2)
-            nc.vector.tensor_tensor(out=flat(gated[half][g][:, u, :], 2), in0=woven(b_bank[k], 2), in1=flat(silu_a[half][k], 2), op=MULT)
+            nc.vector.tensor_tensor(out=flat(gated[half][g][:, u, :], 2), in0=flat(silu_a[half][k], 2), in1=woven(b_bank[k], 2), op=MULT)
 
         def multiply_aside(half, k):
             g, u = divmod(k, 2)
@@ -231,8 +231,8 @@ def tile_list_abbreviation_expansion_features_kernel(
             g, e = divmod(j, 2)
             nc.vector.tensor_tensor(
                 out=h_cols[half][j].rearrange("p (j u e) -> p j u e", u=2, e=2),
-                in0=c_bank[half][j][:].rearrange("p (u e j) -> p j u e", u=2, e=2),
-                in1=gated[half][g][:, :, pair(e)].rearrange("p u (j e) -> p j u e", e=2), op=ADD,
+                in1=c_bank[half][j][:].rearrange("p (u e j) -> p j u e", u=2, e=2),
+                in0=gated[half][g][:, :, pair(e)].rearrange("p u (j e) -> p j u e", e=2), op=ADD,
             )
 
         def quantise_h(half, js, values):
@@ -259,13 +259,13 @@ def tile_list_abbreviation_expansion_features_kernel(
             nc.scalar.copy(out=d_sb[g][m][:], in_=d_bank[g][m][:])
 
         def finish(g, m):
-            nc.vector.tensor_tensor(out=result[g][m][:], in0=y_bank[g][m][:], in1=d_sb[g][m][:], op=MULT)
+            nc.vector.tensor_tensor(out=result[g][m][:], in0=d_sb[g][m][:], in1=y_bank[g][m][:], op=MULT)
             nc.sync.dma_start(
                 out=out[pair(m), pair(g)].rearrange("(i p) j -> p i j", p=P), in_=result[g][m][:].rearrange("p (i j) -> p i j", i=2),
             )
 
         def finish_half(g, m, i):
-            nc.vector.tensor_tensor(out=result[g][m][:, pair(i)], in0=y_bank[g][m][:, pair(i)], in1=d_sb[g][m][:, pair(i)], op=MULT)
+            nc.vector.tensor_tensor(out=result[g][m][:, pair(i)], in0=d_sb[g][m][:, pair(i)], in1=y_bank[g][m][:, pair(i)], op=MULT)
             nc.sync.dma_start(out=out[cols(2 * m + i), pair(g)], in_=result[g][m][:, pair(i)])
 
         nc.vector.memset(w2_s[:].bitcast(I32), 0)

@@ -86,7 +86,6 @@ def tile_list_abbreviation_expansion_features_kernel(
         silu_tiles = [sbuf(f"silu{k}", [P, BANK], F32)[:] for k in range(4)]
         silu_a = [silu_tiles, [w3_q[0]["raw"][:, BANK * k : BANK * (k + 1)] for k in range(4)]]
         gated = [[sbuf(f"gated0{g}", [P, 2, BANK], F32)[:] for g in range(2)]]
-        b_aside = [w1_q[1][1]["raw"][:].rearrange("p (i c) -> p i c", i=PACK)[:, 2 * g : 2 * g + 2, 0:PAIR] for g in range(2)]
         h_first = w3_q[1]["room"][:, 0 : PACK * S]
         h_second = w5_q["room"][:, 0 : PACK * S]
         h_cols = [[h[:, PASS * j : PASS * (j + 1)] for j in range(4)] for h in (h_first, h_second)]
@@ -215,18 +214,6 @@ def tile_list_abbreviation_expansion_features_kernel(
             g, u = divmod(k, 2)
             nc.vector.tensor_tensor(out=flat(gated[half][g][:, u, :], 2), in0=flat(silu_a[half][k], 2), in1=woven(b_bank[k], 2), op=MULT)
 
-        def multiply_aside(half, k):
-            g, u = divmod(k, 2)
-            nc.gpsimd.tensor_tensor(
-                out=gated[half][g][:, u, :].rearrange("p (r c) -> p r c", r=2), in0=b_aside[g],
-                in1=silu_a[half][k].rearrange("p (r c) -> p r c", r=2), op=MULT,
-            )
-
-        def copy_aside(k):
-            nc.scalar.copy(
-                out=b_aside[k // 2].rearrange("p r (j e) -> p r j e", e=2), in_=b_bank[k][:].rearrange("p (e r j) -> p r j e", e=2, r=2),
-            )
-
         def add(half, j):
             g, e = divmod(j, 2)
             nc.vector.tensor_tensor(
@@ -324,15 +311,13 @@ def tile_list_abbreviation_expansion_features_kernel(
             multiply(0, k)
         round_block(w1_q[1][0], 64, "v")
         quantise(w1_q[1][0])
-        round_block(w1_q[1][1], 64, "v")
+        round_block(w1_q[1][1], 72, "v")
         quantise(w1_q[1][1])
         for k in range(4):
             value(1, k, 0)
             value(1, k, 1)
             gate(1, k, 0)
-        copy_aside(1)
-        copy_aside(3)
-        round_block(w3_q[0], 32, "v")
+        round_block(w3_q[0], 40, "v")
         quantise(w3_q[0])
         for k in range(4):
             gate(1, k, 1)
@@ -341,9 +326,9 @@ def tile_list_abbreviation_expansion_features_kernel(
         gated_second = sbuf("gated1", [P, 2, 2, BANK], F32, "tab2_w")
         gated.append([gated_second[:, g, :, :] for g in range(2)])
         multiply(1, 0)
-        multiply_aside(1, 1)
+        multiply(1, 1)
         multiply(1, 2)
-        multiply_aside(1, 3)
+        multiply(1, 3)
         round_halves(w3_q[1], True)
         for j in range(4):
             sense(0, j)

@@ -24,6 +24,7 @@ BANK = 512
 PAIR = 2 * P
 ROWS = 16
 W4_ROW0 = 4
+LEAD = 3 * P
 
 
 def tile_list_abbreviation_expansion_features_kernel(
@@ -58,20 +59,35 @@ def tile_list_abbreviation_expansion_features_kernel(
         w4_w = [sbuf(f"w4_w{a}", [P, N], U32) for a in range(2)]
         w4_s = sbuf("w4_s", [P, 2 * N], U8)
 
-        def operand(name, rows, lead=0, halved=False):
-            room = sbuf("grouped_" + name, [P, lead + PACK * PASS], BF16)
+        def operand(name, rows, raw):
             return {
                 "rows": rows,
-                "raw": [sbuf(f"raw_{name}{e}", [P, PACK, PAIR], F32) for e in range(2)] if halved else sbuf("raw_" + name, [P, PACK * PASS], F32),
-                "room": room,
-                "grouped": room[:, lead : lead + PACK * PASS],
+                "raw": raw,
+                "grouped": sbuf("grouped_" + name, [P, PACK * PASS], BF16)[:],
                 "codes": sbuf("codes_" + name, [P, PASS], U32),
                 "plane": sbuf("plane_" + name, [P, PASS], U8),
             }
 
-        w1_q = [[operand(f"w1_{half}{a}", w1[PASS * a : PASS * (a + 1), PASS * half : PASS * (half + 1)]) for a in range(2)] for half in range(2)]
-        w3_q = [operand("w3_0", w3[:, 0:PASS]), operand("w3_1", w3[:, PASS:H], 3 * PASS, True)]
-        w5_q = operand("w5", w5, PASS, True)
+        def by_rows(ap):
+            return ap.rearrange("p (i c) -> p i c", i=PACK)
+
+        w1_room = sbuf("w1_room", [P, BANK + LEAD + PACK * PASS], F32)
+        w3_first_room = sbuf("w3_first_room", [P, PACK, PAIR + PASS], F32)
+        w3_last_room = sbuf("w3_last_room", [P, PASS + PACK * PAIR], F32)
+        w5_last_room = sbuf("w5_last_room", [P, PAIR + PACK * PAIR], F32)
+        w1_raw = [
+            [by_rows(sbuf(f"raw_w1_0{a}", [P, PACK * PASS], F32)[:]) for a in range(2)],
+            [by_rows(w1_room[:, BANK + LEAD :]), by_rows(sbuf("raw_w1_11", [P, PACK * PASS], F32)[:])],
+        ]
+        w1_q = [
+            [operand(f"w1_{half}{a}", w1[PASS * a : PASS * (a + 1), PASS * half : PASS * (half + 1)], w1_raw[half][a]) for a in range(2)]
+            for half in range(2)
+        ]
+        w3_q = [
+            operand("w3_0", w3[:, 0:PASS], w3_first_room[:, :, PAIR:]),
+            operand("w3_1", w3[:, PASS:H], [by_rows(sbuf("raw_w3_10", [P, PACK * PAIR], F32)[:]), by_rows(w3_last_room[:, PASS:])]),
+        ]
+        w5_q = operand("w5", w5, [by_rows(sbuf("raw_w50", [P, PACK * PAIR], F32)[:]), by_rows(w5_last_room[:, PAIR:])])
 
         v_w = [sbuf(f"v_w{a}", [P, S], U32) for a in range(2)]
         v2_w = sbuf("v2_w", [P, S], U32)
@@ -83,11 +99,10 @@ def tile_list_abbreviation_expansion_features_kernel(
         v2_s = planes23[:, 0:S]
         v3_s = planes23[:, S : 2 * S]
 
-        silu_tiles = [sbuf(f"silu{k}", [P, BANK], F32)[:] for k in range(4)]
-        silu_a = [silu_tiles, [w3_q[0]["raw"][:, BANK * k : BANK * (k + 1)] for k in range(4)]]
-        gated = [[sbuf(f"gated0{g}", [P, 2, BANK], F32)[:] for g in range(2)]]
-        h_first = w3_q[1]["room"][:, 0 : PACK * S]
-        h_second = w5_q["room"][:, 0 : PACK * S]
+        silu_a = [[sbuf(f"silu{k}", [P, BANK], F32)[:] for k in range(4)], [w3_first_room[:, k, 0:BANK] for k in range(4)]]
+        gated = [[sbuf("gated00", [P, 2, BANK], F32)[:], w1_room[:, 0 : 2 * BANK].rearrange("p (u c) -> p u c", u=2)], [sbuf("gated10", [P, 2, BANK], F32)[:]]]
+        h_first = w3_last_room[:, 0 : 2 * S].bitcast(BF16)
+        h_second = w5_last_room[:, 0 : 2 * S].bitcast(BF16)
         h_cols = [[h[:, PASS * j : PASS * (j + 1)] for j in range(4)] for h in (h_first, h_second)]
         h_w = [sbuf(f"h_w{a}", [P, S], U32) for a in range(2)]
         h_s = [sbuf(f"h_s{a}", [P, S], U8) for a in range(2)]
@@ -109,13 +124,13 @@ def tile_list_abbreviation_expansion_features_kernel(
 
         def load_block(part):
             nc.sync.dma_start(
-                out=part["raw"][:].rearrange("p (i c) -> p i c", i=PACK),
+                out=part["raw"],
                 in_=part["rows"].rearrange("(p i) c -> p i c", i=PACK),
             )
 
         def load_halves(part):
             for e in range(2):
-                nc.sync.dma_start(out=part["raw"][e][:], in_=part["rows"][:, pair(e)].rearrange("(p i) c -> p i c", i=PACK))
+                nc.sync.dma_start(out=part["raw"][e], in_=part["rows"][:, pair(e)].rearrange("(p i) c -> p i c", i=PACK))
 
         def load_e4m3_words(tile, words):
             nc.sync.dma_start(out=tile[:].bitcast(I32), in_=words.rearrange("p t i -> p (t i)").bitcast(I32))
@@ -134,16 +149,22 @@ def tile_list_abbreviation_expansion_features_kernel(
         def gather(picked, window, entries, j0=0, j1=S):
             nc.vector.tensor_copy(picked[:, j0:j1], window[:].indirect(entries[:, j0 // 16 : j1 // 16]))
 
-        def deal(dealt, natural):
+        def deal_scales():
             nc.vector.tensor_copy(
-                out=dealt[:].rearrange("p (h a t m) -> p h a t m", h=2, a=2, t=PACK),
-                in_=natural[:].rearrange("p (a h m t) -> p h a t m", a=2, h=2, t=PACK),
+                out=w2_s_dealt[:].rearrange("p (h a t m) -> p h a t m", h=2, a=2, t=PACK),
+                in_=w2_s[:].rearrange("p (a h m t) -> p h a t m", a=2, h=2, t=PACK),
+            )
+
+        def deal_words(half, copy):
+            copy(
+                out=w2_dealt[:, H * half : H * (half + 1)].rearrange("p (a t m) -> p a t m", a=2, t=PACK),
+                in_=w2_w[:].rearrange("p (a h m t) -> p h a t m", a=2, h=2, t=PACK)[:, half, :, :, :],
             )
 
         def round_piece(part, m0, m1, engine, dealt=True):
             order = "p (t m i) -> p m i t" if dealt else "p (m t i) -> p m i t"
             dst = part["grouped"].rearrange(order, t=PACK, i=PACK)[:, m0:m1, :, :]
-            src = part["raw"][:].rearrange("p (i m t) -> p m i t", i=PACK, t=PACK)[:, m0:m1, :, :]
+            src = part["raw"].rearrange("p i (m t) -> p m i t", t=PACK)[:, m0:m1, :, :]
             if engine == "v":
                 nc.vector.tensor_copy(out=dst, in_=src)
             elif engine == "g":
@@ -161,7 +182,7 @@ def tile_list_abbreviation_expansion_features_kernel(
             for e in range(2):
                 nc.scalar.copy(
                     out=part["grouped"].rearrange(order, t=PACK, i=PACK)[:, 64 * e : 64 * (e + 1), :, :],
-                    in_=part["raw"][e][:].rearrange("p i (m t) -> p m i t", t=PACK),
+                    in_=part["raw"][e].rearrange("p i (m t) -> p m i t", t=PACK),
                 )
 
         def quantise(part):
@@ -258,38 +279,38 @@ def tile_list_abbreviation_expansion_features_kernel(
         nc.vector.memset(w2_s[:].bitcast(I32), 0)
         nc.vector.memset(tab_s[32:64, :].bitcast(I32), 0)
         nc.vector.memset(tab_s[64:P, :].bitcast(I32), 0)
-        for plane in (tab3_s, v_s[0], v_s[1], tab2_s, planes23, w4_s):
+        for plane in (tab3_s, tab2_s, v_s[0], v_s[1], planes23, w4_s):
             nc.vector.memset(plane[:].bitcast(I32), 0)
 
         nc.sync.dma_start(list1[:], offs)
         nc.sync.dma_start(out=tab_s[0 : 2 * ROWS, :].bitcast(I32), in_=tab_scales.rearrange("a s t -> (a s) t").bitcast(I32))
-        nc.sync.dma_start(out=w2_w[:].bitcast(I32).rearrange("p (a b) -> p a b", a=2), in_=w2_words.bitcast(I32).rearrange("a p b -> p a b"))
         load_plane(w2_s, w2_scales, 0)
         load_block(w1_q[0][0])
         nc.sync.dma_start(list3[:], offs3)
         load_rows(tab3_s, tab3_scales)
-        nc.sync.dma_start(out=tab3_w[:].bitcast(I32), in_=tab3_words[0].bitcast(I32))
+        nc.sync.dma_start(list2[:], offs2)
+        load_rows(tab2_s, tab2_scales)
+        nc.sync.dma_start(out=w2_w[:].bitcast(I32).rearrange("p (a b) -> p a b", a=2), in_=w2_words.bitcast(I32).rearrange("a p b -> p a b"))
         load_e4m3_words(tab_w[0], tab_words[0])
         gather(picked1, tab_s, list1)
         place_pass(0)
-        nc.sync.dma_start(list2[:], offs2)
-        load_rows(tab2_s, tab2_scales)
         load_block(w1_q[0][1])
         place_pass(1)
         load_e4m3_words(tab_w[1], tab_words[1])
+        nc.sync.dma_start(out=tab3_w[:].bitcast(I32), in_=tab3_words[0].bitcast(I32))
         load_block(w1_q[1][0])
-        deal(w2_dealt, w2_w)
-        deal(w2_s_dealt, w2_s)
+        deal_scales()
         nc.vector.tensor_copy(picked23[:, S : 2 * S], tab3_s[:].indirect(list3[:]))
-        gather(v3_w, tab3_w, list3)
+        nc.vector.tensor_copy(picked23[:, 0:S], tab2_s[:].indirect(list2[:]))
         round_piece(w1_q[0][0], 0, P, "s")
+        deal_words(0, nc.scalar.copy)
+        deal_words(1, nc.scalar.copy)
         quantise(w1_q[0][0])
         gather(v_w[0], tab_w[0], list1)
-        nc.vector.tensor_copy(picked23[:, 0:S], tab2_s[:].indirect(list2[:]))
         load_block(w1_q[1][1])
-        place_rows23()
         load_block(w3_q[0])
         load_e4m3_words(tab2_w, tab2_words[0])
+        place_rows23()
         load_halves(w3_q[1])
         load_plane(w4_s, w4_scales, W4_ROW0)
         load_e4m3_words(w4_w[0], w4_words[0])
@@ -300,41 +321,45 @@ def tile_list_abbreviation_expansion_features_kernel(
             gate(0, k, 0)
         for k in range(4):
             value(0, k, 0)
-        round_block(w1_q[0][1], 48, "v")
+        round_block(w1_q[0][1], 32, "v")
         quantise(w1_q[0][1])
         for g in range(2):
             gather(v_w[1], tab_w[1], list1, PAIR * g, PAIR * (g + 1))
+        gather(v3_w, tab3_w, list3)
         for k in range(4):
             gate(0, k, 1)
             value(0, k, 1)
             silu(0, k)
-            multiply(0, k)
-        round_block(w1_q[1][0], 64, "v")
+        multiply(0, 0)
+        multiply(0, 1)
+        multiply(0, 2)
+        round_block(w1_q[1][0], 40, "v")
+        multiply(0, 3)
         quantise(w1_q[1][0])
-        round_block(w1_q[1][1], 72, "v")
+        round_block(w1_q[1][1], 76, "v")
         quantise(w1_q[1][1])
         for k in range(4):
             value(1, k, 0)
             value(1, k, 1)
             gate(1, k, 0)
-        round_block(w3_q[0], 40, "v")
+        round_block(w3_q[0], 64, "v")
         quantise(w3_q[0])
         for k in range(4):
             gate(1, k, 1)
             silu(1, k)
-        gather(v2_w, tab2_w, list2)
-        gated_second = sbuf("gated1", [P, 2, 2, BANK], F32, "tab2_w")
-        gated.append([gated_second[:, g, :, :] for g in range(2)])
         multiply(1, 0)
         multiply(1, 1)
+        gather(v2_w, tab2_w, list2)
+        gated[1].append(sbuf("gated11", [P, 2, BANK], F32, "picked23")[:])
         multiply(1, 2)
         multiply(1, 3)
         round_halves(w3_q[1], True)
         for j in range(4):
             sense(0, j)
-        for j in range(3):
+        for j in range(2):
             add(0, j)
         quantise(w3_q[1])
+        add(0, 2)
         add(0, 3)
         for j in range(4):
             sense(1, j)

@@ -25,6 +25,7 @@ PAIR = 2 * P
 ROWS = 16
 W4_ROW0 = 4
 LEAD = 3 * P
+EDGE = 40
 
 
 def tile_list_abbreviation_expansion_features_kernel(
@@ -61,9 +62,9 @@ def tile_list_abbreviation_expansion_features_kernel(
 
         def operand(name, rows, raw):
             return {
+                "name": name,
                 "rows": rows,
                 "raw": raw,
-                "grouped": sbuf("grouped_" + name, [P, PACK * PASS], BF16)[:],
                 "codes": sbuf("codes_" + name, [P, PASS], U32),
                 "plane": sbuf("plane_" + name, [P, PASS], U8),
             }
@@ -73,8 +74,8 @@ def tile_list_abbreviation_expansion_features_kernel(
 
         w1_room = sbuf("w1_room", [P, BANK + LEAD + PACK * PASS], F32)
         w3_first_room = sbuf("w3_first_room", [P, PACK, PAIR + PASS], F32)
-        w3_last_room = sbuf("w3_last_room", [P, PASS + PACK * PAIR], F32)
-        w5_last_room = sbuf("w5_last_room", [P, PAIR + PACK * PAIR], F32)
+        w3_last_room = sbuf("w3_last_room", [P, PASS + PACK * PASS], F32)
+        w5_room = sbuf("w5_room", [P, PAIR + PACK * PASS], F32)
         w1_raw = [
             [by_rows(sbuf(f"raw_w1_0{a}", [P, PACK * PASS], F32)[:]) for a in range(2)],
             [by_rows(w1_room[:, BANK + LEAD :]), by_rows(sbuf("raw_w1_11", [P, PACK * PASS], F32)[:])],
@@ -85,25 +86,28 @@ def tile_list_abbreviation_expansion_features_kernel(
         ]
         w3_q = [
             operand("w3_0", w3[:, 0:PASS], w3_first_room[:, :, PAIR:]),
-            operand("w3_1", w3[:, PASS:H], [by_rows(sbuf("raw_w3_10", [P, PACK * PAIR], F32)[:]), by_rows(w3_last_room[:, PASS:])]),
+            operand("w3_1", w3[:, PASS:H], by_rows(w3_last_room[:, PASS:])),
         ]
-        w5_q = operand("w5", w5, [by_rows(sbuf("raw_w50", [P, PACK * PAIR], F32)[:]), by_rows(w5_last_room[:, PAIR:])])
+        w5_q = operand("w5", w5, by_rows(w5_room[:, PAIR:]))
 
         v_w = [sbuf(f"v_w{a}", [P, S], U32) for a in range(2)]
         v2_w = sbuf("v2_w", [P, S], U32)
         v3_w = sbuf("v3_w", [P, S], U16)
         picked1 = sbuf("picked1", [P, S], U8)
-        picked23 = sbuf("picked23", [P, 2 * S], U8)
+        picked2 = sbuf("picked2", [P, S], U8)
+        picked3 = sbuf("picked3", [P, S], U8)
         v_s = [sbuf(f"v_s{a}", [P, S], U8) for a in range(2)]
-        planes23 = sbuf("planes23", [P, 2 * S], U8)
-        v2_s = planes23[:, 0:S]
-        v3_s = planes23[:, S : 2 * S]
+        v2_s = sbuf("v2_s", [P, S], U8)
+        v3_s = sbuf("v3_s", [P, S], U8)
 
         silu_a = [[sbuf(f"silu{k}", [P, BANK], F32)[:] for k in range(4)], [w3_first_room[:, k, 0:BANK] for k in range(4)]]
-        gated = [[sbuf("gated00", [P, 2, BANK], F32)[:], w1_room[:, 0 : 2 * BANK].rearrange("p (u c) -> p u c", u=2)], [sbuf("gated10", [P, 2, BANK], F32)[:]]]
+        gated = [[sbuf("gated00", [P, 2, BANK], F32)[:], w1_room[:, 0 : 2 * BANK].rearrange("p (u c) -> p u c", u=2)]]
         h_first = w3_last_room[:, 0 : 2 * S].bitcast(BF16)
-        h_second = w5_last_room[:, 0 : 2 * S].bitcast(BF16)
-        h_cols = [[h[:, PASS * j : PASS * (j + 1)] for j in range(4)] for h in (h_first, h_second)]
+        h_third = w5_room[:, 0:S].bitcast(BF16)
+        h_cols = [
+            [h_first[:, PASS * j : PASS * (j + 1)] for j in range(4)],
+            [h_third[:, 0:PASS], h_third[:, PASS:]] + [w5_q["raw"][:, i, PAIR:].bitcast(BF16) for i in range(2)],
+        ]
         h_w = [sbuf(f"h_w{a}", [P, S], U32) for a in range(2)]
         h_s = [sbuf(f"h_s{a}", [P, S], U8) for a in range(2)]
         d_sb = [[sbuf(f"d{g}{m}", [P, BANK], F32) for m in range(2)] for g in range(2)]
@@ -128,10 +132,6 @@ def tile_list_abbreviation_expansion_features_kernel(
                 in_=part["rows"].rearrange("(p i) c -> p i c", i=PACK),
             )
 
-        def load_halves(part):
-            for e in range(2):
-                nc.sync.dma_start(out=part["raw"][e], in_=part["rows"][:, pair(e)].rearrange("(p i) c -> p i c", i=PACK))
-
         def load_e4m3_words(tile, words):
             nc.sync.dma_start(out=tile[:].bitcast(I32), in_=words.rearrange("p t i -> p (t i)").bitcast(I32))
 
@@ -142,9 +142,9 @@ def tile_list_abbreviation_expansion_features_kernel(
             for r in range(4):
                 nc.sync.dma_start(out=v_s[a][r:P:32, :].bitcast(I32), in_=picked1[ROWS * a + r : ROWS * (a + 1) : 4, :].bitcast(I32))
 
-        def place_rows23():
+        def place_rows(plane, picked):
             for r in range(4):
-                nc.sync.dma_start(out=planes23[r:P:32, :].bitcast(I32), in_=picked23[8 * r : P : 32, :].bitcast(I32))
+                nc.sync.dma_start(out=plane[r:P:32, :].bitcast(I32), in_=picked[8 * r : P : 32, :].bitcast(I32))
 
         def gather(picked, window, entries, j0=0, j1=S):
             nc.vector.tensor_copy(picked[:, j0:j1], window[:].indirect(entries[:, j0 // 16 : j1 // 16]))
@@ -160,6 +160,9 @@ def tile_list_abbreviation_expansion_features_kernel(
                 out=w2_dealt[:, H * half : H * (half + 1)].rearrange("p (a t m) -> p a t m", a=2, t=PACK),
                 in_=w2_w[:].rearrange("p (a h m t) -> p h a t m", a=2, h=2, t=PACK)[:, half, :, :, :],
             )
+
+        def make_room(part, tag=None):
+            part["grouped"] = sbuf("grouped_" + part["name"], [P, PACK * PASS], BF16, tag)[:]
 
         def round_piece(part, m0, m1, engine, dealt=True):
             order = "p (t m i) -> p m i t" if dealt else "p (m t i) -> p m i t"
@@ -177,13 +180,14 @@ def tile_list_abbreviation_expansion_features_kernel(
             round_piece(part, 0, share, "s", dealt)
             round_piece(part, share, P, other, dealt)
 
-        def round_halves(part, dealt):
-            order = "p (t m i) -> p m i t" if dealt else "p (m t i) -> p m i t"
+        def round_with_gpsimd(part, dealt):
+            order = "p (t e m i) -> p e m i t" if dealt else "p (e m t i) -> p e m i t"
+            nc.scalar.copy(
+                out=part["grouped"].rearrange(order, e=2, t=PACK, i=PACK)[:, :, 0:EDGE, :, :],
+                in_=part["raw"].rearrange("p i (e m t) -> p e m i t", e=2, t=PACK)[:, :, 0:EDGE, :, :],
+            )
             for e in range(2):
-                nc.scalar.copy(
-                    out=part["grouped"].rearrange(order, t=PACK, i=PACK)[:, 64 * e : 64 * (e + 1), :, :],
-                    in_=part["raw"][e].rearrange("p i (m t) -> p m i t", t=PACK),
-                )
+                round_piece(part, 64 * e + EDGE, 64 * (e + 1), "g", dealt)
 
         def quantise(part):
             nc.vector.quantize_mx(out=part["codes"][:].bitcast(FP8X4), scales=part["plane"][:], in_=part["grouped"])
@@ -279,7 +283,7 @@ def tile_list_abbreviation_expansion_features_kernel(
         nc.vector.memset(w2_s[:].bitcast(I32), 0)
         nc.vector.memset(tab_s[32:64, :].bitcast(I32), 0)
         nc.vector.memset(tab_s[64:P, :].bitcast(I32), 0)
-        for plane in (tab3_s, tab2_s, v_s[0], v_s[1], planes23, w4_s):
+        for plane in (tab3_s, tab2_s, v_s[0], v_s[1], v2_s, v3_s, w4_s):
             nc.vector.memset(plane[:].bitcast(I32), 0)
 
         nc.sync.dma_start(list1[:], offs)
@@ -295,13 +299,14 @@ def tile_list_abbreviation_expansion_features_kernel(
         gather(picked1, tab_s, list1)
         place_pass(0)
         load_block(w1_q[0][1])
-        place_pass(1)
         load_e4m3_words(tab_w[1], tab_words[1])
+        place_pass(1)
         nc.sync.dma_start(out=tab3_w[:].bitcast(I32), in_=tab3_words[0].bitcast(I32))
         load_block(w1_q[1][0])
         deal_scales()
-        nc.vector.tensor_copy(picked23[:, S : 2 * S], tab3_s[:].indirect(list3[:]))
-        nc.vector.tensor_copy(picked23[:, 0:S], tab2_s[:].indirect(list2[:]))
+        gather(picked3, tab3_s, list3)
+        gather(picked2, tab2_s, list2)
+        make_room(w1_q[0][0])
         round_piece(w1_q[0][0], 0, P, "s")
         deal_words(0, nc.scalar.copy)
         deal_words(1, nc.scalar.copy)
@@ -310,17 +315,19 @@ def tile_list_abbreviation_expansion_features_kernel(
         load_block(w1_q[1][1])
         load_block(w3_q[0])
         load_e4m3_words(tab2_w, tab2_words[0])
-        place_rows23()
-        load_halves(w3_q[1])
+        place_rows(v2_s, picked2)
+        load_block(w3_q[1])
         load_plane(w4_s, w4_scales, W4_ROW0)
+        load_block(w5_q)
         load_e4m3_words(w4_w[0], w4_words[0])
-        load_halves(w5_q)
+        place_rows(v3_s, picked3)
         load_e4m3_words(w4_w[1], w4_words[1])
 
         for k in range(4):
             gate(0, k, 0)
         for k in range(4):
             value(0, k, 0)
+        make_room(w1_q[0][1])
         round_block(w1_q[0][1], 32, "v")
         quantise(w1_q[0][1])
         for g in range(2):
@@ -333,27 +340,34 @@ def tile_list_abbreviation_expansion_features_kernel(
         multiply(0, 0)
         multiply(0, 1)
         multiply(0, 2)
-        round_block(w1_q[1][0], 40, "v")
+        make_room(w1_q[1][0], "tab3_w")
+        round_piece(w1_q[1][0], 0, 40, "s")
+        round_piece(w1_q[1][0], 40, 80, "g")
+        round_piece(w1_q[1][0], 80, P, "v")
         multiply(0, 3)
         quantise(w1_q[1][0])
+        make_room(w1_q[1][1])
         round_block(w1_q[1][1], 76, "v")
         quantise(w1_q[1][1])
         for k in range(4):
             value(1, k, 0)
             value(1, k, 1)
             gate(1, k, 0)
+        make_room(w3_q[0])
         round_block(w3_q[0], 64, "v")
         quantise(w3_q[0])
         for k in range(4):
             gate(1, k, 1)
             silu(1, k)
+        gather(v2_w, tab2_w, list2)
+        gated_second = sbuf("gated1", [P, 2, 2, BANK], F32, "picked2")
+        gated.append([gated_second[:, g, :, :] for g in range(2)])
         multiply(1, 0)
         multiply(1, 1)
-        gather(v2_w, tab2_w, list2)
-        gated[1].append(sbuf("gated11", [P, 2, BANK], F32, "picked23")[:])
         multiply(1, 2)
         multiply(1, 3)
-        round_halves(w3_q[1], True)
+        make_room(w3_q[1], "tab2_w")
+        round_with_gpsimd(w3_q[1], True)
         for j in range(4):
             sense(0, j)
         for j in range(2):
@@ -363,7 +377,8 @@ def tile_list_abbreviation_expansion_features_kernel(
         add(0, 3)
         for j in range(4):
             sense(1, j)
-        round_halves(w5_q, False)
+        make_room(w5_q, "tab2_w")
+        round_with_gpsimd(w5_q, False)
         add(1, 0)
         quantise_h(0, slice(0, S), h_first)
         mix(0, 0)
@@ -374,7 +389,7 @@ def tile_list_abbreviation_expansion_features_kernel(
         domain(0, 1)
         add(1, 2)
         domain(1, 0)
-        quantise_h(1, pair(0), h_second[:, 0 : 2 * PASS])
+        quantise_h(1, pair(0), h_third)
         mix(1, 0)
         add(1, 3)
         domain(1, 1)

@@ -25,7 +25,6 @@ PAIR = 2 * P
 ROWS = 16
 W4_ROW0 = 4
 LEAD = 3 * P
-EDGE = 40
 
 
 def tile_list_abbreviation_expansion_features_kernel(
@@ -74,8 +73,8 @@ def tile_list_abbreviation_expansion_features_kernel(
 
         w1_room = sbuf("w1_room", [P, BANK + LEAD + PACK * PASS], F32)
         w3_first_room = sbuf("w3_first_room", [P, PACK, PAIR + PASS], F32)
-        w3_last_room = sbuf("w3_last_room", [P, PASS + PACK * PASS], F32)
-        w5_room = sbuf("w5_room", [P, PAIR + PACK * PASS], F32)
+        w3_last_room = sbuf("w3_last_room", [P, PASS + PACK * PAIR], F32)
+        w5_room = sbuf("w5_room", [P, PAIR + PACK * PAIR], F32)
         w1_raw = [
             [by_rows(sbuf(f"raw_w1_0{a}", [P, PACK * PASS], F32)[:]) for a in range(2)],
             [by_rows(w1_room[:, BANK + LEAD :]), by_rows(sbuf("raw_w1_11", [P, PACK * PASS], F32)[:])],
@@ -86,9 +85,9 @@ def tile_list_abbreviation_expansion_features_kernel(
         ]
         w3_q = [
             operand("w3_0", w3[:, 0:PASS], w3_first_room[:, :, PAIR:]),
-            operand("w3_1", w3[:, PASS:H], by_rows(w3_last_room[:, PASS:])),
+            operand("w3_1", w3[:, PASS:H], [by_rows(sbuf("raw_w3_10", [P, PACK * PAIR], F32)[:]), by_rows(w3_last_room[:, PASS:])]),
         ]
-        w5_q = operand("w5", w5, by_rows(w5_room[:, PAIR:]))
+        w5_q = operand("w5", w5, [by_rows(sbuf("raw_w50", [P, PACK * PAIR], F32)[:]), by_rows(w5_room[:, PAIR:])])
 
         v_w = [sbuf(f"v_w{a}", [P, S], U32) for a in range(2)]
         v2_w = sbuf("v2_w", [P, S], U32)
@@ -103,11 +102,8 @@ def tile_list_abbreviation_expansion_features_kernel(
         silu_a = [[sbuf(f"silu{k}", [P, BANK], F32)[:] for k in range(4)], [w3_first_room[:, k, 0:BANK] for k in range(4)]]
         gated = [[sbuf("gated00", [P, 2, BANK], F32)[:], w1_room[:, 0 : 2 * BANK].rearrange("p (u c) -> p u c", u=2)]]
         h_first = w3_last_room[:, 0 : 2 * S].bitcast(BF16)
-        h_third = w5_room[:, 0:S].bitcast(BF16)
-        h_cols = [
-            [h_first[:, PASS * j : PASS * (j + 1)] for j in range(4)],
-            [h_third[:, 0:PASS], h_third[:, PASS:]] + [w5_q["raw"][:, i, PAIR:].bitcast(BF16) for i in range(2)],
-        ]
+        h_second = w5_room[:, 0 : 2 * S].bitcast(BF16)
+        h_cols = [[h[:, PASS * j : PASS * (j + 1)] for j in range(4)] for h in (h_first, h_second)]
         h_w = [sbuf(f"h_w{a}", [P, S], U32) for a in range(2)]
         h_s = [sbuf(f"h_s{a}", [P, S], U8) for a in range(2)]
         d_sb = [[sbuf(f"d{g}{m}", [P, BANK], F32) for m in range(2)] for g in range(2)]
@@ -131,6 +127,10 @@ def tile_list_abbreviation_expansion_features_kernel(
                 out=part["raw"],
                 in_=part["rows"].rearrange("(p i) c -> p i c", i=PACK),
             )
+
+        def load_halves(part):
+            for e in range(2):
+                nc.sync.dma_start(out=part["raw"][e], in_=part["rows"][:, pair(e)].rearrange("(p i) c -> p i c", i=PACK))
 
         def load_e4m3_words(tile, words):
             nc.sync.dma_start(out=tile[:].bitcast(I32), in_=words.rearrange("p t i -> p (t i)").bitcast(I32))
@@ -170,9 +170,6 @@ def tile_list_abbreviation_expansion_features_kernel(
             src = part["raw"].rearrange("p i (m t) -> p m i t", t=PACK)[:, m0:m1, :, :]
             if engine == "v":
                 nc.vector.tensor_copy(out=dst, in_=src)
-            elif engine == "g":
-                walk = "p m i t -> p t m i" if dealt else "p m i t -> p m t i"
-                nc.gpsimd.tensor_scalar(out=dst.rearrange(walk), in0=src.rearrange(walk), scalar1=1.0, scalar2=0.0, op0=MULT, op1=ADD)
             else:
                 nc.scalar.copy(out=dst, in_=src)
 
@@ -180,14 +177,13 @@ def tile_list_abbreviation_expansion_features_kernel(
             round_piece(part, 0, share, "s", dealt)
             round_piece(part, share, P, other, dealt)
 
-        def round_with_gpsimd(part, dealt):
-            order = "p (t e m i) -> p e m i t" if dealt else "p (e m t i) -> p e m i t"
-            nc.scalar.copy(
-                out=part["grouped"].rearrange(order, e=2, t=PACK, i=PACK)[:, :, 0:EDGE, :, :],
-                in_=part["raw"].rearrange("p i (e m t) -> p e m i t", e=2, t=PACK)[:, :, 0:EDGE, :, :],
-            )
+        def round_halves(part, dealt):
+            order = "p (t m i) -> p m i t" if dealt else "p (m t i) -> p m i t"
             for e in range(2):
-                round_piece(part, 64 * e + EDGE, 64 * (e + 1), "g", dealt)
+                nc.scalar.copy(
+                    out=part["grouped"].rearrange(order, t=PACK, i=PACK)[:, 64 * e : 64 * (e + 1), :, :],
+                    in_=part["raw"][e].rearrange("p i (m t) -> p m i t", t=PACK),
+                )
 
         def quantise(part):
             nc.vector.quantize_mx(out=part["codes"][:].bitcast(FP8X4), scales=part["plane"][:], in_=part["grouped"])
@@ -300,8 +296,8 @@ def tile_list_abbreviation_expansion_features_kernel(
         place_pass(0)
         load_block(w1_q[0][1])
         load_e4m3_words(tab_w[1], tab_words[1])
-        place_pass(1)
         nc.sync.dma_start(out=tab3_w[:].bitcast(I32), in_=tab3_words[0].bitcast(I32))
+        place_pass(1)
         load_block(w1_q[1][0])
         deal_scales()
         gather(picked3, tab3_s, list3)
@@ -316,9 +312,9 @@ def tile_list_abbreviation_expansion_features_kernel(
         load_block(w3_q[0])
         load_e4m3_words(tab2_w, tab2_words[0])
         place_rows(v2_s, picked2)
-        load_block(w3_q[1])
+        load_halves(w3_q[1])
         load_plane(w4_s, w4_scales, W4_ROW0)
-        load_block(w5_q)
+        load_halves(w5_q)
         load_e4m3_words(w4_w[0], w4_words[0])
         place_rows(v3_s, picked3)
         load_e4m3_words(w4_w[1], w4_words[1])
@@ -340,10 +336,8 @@ def tile_list_abbreviation_expansion_features_kernel(
         multiply(0, 0)
         multiply(0, 1)
         multiply(0, 2)
-        make_room(w1_q[1][0], "tab3_w")
-        round_piece(w1_q[1][0], 0, 40, "s")
-        round_piece(w1_q[1][0], 40, 80, "g")
-        round_piece(w1_q[1][0], 80, P, "v")
+        make_room(w1_q[1][0])
+        round_block(w1_q[1][0], 40, "v")
         multiply(0, 3)
         quantise(w1_q[1][0])
         make_room(w1_q[1][1])
@@ -366,8 +360,8 @@ def tile_list_abbreviation_expansion_features_kernel(
         multiply(1, 1)
         multiply(1, 2)
         multiply(1, 3)
-        make_room(w3_q[1], "tab2_w")
-        round_with_gpsimd(w3_q[1], True)
+        make_room(w3_q[1])
+        round_halves(w3_q[1], True)
         for j in range(4):
             sense(0, j)
         for j in range(2):
@@ -377,8 +371,8 @@ def tile_list_abbreviation_expansion_features_kernel(
         add(0, 3)
         for j in range(4):
             sense(1, j)
-        make_room(w5_q, "tab2_w")
-        round_with_gpsimd(w5_q, False)
+        make_room(w5_q)
+        round_halves(w5_q, False)
         add(1, 0)
         quantise_h(0, slice(0, S), h_first)
         mix(0, 0)
@@ -389,7 +383,7 @@ def tile_list_abbreviation_expansion_features_kernel(
         domain(0, 1)
         add(1, 2)
         domain(1, 0)
-        quantise_h(1, pair(0), h_third)
+        quantise_h(1, pair(0), h_second[:, 0 : 2 * PASS])
         mix(1, 0)
         add(1, 3)
         domain(1, 1)

@@ -55,7 +55,6 @@ def tile_list_abbreviation_expansion_features_kernel(
         w2_w = sbuf("w2_w", [P, 2 * H], U16)
         w2_s = sbuf("w2_s", [P, 2 * H], U8)
         w2_dealt = sbuf("w2_dealt", [P, 2 * H], U16)
-        w2_s_dealt = sbuf("w2_s_dealt", [P, 2 * H], U8)
         w4_w = [sbuf(f"w4_w{a}", [P, N], U32) for a in range(2)]
         w4_s = sbuf("w4_s", [P, 2 * N], U8)
 
@@ -115,9 +114,9 @@ def tile_list_abbreviation_expansion_features_kernel(
         def pair(g):
             return slice(PAIR * g, PAIR * (g + 1))
 
-        def load_plane(plane, scales, row0):
+        def load_plane(queue, plane, scales, row0):
             for r in range(4):
-                nc.sync.dma_start(
+                queue.dma_start(
                     out=plane[row0 + r : P : 32, :].bitcast(I32).rearrange("q (a t) -> q a t", a=scales.shape[0]),
                     in_=scales[:, r:ROWS:4, :].bitcast(I32).rearrange("a q t -> q a t"),
                 )
@@ -276,7 +275,8 @@ def tile_list_abbreviation_expansion_features_kernel(
             nc.vector.tensor_tensor(out=result[g][m][:, pair(i)], in0=d_sb[g][m][:, pair(i)], in1=y_bank[g][m][:, pair(i)], op=MULT)
             nc.sync.dma_start(out=out[cols(2 * m + i), pair(g)], in_=result[g][m][:, pair(i)])
 
-        nc.vector.memset(w2_s[:].bitcast(I32), 0)
+        nc.gpsimd.memset(w2_s[:].bitcast(I32), 0)
+        load_plane(nc.gpsimd, w2_s, w2_scales, 0)
         nc.vector.memset(tab_s[32:64, :].bitcast(I32), 0)
         nc.vector.memset(tab_s[64:P, :].bitcast(I32), 0)
         for plane in (tab3_s, tab2_s, v_s[0], v_s[1], v2_s, v3_s, w4_s):
@@ -284,7 +284,6 @@ def tile_list_abbreviation_expansion_features_kernel(
 
         nc.sync.dma_start(list1[:], offs)
         nc.sync.dma_start(out=tab_s[0 : 2 * ROWS, :].bitcast(I32), in_=tab_scales.rearrange("a s t -> (a s) t").bitcast(I32))
-        load_plane(w2_s, w2_scales, 0)
         load_block(w1_q[0][0])
         nc.sync.dma_start(list3[:], offs3)
         load_rows(tab3_s, tab3_scales)
@@ -299,7 +298,6 @@ def tile_list_abbreviation_expansion_features_kernel(
         nc.sync.dma_start(out=tab3_w[:].bitcast(I32), in_=tab3_words[0].bitcast(I32))
         place_pass(1)
         load_block(w1_q[1][0])
-        deal_scales()
         gather(picked3, tab3_s, list3)
         gather(picked2, tab2_s, list2)
         make_room(w1_q[0][0])
@@ -308,12 +306,14 @@ def tile_list_abbreviation_expansion_features_kernel(
         deal_words(1, nc.scalar.copy)
         quantise(w1_q[0][0])
         gather(v_w[0], tab_w[0], list1)
+        w2_s_dealt = sbuf("w2_s_dealt", [P, 2 * H], U8, "tab_w0")
+        deal_scales()
         load_block(w1_q[1][1])
         load_block(w3_q[0])
         load_e4m3_words(tab2_w, tab2_words[0])
         place_rows(v2_s, picked2)
         load_halves(w3_q[1])
-        load_plane(w4_s, w4_scales, W4_ROW0)
+        load_plane(nc.sync, w4_s, w4_scales, W4_ROW0)
         load_halves(w5_q)
         load_e4m3_words(w4_w[0], w4_words[0])
         place_rows(v3_s, picked3)
@@ -324,7 +324,7 @@ def tile_list_abbreviation_expansion_features_kernel(
         for k in range(4):
             value(0, k, 0)
         make_room(w1_q[0][1])
-        round_block(w1_q[0][1], 32, "v")
+        round_block(w1_q[0][1], 64, "v")
         quantise(w1_q[0][1])
         for g in range(2):
             gather(v_w[1], tab_w[1], list1, PAIR * g, PAIR * (g + 1))

@@ -73,7 +73,7 @@ def tile_list_abbreviation_expansion_features_kernel(
         w1_room = sbuf("w1_room", [P, BANK + LEAD + PACK * PASS], F32)
         w3_first_room = sbuf("w3_first_room", [P, PACK, PAIR + PASS], F32)
         w3_last_room = sbuf("w3_last_room", [P, PASS + PACK * PAIR], F32)
-        w5_room = sbuf("w5_room", [P, PAIR + PACK * PAIR], F32)
+        w5_room = sbuf("w5_room", [P, PACK * PAIR], F32)
         w1_raw = [
             [by_rows(sbuf(f"raw_w1_0{a}", [P, PACK * PASS], F32)[:]) for a in range(2)],
             [by_rows(w1_room[:, BANK + LEAD :]), by_rows(sbuf("raw_w1_11", [P, PACK * PASS], F32)[:])],
@@ -86,7 +86,7 @@ def tile_list_abbreviation_expansion_features_kernel(
             operand("w3_0", w3[:, 0:PASS], w3_first_room[:, :, PAIR:]),
             operand("w3_1", w3[:, PASS:H], [by_rows(sbuf("raw_w3_10", [P, PACK * PAIR], F32)[:]), by_rows(w3_last_room[:, PASS:])]),
         ]
-        w5_q = operand("w5", w5, [by_rows(sbuf("raw_w50", [P, PACK * PAIR], F32)[:]), by_rows(w5_room[:, PAIR:])])
+        w5_q = operand("w5", w5, [by_rows(sbuf("raw_w50", [P, PACK * PAIR], F32)[:]), by_rows(w5_room[:])])
 
         v_w = [sbuf(f"v_w{a}", [P, S], U32) for a in range(2)]
         v2_w = sbuf("v2_w", [P, S], U32)
@@ -96,14 +96,20 @@ def tile_list_abbreviation_expansion_features_kernel(
         picked3 = sbuf("picked3", [P, S], U8)
         v_s = [sbuf(f"v_s{a}", [P, S], U8) for a in range(2)]
         v2_s = sbuf("v2_s", [P, S], U8)
-        v3_s = sbuf("v3_s", [P, S], U8)
+        v3_s = w4_s[:, 0:S]
 
         silu_a = [[sbuf(f"silu{k}", [P, BANK], F32)[:] for k in range(4)], [w3_first_room[:, k, 0:BANK] for k in range(4)]]
         gated = [[sbuf("gated00", [P, 2, BANK], F32)[:], w1_room[:, 0 : 2 * BANK].rearrange("p (u c) -> p u c", u=2)]]
         h_first = w3_last_room[:, 0 : 2 * S].bitcast(BF16)
-        h_second = w5_room[:, 0 : 2 * S].bitcast(BF16)
-        h_cols = [[h[:, PASS * j : PASS * (j + 1)] for j in range(4)] for h in (h_first, h_second)]
-        h_w = [sbuf(f"h_w{a}", [P, S], U32) for a in range(2)]
+        h_third = sbuf("h_third", [P, 2 * PASS], BF16)[:]
+        h_last = w5_room[:, 0:PASS].bitcast(BF16)
+        h_cols = [
+            [h_first[:, PASS * j : PASS * (j + 1)] for j in range(4)],
+            [h_third[:, 0:PASS], h_third[:, PASS:], h_last[:, 0:PASS], h_last[:, PASS:]],
+        ]
+        h_first_w = sbuf("h_first_w", [P, S], U32)
+        h_last_w = sbuf("h_last_w", [P, PAIR], U32)
+        h_w = {(0, 0): h_first_w[:, 0:PAIR], (0, 1): h_first_w[:, PAIR:S], (1, 1): h_last_w[:]}
         h_s = [sbuf(f"h_s{a}", [P, S], U8) for a in range(2)]
         d_sb = [[sbuf(f"d{g}{m}", [P, BANK], F32) for m in range(2)] for g in range(2)]
         result = [[sbuf(f"result{g}{m}", [P, BANK], F32) for m in range(2)] for g in range(2)]
@@ -114,8 +120,8 @@ def tile_list_abbreviation_expansion_features_kernel(
         def pair(g):
             return slice(PAIR * g, PAIR * (g + 1))
 
-        def load_plane(queue, plane, scales, row0):
-            for r in range(4):
+        def load_plane(queue, plane, scales, row0, rows=range(4)):
+            for r in rows:
                 queue.dma_start(
                     out=plane[row0 + r : P : 32, :].bitcast(I32).rearrange("q (a t) -> q a t", a=scales.shape[0]),
                     in_=scales[:, r:ROWS:4, :].bitcast(I32).rearrange("a q t -> q a t"),
@@ -242,8 +248,8 @@ def tile_list_abbreviation_expansion_features_kernel(
                 in0=gated[half][g][:, :, pair(e)].rearrange("p u (j e) -> p j u e", e=2), op=ADD,
             )
 
-        def quantise_h(half, js, values):
-            nc.vector.quantize_mx(out=h_w[half][:, js].bitcast(FP8X4), scales=h_s[half][:, js], in_=values)
+        def quantise_h(codes, scales, values):
+            nc.vector.quantize_mx(out=codes.bitcast(FP8X4), scales=scales, in_=values)
 
         def mix(a, g):
             for m in range(2):
@@ -252,7 +258,7 @@ def tile_list_abbreviation_expansion_features_kernel(
                     nc.tensor.matmul_mx(
                         out=y_bank[g][m][:, pair(i)], lhsT=w4_w[a][:, ns].bitcast(FP8X4),
                         lhsT_scale=w4_s[W4_ROW0:, cols(PACK * a + 2 * m + i)],
-                        rhs=h_w[a][:, pair(g)].bitcast(FP8X4), rhs_scale=h_s[a][:, pair(g)],
+                        rhs=h_w[a, g].bitcast(FP8X4), rhs_scale=h_s[a][:, pair(g)],
                         start=(a == 0 and i == 0), stop=(a == 1 and i == 1),
                     )
 
@@ -276,10 +282,10 @@ def tile_list_abbreviation_expansion_features_kernel(
             nc.sync.dma_start(out=out[cols(2 * m + i), pair(g)], in_=result[g][m][:, pair(i)])
 
         nc.gpsimd.memset(w2_s[:].bitcast(I32), 0)
-        load_plane(nc.gpsimd, w2_s, w2_scales, 0)
+        load_plane(nc.gpsimd, w2_s, w2_scales, 0, range(3))
         nc.vector.memset(tab_s[32:64, :].bitcast(I32), 0)
         nc.vector.memset(tab_s[64:P, :].bitcast(I32), 0)
-        for plane in (tab3_s, tab2_s, v_s[0], v_s[1], v2_s, v3_s, w4_s):
+        for plane in (tab3_s, tab2_s, v_s[0], v_s[1], v2_s, w4_s):
             nc.vector.memset(plane[:].bitcast(I32), 0)
 
         nc.sync.dma_start(list1[:], offs)
@@ -290,6 +296,7 @@ def tile_list_abbreviation_expansion_features_kernel(
         nc.sync.dma_start(list2[:], offs2)
         load_rows(tab2_s, tab2_scales)
         nc.sync.dma_start(out=w2_w[:].bitcast(I32).rearrange("p (a b) -> p a b", a=2), in_=w2_words.bitcast(I32).rearrange("a p b -> p a b"))
+        load_plane(nc.sync, w2_s, w2_scales, 0, range(3, 4))
         load_e4m3_words(tab_w[0], tab_words[0])
         gather(picked1, tab_s, list1)
         place_pass(0)
@@ -374,21 +381,22 @@ def tile_list_abbreviation_expansion_features_kernel(
         make_room(w5_q)
         round_halves(w5_q, False)
         add(1, 0)
-        quantise_h(0, slice(0, S), h_first)
+        quantise_h(h_first_w[:], h_s[0][:], h_first)
         mix(0, 0)
         mix(0, 1)
+        add(1, 1)
         quantise(w5_q)
         domain(0, 0)
-        add(1, 1)
         domain(0, 1)
         add(1, 2)
         domain(1, 0)
-        quantise_h(1, pair(0), h_second[:, 0 : 2 * PASS])
+        h_w[1, 0] = sbuf("h_third_w", [P, PAIR], U32, "grouped_w5")[:]
+        quantise_h(h_w[1, 0], h_s[1][:, pair(0)], h_third)
         mix(1, 0)
         add(1, 3)
         domain(1, 1)
-        quantise_h(1, cols(2), h_cols[1][2])
-        quantise_h(1, cols(3), h_cols[1][3])
+        for e in range(2):
+            quantise_h(h_last_w[:, cols(e)], h_s[1][:, cols(2 + e)], h_cols[1][2 + e])
         mix(1, 1)
         finish(0, 0)
         finish(0, 1)

from contextlib import ExitStack

import concourse.mybir as mybir

K, M, H, N, T, T2, T3, S = 1024, 512, 1024, 512, 2048, 2048, 1024, 512
FLOPS = 2 * S * (2 * K * H + M * H + H * N + M * N)

F32 = mybir.dt.float32
BF16 = mybir.dt.bfloat16
I32 = mybir.dt.int32
U32 = mybir.dt.uint32
U16 = mybir.dt.uint16
U8 = mybir.dt.uint8
FP8X4 = mybir.dt.float8_e4m3fn_x4
FP4X4 = mybir.dt.float4_e2m1fn_x4
SILU = mybir.ActivationFunctionType.Silu
MULT = mybir.AluOpType.mult
ADD = mybir.AluOpType.add

P = 128
PACK = 4
PASS = P * PACK
BANK = 512
PAIR = 2 * P
ROWS = 16
W4_ROW0 = 4
LEAD = 3 * P


def tile_list_abbreviation_expansion_features_kernel(
    tc, tab_words, tab_scales, tab2_words, tab2_scales, tab3_words, tab3_scales, offs, offs2, offs3,
    w1, w2_words, w2_scales, w3, w4_words, w4_scales, w5, out,
):
    nc = tc.nc
    with ExitStack() as ctx:
        keep = ctx.enter_context(tc.tile_pool(name="keep", bufs=1))
        psum = ctx.enter_context(tc.psum_pool(name="psum", bufs=1))

        def sbuf(name, shape, dtype, tag=None):
            return keep.tile(shape, dtype, name=name, tag=tag or name, align_bytes=64)

        list1 = keep.tile([P, S // 16], U16, name="list1")
        list2 = keep.tile([P, S // 16], U16, name="list2")
        list3 = keep.tile([P, S // 16], U16, name="list3")

        banks = [psum.tile([P, BANK], F32, name=f"bank{i}") for i in range(8)]
        low, high = banks[0:4], banks[4:8]

        tab_w = [sbuf(f"tab_w{a}", [P, T], U32) for a in range(2)]
        tab2_w = sbuf("tab2_w", [P, T2], U32)
        tab3_w = sbuf("tab3_w", [P, T3], U16)
        tab_s = sbuf("tab_s", [P, T], U8)
        tab2_s = sbuf("tab2_s", [P, T2], U8)
        tab3_s = sbuf("tab3_s", [P, T3], U8)
        w2_w = sbuf("w2_w", [P, 2 * H], U16)
        w2_s = sbuf("w2_s", [P, 2 * H], U8)
        w2_dealt = sbuf("w2_dealt", [P, 2 * H], U16)
        w4_w = [sbuf(f"w4_w{a}", [P, N], U32) for a in range(2)]
        w4_s = sbuf("w4_s", [P, 2 * N], U8)

        def operand(name, rows, raw):
            return {
                "name": name,
                "rows": rows,
                "raw": raw,
                "codes": sbuf("codes_" + name, [P, PASS], U32),
                "plane": sbuf("plane_" + name, [P, PASS], U8),
            }

        def by_rows(ap):
            return ap.rearrange("p (i c) -> p i c", i=PACK)

        w1_room = sbuf("w1_room", [P, BANK + LEAD + PACK * PASS], F32)
        w3_first_room = sbuf("w3_first_room", [P, PACK, PAIR + PASS], F32)
        w3_last_room = sbuf("w3_last_room", [P, PASS + PACK * PAIR], F32)
        w5_room = sbuf("w5_room", [P, PACK * PAIR], F32)
        w1_raw = [
            [by_rows(sbuf(f"raw_w1_0{a}", [P, PACK * PASS], F32)[:]) for a in range(2)],
            [by_rows(w1_room[:, BANK + LEAD :]), by_rows(sbuf("raw_w1_11", [P, PACK * PASS], F32)[:])],
        ]
        w1_q = [
            [operand(f"w1_{half}{a}", w1[PASS * a : PASS * (a + 1), PASS * half : PASS * (half + 1)], w1_raw[half][a]) for a in range(2)]
            for half in range(2)
        ]
        w3_q = [
            operand("w3_0", w3[:, 0:PASS], w3_first_room[:, :, PAIR:]),
            operand("w3_1", w3[:, PASS:H], [by_rows(sbuf("raw_w3_10", [P, PACK * PAIR], F32)[:]), by_rows(w3_last_room[:, PASS:])]),
        ]
        w5_q = operand("w5", w5, [by_rows(sbuf("raw_w50", [P, PACK * PAIR], F32)[:]), by_rows(w5_room[:])])

        v_w = [sbuf(f"v_w{a}", [P, S], U32) for a in range(2)]
        v2_w = sbuf("v2_w", [P, S], U32)
        v3_w = sbuf("v3_w", [P, S], U16)
        picked1 = sbuf("picked1", [P, S], U8)
        picked2 = sbuf("picked2", [P, S], U8)
        picked3 = sbuf("picked3", [P, S], U8)
        v_s = [sbuf(f"v_s{a}", [P, S], U8) for a in range(2)]
        v2_s = sbuf("v2_s", [P, S], U8)
        v3_s = w4_s[:, 0:S]

        silu_a = [[sbuf(f"silu{k}", [P, BANK], F32)[:] for k in range(4)], [w3_first_room[:, k, 0:BANK] for k in range(4)]]
        gated = [[sbuf("gated00", [P, 2, BANK], F32)[:], w1_room[:, 0 : 2 * BANK].rearrange("p (u c) -> p u c", u=2)]]
        h_first = w3_last_room[:, 0 : 2 * S].bitcast(BF16)
        h_third = sbuf("h_third", [P, 2 * PASS], BF16)[:]
        h_last = w5_room[:, 0:PASS].bitcast(BF16)
        h_cols = [
            [h_first[:, PASS * j : PASS * (j + 1)] for j in range(4)],
            [h_third[:, 0:PASS], h_third[:, PASS:], h_last[:, 0:PASS], h_last[:, PASS:]],
        ]
        h_first_w = sbuf("h_first_w", [P, S], U32)
        h_last_w = sbuf("h_last_w", [P, PAIR], U32)
        h_w = {(0, 0): h_first_w[:, 0:PAIR], (0, 1): h_first_w[:, PAIR:S], (1, 1): h_last_w[:]}
        h_s = [sbuf(f"h_s{a}", [P, S], U8) for a in range(2)]
        d_sb = [[sbuf(f"d{g}{m}", [P, BANK], F32) for m in range(2)] for g in range(2)]
        result = [[sbuf(f"result{g}{m}", [P, BANK], F32) for m in range(2)] for g in range(2)]

        def cols(t):
            return slice(P * t, P * (t + 1))

        def pair(g):
            return slice(PAIR * g, PAIR * (g + 1))

        def load_plane(queue, plane, scales, row0, rows=range(4)):
            for r in rows:
                queue.dma_start(
                    out=plane[row0 + r : P : 32, :].bitcast(I32).rearrange("q (a t) -> q a t", a=scales.shape[0]),
                    in_=scales[:, r:ROWS:4, :].bitcast(I32).rearrange("a q t -> q a t"),
                )

        def load_block(part):
            nc.sync.dma_start(
                out=part["raw"],
                in_=part["rows"].rearrange("(p i) c -> p i c", i=PACK),
            )

        def load_halves(part):
            for e in range(2):
                nc.sync.dma_start(out=part["raw"][e], in_=part["rows"][:, pair(e)].rearrange("(p i) c -> p i c", i=PACK))

        def load_e4m3_words(tile, words):
            nc.sync.dma_start(out=tile[:].bitcast(I32), in_=words.rearrange("p t i -> p (t i)").bitcast(I32))

        def load_rows(tile, scales):
            nc.sync.dma_start(out=tile[0:P:8, :].bitcast(I32), in_=scales[0].bitcast(I32))

        def place_pass(a):
            for r in range(4):
                nc.sync.dma_start(out=v_s[a][r:P:32, :].bitcast(I32), in_=picked1[ROWS * a + r : ROWS * (a + 1) : 4, :].bitcast(I32))

        def place_rows(plane, picked):
            for r in range(4):
                nc.sync.dma_start(out=plane[r:P:32, :].bitcast(I32), in_=picked[8 * r : P : 32, :].bitcast(I32))

        def gather(picked, window, entries, j0=0, j1=S):
            nc.vector.tensor_copy(picked[:, j0:j1], window[:].indirect(entries[:, j0 // 16 : j1 // 16]))

        def deal_scales():
            nc.vector.tensor_copy(
                out=w2_s_dealt[:].rearrange("p (h a t m) -> p h a t m", h=2, a=2, t=PACK),
                in_=w2_s[:].rearrange("p (a h m t) -> p h a t m", a=2, h=2, t=PACK),
            )

        def deal_words(half, copy):
            copy(
                out=w2_dealt[:, H * half : H * (half + 1)].rearrange("p (a t m) -> p a t m", a=2, t=PACK),
                in_=w2_w[:].rearrange("p (a h m t) -> p h a t m", a=2, h=2, t=PACK)[:, half, :, :, :],
            )

        def make_room(part, tag=None):
            part["grouped"] = sbuf("grouped_" + part["name"], [P, PACK * PASS], BF16, tag)[:]

        def round_piece(part, m0, m1, engine, dealt=True):
            order = "p (t m i) -> p m i t" if dealt else "p (m t i) -> p m i t"
            dst = part["grouped"].rearrange(order, t=PACK, i=PACK)[:, m0:m1, :, :]
            src = part["raw"].rearrange("p i (m t) -> p m i t", t=PACK)[:, m0:m1, :, :]
            if engine == "v":
                nc.vector.tensor_copy(out=dst, in_=src)
            else:
                nc.scalar.copy(out=dst, in_=src)

        def round_block(part, share, other="g", dealt=True):
            round_piece(part, 0, share, "s", dealt)
            round_piece(part, share, P, other, dealt)

        def round_halves(part, dealt):
            order = "p (t m i) -> p m i t" if dealt else "p (m t i) -> p m i t"
            for e in range(2):
                nc.scalar.copy(
                    out=part["grouped"].rearrange(order, t=PACK, i=PACK)[:, 64 * e : 64 * (e + 1), :, :],
                    in_=part["raw"][e].rearrange("p i (m t) -> p m i t", t=PACK),
                )

        def quantise(part):
            nc.vector.quantize_mx(out=part["codes"][:].bitcast(FP8X4), scales=part["plane"][:], in_=part["grouped"])

        a_bank, b_bank = low, high
        c_bank = [low, high]
        y_bank = [low[0:2], low[2:4]]
        d_bank = [high[0:2], high[2:4]]

        def woven(bank, ways):
            return bank[:].rearrange("p (t j) -> p j t", t=ways)

        def flat(ap, ways):
            return ap.rearrange("p (j t) -> p j t", t=ways)

        def gate(half, k, a):
            g, u = divmod(k, 2)
            part = w1_q[half][a]
            for e in range(2):
                ws = cols(2 * u + e)
                nc.tensor.matmul_mx(
                    out=a_bank[k][:, pair(e)], lhsT=part["codes"][:, ws].bitcast(FP8X4), lhsT_scale=part["plane"][:, ws],
                    rhs=v_w[a][:, pair(g)].bitcast(FP8X4), rhs_scale=v_s[a][:, pair(g)],
                    start=(a == 0 and e == 0), stop=(a == 1 and e == 1),
                )

        def value(half, k, a):
            g, u = divmod(k, 2)
            for e in range(2):
                ws = cols(PACK * (2 * half + a) + 2 * u + e)
                nc.tensor.matmul_mx(
                    out=b_bank[k][:, pair(e)], lhsT=w2_dealt[:, ws].bitcast(FP4X4), lhsT_scale=w2_s_dealt[:, ws],
                    rhs=v_w[a][:, pair(g)].bitcast(FP8X4), rhs_scale=v_s[a][:, pair(g)],
                    start=(a == 0 and e == 0), stop=(a == 1 and e == 1),
                )

        def sense(half, j):
            part = w3_q[half]
            for t in range(PACK):
                nc.tensor.matmul_mx(
                    out=c_bank[half][j][:, cols(t)], lhsT=part["codes"][:, cols(t)].bitcast(FP8X4), lhsT_scale=part["plane"][:, cols(t)],
                    rhs=v2_w[:, cols(j)].bitcast(FP8X4), rhs_scale=v2_s[:, cols(j)], start=True, stop=True,
                )

        def silu(half, k):
            nc.scalar.activation(out=flat(silu_a[half][k], 2), in_=woven(a_bank[k], 2), func=SILU)

        def multiply(half, k):
            g, u = divmod(k, 2)
            nc.vector.tensor_tensor(out=flat(gated[half][g][:, u, :], 2), in0=flat(silu_a[half][k], 2), in1=woven(b_bank[k], 2), op=MULT)

        def add(half, j):
            g, e = divmod(j, 2)
            nc.vector.tensor_tensor(
                out=h_cols[half][j].rearrange("p (j u e) -> p j u e", u=2, e=2),
                in1=c_bank[half][j][:].rearrange("p (u e j) -> p j u e", u=2, e=2),
                in0=gated[half][g][:, :, pair(e)].rearrange("p u (j e) -> p j u e", e=2), op=ADD,
            )

        def quantise_h(codes, scales, values):
            nc.vector.quantize_mx(out=codes.bitcast(FP8X4), scales=scales, in_=values)

        def mix(a, g):
            for m in range(2):
                for i in range(2):
                    ns = cols(2 * m + i)
                    nc.tensor.matmul_mx(
                        out=y_bank[g][m][:, pair(i)], lhsT=w4_w[a][:, ns].bitcast(FP8X4),
                        lhsT_scale=w4_s[W4_ROW0:, cols(PACK * a + 2 * m + i)],
                        rhs=h_w[a, g].bitcast(FP8X4), rhs_scale=h_s[a][:, pair(g)],
                        start=(a == 0 and i == 0), stop=(a == 1 and i == 1),
                    )

        def domain(g, m):
            for i in range(2):
                ns = cols(2 * m + i)
                nc.tensor.matmul_mx(
                    out=d_bank[g][m][:, pair(i)], lhsT=w5_q["codes"][:, ns].bitcast(FP8X4), lhsT_scale=w5_q["plane"][:, ns],
                    rhs=v3_w[:, pair(g)].bitcast(FP4X4), rhs_scale=v3_s[:, pair(g)], start=True, stop=True,
                )
            nc.scalar.copy(out=d_sb[g][m][:], in_=d_bank[g][m][:])

        def finish(g, m):
            nc.vector.tensor_tensor(out=result[g][m][:], in0=d_sb[g][m][:], in1=y_bank[g][m][:], op=MULT)
            nc.sync.dma_start(
                out=out[pair(m), pair(g)].rearrange("(i p) j -> p i j", p=P), in_=result[g][m][:].rearrange("p (i j) -> p i j", i=2),
            )

        def finish_half(g, m, i):
            nc.vector.tensor_tensor(out=result[g][m][:, pair(i)], in0=d_sb[g][m][:, pair(i)], in1=y_bank[g][m][:, pair(i)], op=MULT)
            nc.sync.dma_start(out=out[cols(2 * m + i), pair(g)], in_=result[g][m][:, pair(i)])

        nc.gpsimd.memset(w2_s[:].bitcast(I32), 0)
        load_plane(nc.gpsimd, w2_s, w2_scales, 0, range(3))
        nc.vector.memset(tab_s[32:64, :].bitcast(I32), 0)
        nc.vector.memset(tab_s[64:P, :].bitcast(I32), 0)
        for plane in (tab3_s, tab2_s, v_s[0], v_s[1], v2_s, w4_s):
            nc.vector.memset(plane[:].bitcast(I32), 0)

        nc.sync.dma_start(list1[:], offs)
        nc.sync.dma_start(out=tab_s[0 : 2 * ROWS, :].bitcast(I32), in_=tab_scales.rearrange("a s t -> (a s) t").bitcast(I32))
        load_block(w1_q[0][0])
        nc.sync.dma_start(list3[:], offs3)
        load_rows(tab3_s, tab3_scales)
        nc.sync.dma_start(list2[:], offs2)
        load_rows(tab2_s, tab2_scales)
        nc.sync.dma_start(out=w2_w[:].bitcast(I32).rearrange("p (a b) -> p a b", a=2), in_=w2_words.bitcast(I32).rearrange("a p b -> p a b"))
        load_plane(nc.sync, w2_s, w2_scales, 0, range(3, 4))
        load_e4m3_words(tab_w[0], tab_words[0])
        gather(picked1, tab_s, list1)
        place_pass(0)
        load_block(w1_q[0][1])
        load_e4m3_words(tab_w[1], tab_words[1])
        nc.sync.dma_start(out=tab3_w[:].bitcast(I32), in_=tab3_words[0].bitcast(I32))
        place_pass(1)
        load_block(w1_q[1][0])
        gather(picked3, tab3_s, list3)
        gather(picked2, tab2_s, list2)
        make_room(w1_q[0][0])
        round_piece(w1_q[0][0], 0, P, "s")
        deal_words(0, nc.scalar.copy)
        deal_words(1, nc.scalar.copy)
        quantise(w1_q[0][0])
        gather(v_w[0], tab_w[0], list1)
        w2_s_dealt = sbuf("w2_s_dealt", [P, 2 * H], U8, "tab_w0")
        deal_scales()
        load_block(w1_q[1][1])
        load_block(w3_q[0])
        load_e4m3_words(tab2_w, tab2_words[0])
        place_rows(v2_s, picked2)
        load_halves(w3_q[1])
        load_plane(nc.sync, w4_s, w4_scales, W4_ROW0)
        load_halves(w5_q)
        load_e4m3_words(w4_w[0], w4_words[0])
        place_rows(v3_s, picked3)
        load_e4m3_words(w4_w[1], w4_words[1])

        for k in range(4):
            gate(0, k, 0)
        for k in range(4):
            value(0, k, 0)
        make_room(w1_q[0][1])
        round_block(w1_q[0][1], 64, "v")
        quantise(w1_q[0][1])
        for g in range(2):
            gather(v_w[1], tab_w[1], list1, PAIR * g, PAIR * (g + 1))
        gather(v3_w, tab3_w, list3)
        for k in range(4):
            gate(0, k, 1)
            value(0, k, 1)
            silu(0, k)
        multiply(0, 0)
        multiply(0, 1)
        multiply(0, 2)
        make_room(w1_q[1][0])
        round_block(w1_q[1][0], 40, "v")
        multiply(0, 3)
        quantise(w1_q[1][0])
        make_room(w1_q[1][1])
        round_block(w1_q[1][1], 76, "v")
        quantise(w1_q[1][1])
        for k in range(4):
            value(1, k, 0)
            value(1, k, 1)
            gate(1, k, 0)
        make_room(w3_q[0])
        round_block(w3_q[0], 64, "v")
        quantise(w3_q[0])
        for k in range(4):
            gate(1, k, 1)
            silu(1, k)
        gather(v2_w, tab2_w, list2)
        gated_second = sbuf("gated1", [P, 2, 2, BANK], F32, "picked2")
        gated.append([gated_second[:, g, :, :] for g in range(2)])
        multiply(1, 0)
        multiply(1, 1)
        multiply(1, 2)
        multiply(1, 3)
        make_room(w3_q[1])
        round_halves(w3_q[1], True)
        for j in range(4):
            sense(0, j)
        for j in range(2):
            add(0, j)
        quantise(w3_q[1])
        add(0, 2)
        add(0, 3)
        for j in range(4):
            sense(1, j)
        make_room(w5_q)
        round_halves(w5_q, False)
        add(1, 0)
        quantise_h(h_first_w[:], h_s[0][:], h_first)
        mix(0, 0)
        mix(0, 1)
        add(1, 1)
        quantise(w5_q)
        domain(0, 0)
        domain(0, 1)
        add(1, 2)
        domain(1, 0)
        h_w[1, 0] = sbuf("h_third_w", [P, PAIR], U32, "grouped_w5")[:]
        quantise_h(h_w[1, 0], h_s[1][:, pair(0)], h_third)
        mix(1, 0)
        add(1, 3)
        domain(1, 1)
        for e in range(2):
            quantise_h(h_last_w[:, cols(e)], h_s[1][:, cols(2 + e)], h_cols[1][2 + e])
        mix(1, 1)
        finish(0, 0)
        finish(0, 1)
        finish(1, 0)
        finish_half(1, 1, 0)
        finish_half(1, 1, 1)
